import numpy as np, ml_dtypes
CORES = [1,5,17,21,33,37,49,53]
N = 8
import mx_ref
BF = ml_dtypes.bfloat16
def gentries(a):
    return np.ascontiguousarray(a.reshape(8, 16, -1).transpose(0, 2, 1)).reshape(8, -1)
def gtable(e):
    e = np.asarray(e); return np.ascontiguousarray(e.reshape(8, -1, 16).transpose(0, 2, 1)).reshape(128, -1).astype(np.int32)
def gcols(t, e):
    v = np.concatenate([t.reshape(8, 16, -1, 4), np.zeros((8, 16, 1, 4), BF)], axis=2)
    return np.ascontiguousarray(np.stack([v[g][:, e[g]] for g in range(8)])).reshape(128, -1)
def tile(rs):
    return np.stack(rs, axis=2).reshape(128, -1).astype(BF)
def cut(t, i, w=512):
    return t[:, w * i:w * i + w]
def pick(q, e):
    c = np.concatenate([q[0].reshape(128, -1, 4), np.zeros((128, 1, 4), np.uint8)], axis=1); s = np.concatenate([q[1], np.ones((16, 1), np.uint8)], axis=1)
    return (np.ascontiguousarray(c[:, e].reshape(128, -1)), np.ascontiguousarray(s[:, e]))
def join(*qs):
    return (np.concatenate([q[0] for q in qs], axis=1), np.concatenate([q[1] for q in qs], axis=1))
def put(q, e, v):
    c, s = q[0].reshape(128, -1, 4).copy(), q[1].copy(); c[:, e] = v[0].reshape(128, -1, 4); s[:, e] = v[1]
    return (c.reshape(128, -1), s)
def pk(c, s):
    return (np.ascontiguousarray(c), mx_ref.live(s))
def emit(q):
    return q[0], q[1]
def packed(v, rng):
    q = [mx_ref.quantize(np.ascontiguousarray(v[r])) for r in range(N)]
    return np.stack([a for a, b in q]), np.stack([mx_ref.plane(b, rng) for a, b in q])
def values_of_codes():
    e, c = np.zeros((128, 128, 4), np.float32), np.zeros((128, 2, 4), np.uint8)
    e[np.arange(128), np.arange(128), 0] = 1
    c[:127, :, 0] = np.arange(256).reshape(2, 128).T[:127]
    return mx_ref.matmul(mx_ref.quantize(e.reshape(128, 512).astype(BF)), (c.reshape(128, 8), np.full((16, 2), 127, np.uint8))).T.reshape(-1).astype(np.float64)
CODE_VALUE, SCALE_VALUE = values_of_codes(), 2.0 ** (np.arange(256) - 127.0)
def decode(q):
    return (CODE_VALUE[q[0]].reshape(16, 8, -1, 4) * SCALE_VALUE[q[1]][:, None, :, None] + 0.0).reshape(128, -1).astype(np.float32)
def f(rng, *shape):
    return mx_ref.flush((rng.standard_normal(shape, dtype=np.float32) * np.exp2(rng.integers(-2, 3, shape[:-1] + (1,)))).astype(BF))
def wide(rng, *shape, cols=0):
    v = rng.standard_normal(shape, dtype=np.float32) * np.exp2(rng.integers(-12, 13, shape)).astype(np.float32)
    if cols: v *= np.repeat(np.exp2(rng.integers(-cols, cols + 1, shape[:-2] + (1, shape[-1] // 4))) * (rng.random(shape[:-2] + (1, shape[-1] // 4)) > 0.0625), 4, axis=-1).astype(np.float32)
    return mx_ref.flush(v.astype(BF))
C, K, R = 320, 160, 3
def trim(v):
    v = np.array(v, dtype=np.float32)
    v[np.abs(v) < np.float32(2.0 ** -16)] = 0
    return v.astype(BF)
def stored(t):
    return np.stack([gtable(e) for e in t])
def numbers_of(rng):
    return {"x": trim(f(rng, N, 128, 4 * C)), "tg": stored(rng.integers(0, C, (N, 8, C))), "u": np.array(f(rng, N, 128, 512)), "v": np.array(f(rng, N, 128, 512))}
def weights(rng, w):
    c, p = packed(w, rng)
    return {"wc": c, "ws": p}
def keeping(rng, n):
    w = trim(f(rng, N, 128, 2048)).reshape(N, 8, 16, 4, 8, 16, 4)
    w[:, :, :n] = 0
    w[:, :, :, :, :, :n] = 0
    w = w.reshape(N, 128, 4, 128, 4)
    i = np.flatnonzero(np.arange(128) % 16 < n)
    for b in range(4): w[:, i, b, i, b] = 32
    return weights(rng, w.reshape(N, 128, 2048))
def signs(rng):
    return np.stack([rng.permutation(8) % 2 * 2.0 - 1.0 for r in range(N)])
def sizes(rng):
    return np.where(rng.permutation(N) < N // 2, 2.0 ** -30, 1.0).astype(np.float32)
def marked(rng, fire, late, t):
    d = numbers_of(rng)
    k = sizes(rng)
    x = d["x"].astype(np.float32).reshape(N, 8, 16, C, 4)
    x[:, :, :8] = rng.integers(8, 14, (N, 8, 8, C, 4))
    x[:, :, 0, :, 0] = 8 + (fire > 0)
    x[:, :, 0, :, 1] = 8 + (fire < 0)
    x[:, :, 1, :, 0] = 8 + (late > 0)
    x[:, :, 1, :, 1] = 8 + (late < 0)
    x[:, :, :8] *= k[:, None, None, None, None]
    u = d["u"].reshape(N, 128, 128, 4)
    for h in range(0, 128, 16):
        for i in (h, h + 1):
            u[:, :, i] = 0
            u[:, i, i, 0] = k.astype(BF)
            u[:, i, i, 1] = (-k).astype(BF)
    return {"x": x.reshape(N, 128, 4 * C).astype(BF), "tg": stored(t), "u": u.reshape(N, 128, 512), "v": d["v"], **keeping(rng, 8)}
def setup_inputs(rng):
    return {**numbers_of(rng), **weights(rng, trim(f(rng, N, 128, 2048)))}
def setup_inputs_counts(rng):
    o = rng.permutation(N)
    fire = -rng.integers(0, 2, (N, 8, C))
    late = rng.integers(-1, 2, (N, 8, C))
    t = rng.integers(0, C, (N, 8, C))
    for r in range(N):
        n = rng.permutation([K, K, K - 1, K + 1, C, 1, 0, K // 2])
        if o[r] == 0: n[:] = 0
        if o[r] == 1: n[:] = C
        for g in range(8): fire[r, g, rng.permutation(C)[:n[g]]] = 1
        a = rng.permutation(8)
        late[r, a[0]] = 1
        late[r, a[1]] = 0
        t[r, a[2]] = rng.integers(C)
        t[r, a[3]] = np.arange(C)
        t[r, a[4]] = np.arange(C) // 2
    return marked(rng, fire, late, t)
def setup_inputs_waves(rng):
    n = min(K, C // 2) // 4 * 4
    h = n // 2
    p = np.argsort(rng.random((N, 8, C)), axis=2)
    i = np.arange(C)
    z = n + np.where(i < h, i // 2, np.where(i < n, i, h + (i - n) % h))
    fire = -rng.integers(0, 2, (N, 8, C))
    late = -rng.integers(0, 2, (N, 8, C))
    t = np.zeros((N, 8, C), np.int64)
    np.put_along_axis(t, p, np.roll(p, -1, axis=0)[:, :, z], axis=2)
    np.put_along_axis(fire, p[:, :, :n], 1, axis=2)
    np.put_along_axis(late, p[:, :, h:n], 1, axis=2)
    return marked(rng, fire, late, t)
def setup_inputs_near(rng):
    d = numbers_of(rng)
    p = rng.permutation(C)
    back = np.argsort(p)
    s = p // 2
    way = 1 - s % 2 * 2
    digit = ((s[:, None] >> np.arange(8)) & 1) * np.exp2(np.arange(8) - 22.0)
    x = np.zeros((N, 8, 16, C, 4), np.float32)
    x[:, :, 0, :, 0] = 1
    x[:, :, 8] = digit[:, :4]
    x[:, :, 9] = digit[:, 4:]
    x[:, :, 10:] = rng.integers(4, 8, (N, 8, 6, C, 4)) * rng.choice([-1.0, 1.0], (N, 8, 6, C, 4)) * 2.0 ** -19
    k, sign = sizes(rng), signs(rng)
    u = d["u"].reshape(N, 128, 128, 4)
    u[:, :, ::16] = 0
    u[:, :, 1::16] = 0
    t = rng.integers(0, C, (N, 8, C))
    for g in range(8):
        h = 16 * g
        a = (k * sign[:, g]).astype(np.float32).astype(BF)
        u[:, h, h, 0] = a
        u[:, h + 8:h + 10, h] = a[:, None, None]
        u[:, h + 10, h + 1] = k.astype(BF)[:, None]
    for r in range(N):
        a = rng.permutation(8)
        a = a[np.argsort(-sign[r, a], kind="stable")]
        for i in (0, 4):
            t[r, a[i]] = np.arange(C)
            t[r, a[i + 1]] = back[(p + way) % C]
            t[r, a[i + 2]] = back[(p - way) % C]
    return {"x": x.reshape(N, 128, 4 * C).astype(BF), "tg": stored(t), "u": u.reshape(N, 128, 512), "v": d["v"], **keeping(rng, 16)}
def setup_inputs_huge(rng):
    d = numbers_of(rng)
    o = rng.permutation(N)
    g = signs(rng)
    g[o == 0] = -1
    g[o == 1] = 1
    c = np.stack([rng.permutation(C) % 2 * 2.0 - 1.0 for r in range(N)])
    c[o < 3] = 1
    x = 2.0 ** 30 * (0.6 + 0.4 * rng.random((N, 128, C, 4))) * c[:, None, :, None]
    u = d["u"].reshape(N, 128, 128, 4)
    u[:, :, ::16] = (2.0 ** 30 * (1 - 0.25 * rng.random((N, 128, 8, 4))) * g[:, None, :, None]).astype(np.float32).astype(BF)
    return {"x": x.astype(np.float32).reshape(N, 128, 4 * C).astype(BF), "tg": d["tg"], "u": u.reshape(N, 128, 512), "v": d["v"], **keeping(rng, 16)}
def setup_inputs_spread(rng):
    d = setup_inputs(rng)
    d["x"] = trim(wide(rng, N, 128, 4 * C, cols=6))
    return d
def check_inputs(d):
    b = []
    for k in ("x", "u", "v"):
        a = np.abs(d[k].astype(np.float32))
        if not (np.isfinite(a).all() and ((a == 0) | (a >= 2.0 ** -30) & (a <= 2.0 ** 30)).all()): b.append("a value of " + k)
    if ((d["tg"] < 0) | (d["tg"] >= C)).any(): b.append("an entry of tg")
    for r in range(N):
        if ((d["wc"][r] & 127) == 127).any(): b.append("wc: a code that is no number")
        if not (np.abs(decode(pk(d["wc"][r], d["ws"][r]))) <= 2.0 ** 30).all(): b.append("a number of W")
    return b
def spreadout(m):
    return np.repeat(np.repeat(m, 16, axis=0), 4, axis=1)
def reference(x, tg, u, v, wc, ws):
    qu = [mx_ref.quantize(u[r]) for r in range(N)]
    lay = [pk(wc[r], ws[r]) for r in range(N)]
    to = [gentries(tg[r]).astype(np.int64) for r in range(N)]
    now = [x[r] for r in range(N)]
    last = [np.zeros((8, C), np.float32) for r in range(N)]
    fired = [np.zeros((8, C), bool) for r in range(N)]
    kept = [[] for r in range(N)]
    due = np.full((N, R + 2, 8, C), -1)
    lists = [None] * N
    for t in range(R + 1):
        if t > 0:
            for r in range(N):
                got = gcols(np.concatenate(kept[r], axis=1), due[r, t])
                mean = ((now[r].astype(np.float32) + got.astype(np.float32)) * np.float32(0.5)).astype(BF)
                now[r] = np.where(spreadout(due[r, t] >= 0), np.where(spreadout(fired[r]), mean, got), now[r])
        if t == R: break
        sent, target, delay = [], [], []
        for r in range(N):
            s = mx_ref.matmul(qu[r], mx_ref.quantize(now[r])) + np.float32(0.0)
            rise = s[::16] > last[r]
            last[r] = s[::16]
            e = np.argsort(~rise, axis=1, kind="stable")[:, :K]
            e = np.where(np.take_along_axis(rise, e, axis=1), e, -1)
            m = np.zeros((8, C + 1), bool)
            np.put_along_axis(m, np.where(e < 0, C, e), True, axis=1)
            fired[r] = m[:, :C]
            q = mx_ref.quantize(gcols(now[r], e))
            h = tile([np.maximum(mx_ref.matmul(pick(lay[r], np.arange(128 * b, 128 * b + 128)), q), np.float32(0.0)) * np.float32(0.03125) for b in range(4)])
            sent.append(mx_ref.quantize(h))
            some = np.maximum(e, 0)
            target.append(np.take_along_axis(to[r], some, axis=1))
            delay.append(np.where(e < 0, 0, 1 + (np.take_along_axis(s[1::16], some, axis=1) > 0)))
            lists[r] = e
        came = decode(join(*sent)).astype(BF)
        for r in range(N):
            n = (r + 1) % N
            kept[n].append(cut(came, r, 4 * K))
            for w in (1, 2):
                for g in range(8):
                    k = np.flatnonzero(delay[r][g] == w)[::-1]
                    new = np.full(C, -1)
                    new[target[r][g, k]] = K * t + k
                    due[n, t + w, g] = np.where(due[n, t + w, g] < 0, new, due[n, t + w, g])
    y, ol = np.zeros((N, 128, C), np.float32), np.zeros((N, 8, K), np.float32)
    oc, osc = np.zeros((N, 128, 4 * C), np.uint8), np.zeros((N, 16, C), np.uint8)
    for r in range(N):
        q = mx_ref.quantize(now[r])
        y[r] = mx_ref.matmul(mx_ref.quantize(v[r]), q)
        ol[r] = lists[r]
        oc[r], osc[r] = emit(q)
    return {"y": y, "ol": ol, "oc": oc, "osc": osc}

@@ -1,0 +1,410 @@
+from concourse.mybir import dt, AluOpType, ActivationFunctionType
+
+C, K, R = 320, 160, 3
+P = 2576
+TOP = 480
+BIG = 16384.0
+NO = 2048.0
+F32, BF, F16, I32, U16, Q4, U8 = "float32", "bfloat16", "float16", "int32", "uint16", "float8_e4m3fn_x4", "uint8"
+
+
+def sb(n, t):
+    return ("sbuf", [128, n], t)
+
+
+SCRATCH = {
+    "st": sb(3 * P + 1280 + 1280, BF),
+    "ub": sb(512, BF), "vb": sb(512, BF), "tgi": sb(20, I32), "tgu": sb(20, U16),
+    "uq": sb(128, Q4), "us": sb(128, U8), "upq": sb(256, Q4), "ups": sb(256, U8), "vq": sb(128, Q4), "vs": sb(128, U8),
+    "wq": sb(512, Q4), "wp": sb(512, U8), "half": sb(512, BF), "eye": sb(2048, BF), "iq": sb(512, Q4), "ip": sb(512, U8),
+    "xq": sb(4 * C, Q4), "xs": sb(4 * C, U8), "et": sb(3 * 640, BF), "eq": sb(3 * K, Q4), "es": sb(3 * K, U8),
+    "ht": sb(3 * 640, BF), "hq": sb(3 * K, Q4), "hs": sb(3 * K, U8), "lq": sb(3 * K, Q4), "ls": sb(3 * K, U8),
+    "pi": sb(2, I32), "pj": sb(8, I32), "col": sb(8, F32), "uoi": sb(16, I32), "uo": sb(16, U16),
+    "jm": sb(C, BF), "cj": sb(C, F32), "km4": sb(K, BF),
+    "km": sb(C, BF), "ka": sb(C + 2, BF), "kr": sb(C, BF), "k1": sb(C, BF), "kb": sb(K, F32),
+    "cjf": sb(C, F32), "cjk": sb(C, F32), "mb": sb(32, F32), "cw": sb(20, F32), "cwf": sb(20, F32), "tj": sb(20, F32),
+    "bias": sb(22, F32), "acc": sb(22, F32), "junk": sb(22 * C, BF), "key": sb(C, F32), "kx": sb(C, F32), "k2": sb(C, F32),
+    "spu": sb(20, U16), "endu": sb(2, U16), "keys": sb(C, F32), "keyh": sb(C, F32), "ki": sb(20, I32), "kf": sb(20, F32),
+    "sig": sb(20, U16), "tbc": sb(C + 8, F32), "dk": sb(C, F32),
+    "r1": sb(6, I32), "r2": sb(6, F32), "r3": sb(6, F32), "rep": sb(6, U16), "bq": sb(80, F32), "xo": sb(80, F32),
+    "nr": sb(C + 2, BF), "prev": sb(C, F32), "hh": sb(C, BF), "ww": sb(C, F16), "wh": sb(C, F16),
+    "ta": sb(20, F32), "pos": sb(3 * 24, F32), "posu": sb(20, U16), "sc": sb(3 * 496, F32), "sh": sb(K, F32), "eo": sb(40, U16),
+    "ti": sb(40, I32), "tm": sb(40, I32), "t4": sb(120, U16), "lt4": sb(120, U16),
+    "sg": sb(C, F32), "na": sb(C, BF), "nb": sb(C, BF), "ns": sb(C, F16), "pen": sb(C, F32),
+    "lbn": sb(C, F32), "lb1": sb(C, F32), "lb2": sb(C, F32), "w2": sb(C, F32), "y2": sb(3 * C, F32),
+    "vn": sb(C, F32), "va": sb(C, F32), "vl": sb(2 * C, F32), "so": sb(C + 8, F32),
+    "win": sb(3 * 32, F32), "lwin": sb(3 * 24, F32),
+    "f1": sb(80, F32), "c1": sb(80, F32), "i1": sb(80, F32), "i2": sb(80, F32), "fo": sb(80, U16),
+    "a1": sb(640, BF), "m2": sb(640, BF),
+    "oi": sb(K, I32), "oe": sb(K, F32), "oo": sb(K, F32), "yo": sb(C, F32),
+    "ps": ("psum", [128, 4096], F32),
+}
+SEMAPHORES = (["cv", "cs", "ct", "cg", "sent", "lx", "ltg", "lu", "lv", "lw", "out"]
+              + ["at%d" % t for t in range(R)] + ["ah%d" % t for t in range(R)] + ["aw%d" % t for t in range(R)])
+
+
+def rank_program(g, core, T, topo):
+    rank = T.rank_of(core)
+    if rank is None:
+        return
+    A, F = AluOpType, ActivationFunctionType
+    n = len(T.cores)
+    nxt, prv = T.cores[(rank + 1) % n], T.cores[(rank - 1) % n]
+    rid, pid = topo.addr(nxt)[0], topo.addr(nxt)[1]
+    out_mask, out_n, in_n = topo.mask(core, nxt), len(topo.engines(core, nxt)), len(topo.engines(prv, core))
+    V, S, PE = g.vector, g.scalar, g.tensor
+    queue = {"v": V, "s": S, "t": PE, "g": g, "y": g.sync}
+    count = {"v": 0, "s": 0, "t": 0, "g": 0}
+    seen = {q: {} for q in queue}
+    wrote, readers = {}, {}
+    sent = [0]
+
+    def wait(q, tok):
+        if seen[q].get(tok[0], 0) < tok[1]:
+            queue[q].wait_ge(T.sem[tok[0]], tok[1])
+            seen[q][tok[0]] = tok[1]
+
+    def order(q, r, w):
+        need = {}
+        toks = [wrote[k] for k in list(r) + list(w) if k in wrote]
+        for k in w:
+            toks += readers.get(k, [])
+        for s, c in toks:
+            need[s] = max(need.get(s, 0), c)
+        for s in need:
+            wait(q, (s, need[s]))
+
+    def done(tok, r, w):
+        for k in r:
+            readers.setdefault(k, []).append(tok)
+        for k in w:
+            wrote[k] = tok
+            readers[k] = []
+
+    def op(q, call, r, w):
+        r, w = r.split(), w.split()
+        order(q, r, w)
+        count[q] += 1
+        call().then_inc(T.sem["c" + q], 1)
+        done(("c" + q, count[q]), r, w)
+
+    def load(q, sem, pairs, w):
+        for o, i in pairs:
+            queue[q].dma_start(o, i).then_inc(T.sem[sem], 16)
+        done((sem, 16 * len(pairs)), [], w.split())
+
+    def store(q, o, i, r):
+        order(q, r.split(), [])
+        queue[q].dma_start(o, i).then_inc(T.sem.out, 16)
+
+    def send(o, i, sem, r):
+        order("g", r.split(), [])
+        g.remote_dma(o, i, T.sem[sem], T.sem.sent, pid, rid, out_mask)
+        sent[0] += out_n
+
+    def ts(o, i, s1, s2, o0, o1, r, w):
+        if o1 is None:
+            op("v", lambda: V.tensor_scalar(o, i, s1, None, o0), r, w)
+        else:
+            op("v", lambda: V.tensor_scalar(o, i, s1, s2, o0, o1), r, w)
+
+    def tt(o, a, b, alu, r, w):
+        op("v", lambda: V.tensor_tensor(o, a, b, alu), r, w)
+
+    def cp(o, i, r, w):
+        op("v", lambda: V.tensor_copy(o, i), r, w)
+
+    def scan(o, d0, d1, init, o0, o1, r, w):
+        op("v", lambda: V.tensor_tensor_scan(o, d0, d1, init, o0, o1), r, w)
+
+    def act(o, i, f, r, w, bias=0.0, scale=1.0, acc=None):
+        if f == F.Copy and scale == 1.0:
+            op("s", lambda: S.activation(o, i, f), r, w)
+        elif f == F.Copy:
+            op("s", lambda: S.activation(o, i, f, scale=scale), r, w)
+        else:
+            op("s", lambda: S.activation(o, i, f, bias=bias, scale=scale, accum_out=acc), r, w)
+
+    def quant(q, s, i, r, w):
+        op("v", lambda: V.quantize_mx(q, s, i), r, w)
+
+    def bank(b, m):
+        return T.ps[:, 512 * b:512 * b + m]
+
+    def mm(b, m, lq, ls, rq, rs, r):
+        op("t", lambda: PE.matmul_mx(bank(b, m), lq, ls, rq, rs, True, True), r, "ps%d" % b)
+
+    def iota(o, pat, ch, w, whole=False, base=0):
+        if whole:
+            op("g", lambda: g.iota(o, pat, base, ch), "", w)
+        else:
+            op("g", lambda: g.iota(o, pat, base, ch, allow_small_or_imprecise_dtypes=True), "", w)
+
+    def const(o, m, c, w):
+        iota(o, [[0, m]], 0, w, base=c)
+
+    def X(t):
+        return P * t + 1280
+
+    st = T.st
+    icol, tcol, qcol, k1col, w0col, mbcol = [T.col[:, i:i + 1] for i in range(6)]
+
+    load("y", "ltg", [(T.tgi[:], T.tg[:])], "tgi")
+    load("s", "lu", [(T.ub[:], T.u[:])], "ub")
+    load("y", "lx", [(st[:, X(0):X(0) + 1280], T.x[:])], "x0")
+    load("y", "lw", [(T.wq[:].bitcast(dt.uint8), T.wc[:]), (T.wp[:], T.ws[:])], "wq")
+    load("y", "lv", [(T.vb[:], T.v[:])], "vb")
+    for t in range(R):
+        wrote["lt4%d" % t] = ("at%d" % t, in_n)
+        wrote["lq%d" % t] = ("ah%d" % t, 2 * in_n)
+        wrote["lwin%d" % t] = ("aw%d" % t, in_n)
+
+    iota(T.pi[:, 0:1], [[0, 1]], 1, "pi", True)
+    iota(T.jm[:], [[0, 20], [1, 16]], 0, "jm")
+    iota(T.uoi[:], [[1, 2], [16, 8]], 0, "uoi", True)
+    const(T.ka[:, 0:1], 1, 0, "ka0")
+    const(T.nr[:, 0:1], 1, 1, "nr0")
+    iota(T.cjk[:], [[4096, C]], 0, "cjk")
+    iota(T.km4[:], [[0, 40], [1, 4]], 0, "km4")
+    const(T.sc[:, 0:K], K, 4096 * C, "sc0")
+    const(st[:, X(0) + 1280:X(0) + 1296], 16, 0, "z0")
+    op("v", lambda: V.memset(T.half[:], 0.5), "", "half")
+    scan(T.cj[:], T.half[:, 0:C], T.half[:, 0:C], -1.0, A.add, A.add, "half", "cj")
+    ts(T.pj[:, 0:1], T.pi[:, 0:1], 15, None, A.bitwise_and, None, "pi", "pj0")
+    ts(T.pj[:, 1:2], T.pi[:, 0:1], 3, None, A.bitwise_and, None, "pi", "pj1")
+    ts(T.pj[:, 2:3], T.pi[:, 0:1], 2, 3, A.logical_shift_right, A.bitwise_and, "pi", "pj2")
+    act(T.cjf[:], T.cj[:], F.Copy, "cj", "cjf", scale=-1.0 / 512)
+    cp(T.col[:, 0:3], T.pj[:, 0:3], "pj0 pj1 pj2", "col")
+    ts(T.cw[:], T.cj[:, 0:C:16], icol, None, A.add, None, "cj col", "cw")
+    ts(mbcol, icol, 512.0, BIG, A.mult, A.add, "col", "mbcol")
+    ts(T.cwf[:], T.cw[:], -1.0 / 512, None, A.mult, None, "cw", "cwf")
+    ts(T.km[:], T.jm[:], icol, BIG, A.is_equal, A.mult, "jm col", "km")
+    cp(T.uo[:], T.uoi[:], "uoi", "uo")
+    act(T.bias[:, 20:22], T.cw[:, 0:2], F.Identity, "cw", "biasb", bias=15.25, scale=16.0)
+    act(T.mb[:], T.cj[:, 0:32], F.Identity, "cj mbcol", "mb", bias=mbcol, scale=8192.0)
+    act(T.tj[:], T.cw[:], F.Identity, "cw", "tj", bias=float(TOP), scale=-1.0)
+    for b in range(4):
+        act(T.xo[:, 20 * b:20 * b + 20], T.cw[:], F.Identity, "cw", "xo%d" % b, bias=C + 0.25 * b)
+        act(T.bq[:, 20 * b:20 * b + 20], T.cw[:], F.Identity, "cw", "bq%d" % b, bias=0.25 * b, scale=0.0)
+
+    def ranks(a, b):
+        for m in range(a, b):
+            act(T.junk[:, C * m:C * m + C], T.key[:], F.Sign, "key biasa biasb", "acc%d" % m,
+                bias=T.bias[:, m:m + 1], scale=-1.0, acc=T.acc[:, m:m + 1])
+
+    cp(T.tgu[:], T.tgi[:], "tgi", "tgu")
+    tt(T.bias[:, 0:20], T.tgi[:], T.cwf[:], A.add, "tgi cwf", "biasa")
+    tt(T.key[:], T.cj[:].indirect(T.tgu[:]), T.cjf[:], A.add, "cj tgu cjf", "key")
+    quant(T.uq[:], T.us[:], T.ub[:], "ub", "uq")
+    ranks(0, 1)
+    cp(T.upq[:].bitcast(dt.uint32), T.uq[:].bitcast(dt.uint32).indirect(T.uo[:]), "uq uo", "upq")
+    act(T.ups[:], T.us[:].indirect(T.uo[:]), F.Copy, "uq uo", "ups")
+    for b in range(4):
+        op("g", lambda: g.affine_select(T.eye[:, 512 * b:512 * b + 512], T.half[:], [[1, 512]], A.is_equal, 0.0, -b, -4),
+           "half", "eye%d" % b)
+
+    def y2(t):
+        return T.y2[:, C * t:C * t + C]
+
+    def unfired(t):
+        scan(T.ns[:], T.na[:], T.nb[:], 512.0, A.add, A.subtract, "na nb", "ns")
+        act(T.pen[:], T.ns[:], F.Relu, "ns", "pen", bias=-2 * NO * (K - 0.5), scale=2 * NO)
+
+    def entries(t):
+        scan(T.w2[:], T.dk[:], T.nr[:, 0:C], 1.0, A.add, A.subtract, "dk nr nr0", "w2")
+
+    def counting(t):
+        tt(y2(t), T.w2[:], T.pen[:], A.add, "w2 pen", "y2%d" % t)
+
+    def late(t):
+        tt(T.vl[:, C * t:C * t + C], y2(t).indirect(T.sig[:]), T.lb2[:], A.add, "y2%d sig lb2" % t, "vl%d" % t)
+
+    def fired(t):
+        ts(T.f1[:], T.pos[:, 24 * t:24 * t + 20].indirect(T.rep[:, 0:5]), float(K), float(K), A.is_lt, A.mult,
+           "pos%d rep" % t, "f1")
+
+    def fire(t):
+        x, xk = X(t), "x%d" % t
+        xq, xs = T.xq[:, C * t:C * t + C], T.xs[:, C * t:C * t + C]
+        quant(xq, xs, st[:, x:x + 1280], xk, "xq%d" % t)
+        mm(4, C, T.upq[:, 0:128], T.ups[:, 0:128], xq, xs, "upq ups xq%d" % t)
+        mm(5, C, T.upq[:, 128:256], T.ups[:, 128:256], xq, xs, "upq ups xq%d" % t)
+        if t == 0:
+            ranks(1, 6)
+            ts(k1col, icol, 15.0, 1.0, A.is_lt, A.add, "col", "k1col")
+            ts(w0col, icol, 15.0, -(TOP + 1.0), A.is_lt, A.mult, "col", "w0col")
+            ts(T.ka[:, 1:C + 1], T.jm[:], icol, -1.0 / BIG, A.is_equal, A.mult, "jm col", "ka")
+            ts(T.k1[:], T.jm[:], 0.0, k1col, A.mult, A.add, "jm k1col", "k1")
+            ts(T.nr[:, 1:C + 1], bank(4, C), 0.0, None, A.is_le, None, "", "ps4 nr")
+            scan(T.kr[:], T.ka[:, 0:C], T.km[:], 0.0, A.mult, A.subtract, "ka ka0 km", "kr")
+            act(T.sg[:], bank(5, C), F.Sign, "", "ps5 sg")
+            act(T.kx[:], T.key[:], F.Copy, "key", "kx", scale=512.0)
+            act(T.lbn[:], T.sg[:], F.Relu, "sg", "lbn", scale=NO)
+            ranks(6, 10)
+        else:
+            if t == 1:
+                late(0)
+            act(T.sg[:], bank(5, C), F.Sign, "", "ps5 sg")
+            tt(T.nr[:, 1:C + 1], bank(4, C), T.prev[:], A.is_le, "prev", "ps4 nr")
+            act(T.na[:], T.nr[:, 1:C + 1], F.Copy, "nr", "na", scale=512.0)
+            act(T.nb[:], T.nr[:, 0:C], F.Identity, "nr nr0", "nb", bias=-1.0, scale=513.0)
+            act(T.lb1[:], T.sg[:].indirect(T.sig[:]), F.Relu, "sg sig", "lb1", scale=NO)
+            if t < R - 1:
+                act(T.prev[:], bank(4, C), F.Copy, "", "ps4 prev")
+        scan(T.ww[:], T.k1[:], T.nr[:, 0:C], w0col, A.add, A.subtract, "k1 nr nr0 w0col", "ww")
+        scan(T.hh[:], T.kr[:], T.nr[:, 1:C + 1], 0.0, A.add, A.max, "kr nr", "hh")
+        scan(T.wh[:], T.km[:], T.ww[:], 0.0, A.add, A.min, "km ww", "wh")
+        tt(T.ta[:], T.hh[:, 15:C:16], T.tj[:], A.mult, "hh tj", "ta")
+        pos = T.pos[:, 24 * t:24 * t + 20]
+        tt(pos, T.wh[:, 15:C:16], T.ta[:], A.add, "wh ta", "pos%d" % t)
+        if t == 0:
+            tt(T.k2[:], T.cj[:].indirect(T.tgu[:]), T.cjk[:], A.add, "cj tgu cjk", "k2")
+        cp(T.posu[:], pos, "pos%d" % t, "posu")
+        if t == 0:
+            ts(T.kb[:], T.km4[:], qcol, 2.0 ** 22, A.is_equal, A.mult, "km4 col", "kb")
+        sc = T.sc[:, 496 * t:496 * t + 496]
+        cp(sc.indirect(T.posu[:]), T.k2[:], "k2 posu", "sc%d" % t)
+        if t > 0:
+            unfired(t)
+        scan(T.sh[:], T.kb[:], T.sc[:, 496 * t:496 * t + K], 0.0, A.add, A.min, "kb sc%d" % t, "sh")
+        ts(T.eo[:], T.sh[:, 3:K:4], 1.0 / 1024, tcol, A.mult, A.add, "sh col", "eo")
+        cp(T.ti[:], T.sh[:, 3:K:4], "sh", "ti")
+        e0, xw = 640 * t, st[:, x:x + 1296]
+        src = "%s z%d eo" % (xk, t)
+        cp(T.et[:, e0:e0 + 320], xw.indirect(T.eo[:, 0:20]), src, "ea")
+        act(T.et[:, e0 + 320:e0 + 640], xw.indirect(T.eo[:, 20:40]), F.Copy, src, "eb")
+        if t == 0:
+            ranks(10, 11)
+        ts(T.tm[:], T.ti[:], 4095, None, A.bitwise_and, None, "ti", "tm")
+        eq, es = T.eq[:, K * t:K * t + K], T.es[:, K * t:K * t + K]
+        quant(eq, es, T.et[:, e0:e0 + 640], "ea eb", "eq")
+        for b in (2, 0, 3, 1):
+            mm(b, K, T.wq[:, 128 * b:128 * b + 128], T.wp[:, 128 * b:128 * b + 128], eq, es, "wq eq")
+        ts(T.t4[:, 40 * t:40 * t + 40], T.tm[:], 4.0, tcol, A.mult, A.add, "tm col", "t4%d" % t)
+        send(T.lt4[:, 40 * t:40 * t + 40], T.t4[:, 40 * t:40 * t + 40], "at%d" % t, "t4%d" % t)
+        if t > 0:
+            entries(t)
+        else:
+            ts(T.na[:], T.nr[:, 1:C + 1], 512.0, None, A.mult, None, "nr", "na")
+        for b in range(4):
+            h = T.ht[:, e0 + b:e0 + 640:4]
+            if b < 2:
+                ts(h, bank(b, K), 0.0, 0.03125, A.max, A.mult, "", "ps%d h%d" % (b, b))
+            else:
+                act(h, bank(b, K), F.Relu, "", "ps%d h%d" % (b, b), scale=0.03125)
+        hq, hs = T.hq[:, K * t:K * t + K], T.hs[:, K * t:K * t + K]
+        quant(hq, hs, T.ht[:, e0:e0 + 640], "h0 h1 h2 h3", "hq%d" % t)
+        send(T.lq[:, K * t:K * t + K].bitcast(dt.uint8), hq.bitcast(dt.uint8), "ah%d" % t, "hq%d" % t)
+        send(T.ls[:, K * t:K * t + K], hs, "ah%d" % t, "hq%d" % t)
+        if t == 0:
+            ts(T.nb[:], T.nr[:, 0:C], 513.0, -1.0, A.mult, A.add, "nr nr0", "nb")
+            const(T.tbc[:, 0:1], 1, 0, "tbc0")
+            const(T.so[:, 0:1], 1, 0, "so0")
+            for k in (1, 2):
+                const(st[:, X(k) + 1280:X(k) + 1296], 16, 0, "z%d" % k)
+                const(T.sc[:, 496 * k:496 * k + K], K, 4096 * C, "sc%d" % k)
+            tt(T.tbc[:, 1:C + 1], T.km[:].indirect(T.tgu[:]), T.kx[:], A.add, "km tgu kx", "tbc")
+            ranks(11, 14)
+            unfired(t)
+            ranks(14, 22)
+            ts(T.r1[:], T.cw[:, 0:6], 0.05, -0.475, A.mult, A.add, "cw", "r1")
+            tt(T.dk[:], T.tbc[:, 0:C], T.tbc[:, 1:C + 1], A.subtract, "tbc tbc0", "dk")
+            ts(T.r2[:], T.r1[:], -20.0, None, A.mult, None, "r1", "r2")
+            entries(t)
+            tt(T.r3[:], T.r2[:], T.cw[:, 0:6], A.add, "r2 cw", "r3")
+            counting(t)
+            cp(T.rep[:], T.r3[:], "r3", "rep")
+            tt(T.vn[:], y2(t), T.lbn[:], A.add, "y20 lbn", "vn")
+            fired(t)
+            quant(T.iq[:], T.ip[:], T.eye[:], "eye0 eye1 eye2 eye3", "iq")
+            accs = " ".join("acc%d" % m for m in range(22))
+            ts(T.spu[:], T.acc[:, 0:20], 0.5, 159.5, A.mult, A.add, accs, "spu")
+            ts(T.endu[:], T.acc[:, 20:22], 0.5, 160.0, A.mult, A.add, accs, "endu")
+            cp(T.va[:].indirect(T.spu[:]), T.vn[:], "vn spu", "va")
+            second, sk = T.va[:], "va"
+        else:
+            counting(t)
+            fired(t)
+            tt(T.va[:], y2(t).indirect(T.sig[:]), T.lb1[:], A.add, "y2%d sig lb1" % t, "va")
+            second, sk = T.vl[:, C * (t - 1):C * t], "va vl%d" % (t - 1)
+        if t == 1:
+            act(T.lb2[:], T.lb1[:], F.Identity, "lb1", "lb2", bias=NO - P / 4, scale=-1.0)
+        act(T.a1[:], st[:, x:x + 1280].indirect(T.lt4[:, 40 * t:40 * t + 40]), F.Copy, "%s lt4%d" % (xk, t), "a1", scale=0.5)
+        if t == 0:
+            act(T.prev[:], bank(4, C), F.Copy, "", "ps4 prev")
+        tt(T.c1[:], T.f1[:], T.bq[:], A.add, "f1 bq0 bq1 bq2 bq3", "c1")
+        scan(T.so[:, 1:C + 1], T.va[:], second, 0.0, A.min, A.min, sk, "so")
+        tt(T.win[:, 32 * t:32 * t + 32], T.so[:, 0:C + 1].indirect(T.endu[:]), T.mb[:], A.add, "so so0 endu mb", "win%d" % t)
+        send(T.lwin[:, 24 * t:24 * t + 20], T.win[:, 32 * t:32 * t + 20], "aw%d" % t, "win%d" % t)
+        if t == 0:
+            cp(T.keys[:].indirect(T.spu[:]), T.key[:], "key spu", "keys")
+        else:
+            d = P * (t - 1)
+            tt(T.m2[:], st[:, x:x + 1280].indirect(T.lt4[:, 40 * (t - 1):40 * t]), st[:, d:d + 640], A.add,
+               "%s lt4%d" % (xk, t - 1), "m2")
+            act(st[:, d + 640:d + 1280], T.m2[:], F.Copy, "m2", "m%d" % (t - 1), scale=0.5)
+        if t == 1:
+            late(1)
+        if t == R - 1:
+            quant(T.vq[:], T.vs[:], T.vb[:], "vb", "vq")
+            ts(T.oi[:], T.sc[:, 496 * t:496 * t + K], 1.0 / 4096, None, A.mult, None, "sc%d" % t, "oi")
+            ts(T.oe[:], T.oi[:], float(C), -(C + 1.0), A.is_ge, A.mult, "oi", "oe")
+            tt(T.oo[:], T.oi[:], T.oe[:], A.add, "oi oe", "oo")
+            store("y", T.ol[:], T.oo[0:128:16, :], "oo")
+
+    def merge(t):
+        d, lo = P * (t - 1), P * max(t - 2, 0)
+        lq, ls = T.lq[:, K * (t - 1):K * t], T.ls[:, K * (t - 1):K * t]
+        for b in range(4):
+            for k in (b, 4 + b):
+                mm(k, K, T.iq[:, 128 * b:128 * b + 128], T.ip[:, 128 * b:128 * b + 128], lq, ls, "iq lq%d" % (t - 1))
+        if t == 1:
+            scan(T.keyh[:], T.km[:], T.keys[:], 0.0, A.add, A.min, "km keys", "keyh")
+        for b in range(4):
+            tt(st[:, d + 640 + b:d + 1280:4], bank(b, K), T.a1[:, b:640:4], A.add, "a1", "ps%d n%d%d" % (b, t, b))
+            act(st[:, d + b:d + 640:4], bank(4 + b, K), F.Copy, "", "ps%d d%d%d" % (4 + b, t, b), scale=2.0)
+            if t == 1 and b == 0:
+                ts(T.ki[:], T.keyh[:, 15:C:16], 0.3125, None, A.add, None, "keyh", "ki")
+            if t == 1 and b == 1:
+                tt(T.kf[:], T.ki[:], T.keyh[:, 15:C:16], A.subtract, "keyh ki", "kf")
+            if t == 1 and b == 2:
+                ts(T.sig[:], T.kf[:], 512.0, None, A.mult, None, "kf", "sig")
+        if t == 1:
+            act(T.lb2[:], T.lbn[:].indirect(T.sig[:]), F.Identity, "lbn sig", "lb2", bias=NO - P / 4, scale=-1.0)
+        tt(T.i1[:], T.lwin[:, 24 * (t - 1):24 * (t - 1) + 20].indirect(T.rep[:, 0:5]), T.c1[:], A.add,
+           "lwin%d rep c1" % (t - 1), "i1")
+        tt(T.i2[:], T.i1[:], T.xo[:], A.min, "i1 xo0 xo1 xo2 xo3", "i2")
+        ts(T.fo[:], T.i2[:], (d - lo) / 4, 4.0, A.add, A.mult, "i2", "fo")
+        w = st[:, lo:d + 2560]
+        src = "fo x%d m%d m%d " % (t - 1, t - 1, t - 2) + " ".join("n%d%d d%d%d" % (t, b, t, b) for b in range(4))
+        x = X(t)
+        for b in (0, 2, 1, 3):
+            o, i = st[:, x + b:x + 1280:4], w.indirect(T.fo[:, 20 * b:20 * b + 20])
+            if b < 2:
+                cp(o, i, src, "x%d%d" % (t, b))
+            else:
+                act(o, i, F.Copy, src, "x%d%d" % (t, b))
+        for q in ("v", "s"):
+            wait(q, wrote["x%d1" % t])
+            wait(q, wrote["x%d3" % t])
+
+    for t in range(R):
+        if t > 0:
+            merge(t)
+        fire(t)
+    merge(R)
+    x, c0 = X(R), C * R
+    quant(T.xq[:, c0:c0 + C], T.xs[:, c0:c0 + C], st[:, x:x + 1280], "", "xq3")
+    for h in range(2):
+        a = c0 + K * h
+        mm(h, K, T.vq[:], T.vs[:], T.xq[:, a:a + K], T.xs[:, a:a + K], "vq xq3")
+    store("y", T.oc[:], T.xq[:, c0:c0 + C].bitcast(dt.uint8), "xq3")
+    for k in range(4):
+        store("y", T.osc[4 * k:4 * k + 4, :], T.xs[32 * k:32 * k + 4, c0:c0 + C], "xq3")
+    cp(T.yo[:, 0:K], bank(0, K), "", "ps0 ya")
+    act(T.yo[:, K:C], bank(1, K), F.Copy, "", "ps1 yb")
+    store("s", T.y[:], T.yo[:], "ya yb")
+    g.wait_ge(T.sem.out, 16 * 7)
+    g.wait_ge(T.sem.sent, sent[0])
+    for q in ("v", "s", "t", "g"):
+        wait("g", ("c" + q, count[q]))

@@ -23,7 +23,8 @@ SCRATCH = {
     "jm": sb(C, BF), "cj": sb(C, F32), "km4": sb(K, BF),
     "km": sb(C, BF), "ka": sb(C + 2, BF), "kr": sb(C, BF), "k1": sb(C, BF), "kb": sb(K, F32),
     "cjf": sb(C, F32), "cjk": sb(C, F32), "mb": sb(32, F32), "cw": sb(20, F32), "cwf": sb(20, F32), "tj": sb(20, F32),
-    "bias": sb(22, F32), "acc": sb(22, F32), "junk": sb(22 * C, BF), "key": sb(C, F32), "kx": sb(C, F32), "k2": sb(C, F32),
+    "bias": sb(22, F32), "acc": sb(22, F32), "junk": sb(22 * C, BF), "key": sb(C, F32), "k2": sb(C, F32),
+    "kx": sb(C, F32), "kmx": sb(C, F32), "tb0": sb(C, F32),
     "spu": sb(20, U16), "endu": sb(2, U16), "keys": sb(C, F32), "keyh": sb(C, F32), "ki": sb(20, I32), "kf": sb(20, F32),
     "sig": sb(20, U16), "tbc": sb(C + 8, F32), "dk": sb(C, F32),
     "r1": sb(6, I32), "r2": sb(6, F32), "r3": sb(6, F32), "rep": sb(6, U16), "bq": sb(80, F32), "xo": sb(80, F32),
@@ -32,14 +33,14 @@ SCRATCH = {
     "ti": sb(40, I32), "tm": sb(40, I32), "t4": sb(120, U16), "lt4": sb(120, U16),
     "sg": sb(C, F32), "na": sb(C, BF), "nb": sb(C, BF), "ns": sb(C, F16), "pen": sb(C, F32),
     "lbn": sb(C, F32), "lb1": sb(C, F32), "lb2": sb(C, F32), "w2": sb(C, F32), "y2": sb(3 * C, F32),
-    "vn": sb(C, F32), "va": sb(C, F32), "vl": sb(2 * C, F32), "so": sb(C + 8, F32),
+    "va": sb(C, F32), "vl": sb(2 * C, F32), "so": sb(C + 8, F32),
     "win": sb(3 * 32, F32), "lwin": sb(3 * 24, F32),
     "f1": sb(80, F32), "c1": sb(80, F32), "i1": sb(80, F32), "i2": sb(80, F32), "fo": sb(80, U16),
     "a1": sb(640, BF), "m2": sb(640, BF),
     "oi": sb(K, I32), "oe": sb(K, F32), "oo": sb(K, F32), "yo": sb(C, F32),
     "ps": ("psum", [128, 4096], F32),
 }
-SEMAPHORES = (["cv", "cs", "ct", "cg", "sent", "lx", "ltg", "lu", "lv", "lw", "out"]
+SEMAPHORES = (["cv", "cs", "ct", "cg", "sent", "lx", "ltg", "lu", "lv", "lw", "out", "ga", "gb", "gm1", "gm2"]
               + ["at%d" % t for t in range(R)] + ["ah%d" % t for t in range(R)] + ["aw%d" % t for t in range(R)])
 
 
@@ -96,6 +97,11 @@ def rank_program(g, core, T, topo):
     def store(q, o, i, r):
         order(q, r.split(), [])
         queue[q].dma_start(o, i).then_inc(T.sem.out, 16)
+
+    def add(o, i, sem, r, w):
+        order("g", r.split(), [w])
+        g.dma_start(o, i, accum_op=A.add).then_inc(T.sem[sem], 16)
+        done((sem, 16), r.split(), [w])
 
     def send(o, i, sem, r):
         order("g", r.split(), [])
@@ -174,6 +180,7 @@ def rank_program(g, core, T, topo):
     ts(T.pj[:, 1:2], T.pi[:, 0:1], 3, None, A.bitwise_and, None, "pi", "pj1")
     ts(T.pj[:, 2:3], T.pi[:, 0:1], 2, 3, A.logical_shift_right, A.bitwise_and, "pi", "pj2")
     act(T.cjf[:], T.cj[:], F.Copy, "cj", "cjf", scale=-1.0 / 512)
+    act(T.kx[:], T.cj[:], F.Copy, "cj", "kx", scale=512.0)
     cp(T.col[:, 0:3], T.pj[:, 0:3], "pj0 pj1 pj2", "col")
     ts(T.cw[:], T.cj[:, 0:C:16], icol, None, A.add, None, "cj col", "cw")
     ts(mbcol, icol, 512.0, BIG, A.mult, A.add, "col", "mbcol")
@@ -183,9 +190,6 @@ def rank_program(g, core, T, topo):
     act(T.bias[:, 20:22], T.cw[:, 0:2], F.Identity, "cw", "biasb", bias=15.25, scale=16.0)
     act(T.mb[:], T.cj[:, 0:32], F.Identity, "cj mbcol", "mb", bias=mbcol, scale=8192.0)
     act(T.tj[:], T.cw[:], F.Identity, "cw", "tj", bias=float(TOP), scale=-1.0)
-    for b in range(4):
-        act(T.xo[:, 20 * b:20 * b + 20], T.cw[:], F.Identity, "cw", "xo%d" % b, bias=C + 0.25 * b)
-        act(T.bq[:, 20 * b:20 * b + 20], T.cw[:], F.Identity, "cw", "bq%d" % b, bias=0.25 * b, scale=0.0)
 
     def ranks(a, b):
         for m in range(a, b):
@@ -198,6 +202,9 @@ def rank_program(g, core, T, topo):
     quant(T.uq[:], T.us[:], T.ub[:], "ub", "uq")
     ranks(0, 1)
     cp(T.upq[:].bitcast(dt.uint32), T.uq[:].bitcast(dt.uint32).indirect(T.uo[:]), "uq uo", "upq")
+    ts(k1col, icol, 15.0, 1.0, A.is_lt, A.add, "col", "k1col")
+    ts(w0col, icol, 15.0, -(TOP + 1.0), A.is_lt, A.mult, "col", "w0col")
+    ts(T.ka[:, 1:C + 1], T.jm[:], icol, -1.0 / BIG, A.is_equal, A.mult, "jm col", "ka")
     act(T.ups[:], T.us[:].indirect(T.uo[:]), F.Copy, "uq uo", "ups")
     for b in range(4):
         op("g", lambda: g.affine_select(T.eye[:, 512 * b:512 * b + 512], T.half[:], [[1, 512]], A.is_equal, 0.0, -b, -4),
@@ -210,9 +217,6 @@ def rank_program(g, core, T, topo):
         scan(T.ns[:], T.na[:], T.nb[:], 512.0, A.add, A.subtract, "na nb", "ns")
         act(T.pen[:], T.ns[:], F.Relu, "ns", "pen", bias=-2 * NO * (K - 0.5), scale=2 * NO)
 
-    def entries(t):
-        scan(T.w2[:], T.dk[:], T.nr[:, 0:C], 1.0, A.add, A.subtract, "dk nr nr0", "w2")
-
     def counting(t):
         tt(y2(t), T.w2[:], T.pen[:], A.add, "w2 pen", "y2%d" % t)
 
@@ -223,6 +227,9 @@ def rank_program(g, core, T, topo):
         ts(T.f1[:], T.pos[:, 24 * t:24 * t + 20].indirect(T.rep[:, 0:5]), float(K), float(K), A.is_lt, A.mult,
            "pos%d rep" % t, "f1")
 
+    def choice():
+        tt(T.c1[:], T.f1[:], T.bq[:], A.add, "f1 bq0 bq1 bq2 bq3", "c1")
+
     def fire(t):
         x, xk = X(t), "x%d" % t
         xq, xs = T.xq[:, C * t:C * t + C], T.xs[:, C * t:C * t + C]
@@ -231,19 +238,22 @@ def rank_program(g, core, T, topo):
         mm(5, C, T.upq[:, 128:256], T.ups[:, 128:256], xq, xs, "upq ups xq%d" % t)
         if t == 0:
             ranks(1, 6)
-            ts(k1col, icol, 15.0, 1.0, A.is_lt, A.add, "col", "k1col")
-            ts(w0col, icol, 15.0, -(TOP + 1.0), A.is_lt, A.mult, "col", "w0col")
-            ts(T.ka[:, 1:C + 1], T.jm[:], icol, -1.0 / BIG, A.is_equal, A.mult, "jm col", "ka")
+            tt(T.kmx[:], T.kx[:], T.km[:], A.add, "kx km", "kmx")
             ts(T.k1[:], T.jm[:], 0.0, k1col, A.mult, A.add, "jm k1col", "k1")
-            ts(T.nr[:, 1:C + 1], bank(4, C), 0.0, None, A.is_le, None, "", "ps4 nr")
             scan(T.kr[:], T.ka[:, 0:C], T.km[:], 0.0, A.mult, A.subtract, "ka ka0 km", "kr")
+            ts(T.nr[:, 1:C + 1], bank(4, C), 0.0, None, A.is_le, None, "", "ps4 nr")
+            tt(T.k2[:], T.cj[:].indirect(T.tgu[:]), T.cjk[:], A.add, "cj tgu cjk", "k2")
             act(T.sg[:], bank(5, C), F.Sign, "", "ps5 sg")
-            act(T.kx[:], T.key[:], F.Copy, "key", "kx", scale=512.0)
+            act(T.tb0[:], T.kmx[:].indirect(T.tgu[:]), F.Copy, "kmx tgu", "tb0", scale=-1.0)
             act(T.lbn[:], T.sg[:], F.Relu, "sg", "lbn", scale=NO)
-            ranks(6, 10)
+            add(T.tb0[:], T.lbn[:], "ga", "lbn", "tb0")
+            ranks(6, 19)
         else:
             if t == 1:
                 late(0)
+            act(T.m2[:], st[:, x:x + 1280].indirect(T.lt4[:, 40 * (t - 1):40 * t]), F.Copy, "lt4%d" % (t - 1), "m2")
+            wait("g", wrote["d%d3" % t])
+            add(T.m2[:], st[:, P * (t - 1):P * (t - 1) + 640], "gm%d" % t, "", "m2")
             act(T.sg[:], bank(5, C), F.Sign, "", "ps5 sg")
             tt(T.nr[:, 1:C + 1], bank(4, C), T.prev[:], A.is_le, "prev", "ps4 nr")
             act(T.na[:], T.nr[:, 1:C + 1], F.Copy, "nr", "na", scale=512.0)
@@ -258,10 +268,8 @@ def rank_program(g, core, T, topo):
         pos = T.pos[:, 24 * t:24 * t + 20]
         tt(pos, T.wh[:, 15:C:16], T.ta[:], A.add, "wh ta", "pos%d" % t)
         if t == 0:
-            tt(T.k2[:], T.cj[:].indirect(T.tgu[:]), T.cjk[:], A.add, "cj tgu cjk", "k2")
-        cp(T.posu[:], pos, "pos%d" % t, "posu")
-        if t == 0:
             ts(T.kb[:], T.km4[:], qcol, 2.0 ** 22, A.is_equal, A.mult, "km4 col", "kb")
+        cp(T.posu[:], pos, "pos%d" % t, "posu")
         sc = T.sc[:, 496 * t:496 * t + 496]
         cp(sc.indirect(T.posu[:]), T.k2[:], "k2 posu", "sc%d" % t)
         if t > 0:
@@ -271,78 +279,81 @@ def rank_program(g, core, T, topo):
         cp(T.ti[:], T.sh[:, 3:K:4], "sh", "ti")
         e0, xw = 640 * t, st[:, x:x + 1296]
         src = "%s z%d eo" % (xk, t)
-        cp(T.et[:, e0:e0 + 320], xw.indirect(T.eo[:, 0:20]), src, "ea")
-        act(T.et[:, e0 + 320:e0 + 640], xw.indirect(T.eo[:, 20:40]), F.Copy, src, "eb")
         if t == 0:
-            ranks(10, 11)
+            cp(T.et[:, e0:e0 + 640], xw.indirect(T.eo[:]), src, "ea eb")
+        else:
+            cp(T.et[:, e0:e0 + 320], xw.indirect(T.eo[:, 0:20]), src, "ea")
+            act(T.et[:, e0 + 320:e0 + 640], xw.indirect(T.eo[:, 20:40]), F.Copy, src, "eb")
         ts(T.tm[:], T.ti[:], 4095, None, A.bitwise_and, None, "ti", "tm")
         eq, es = T.eq[:, K * t:K * t + K], T.es[:, K * t:K * t + K]
         quant(eq, es, T.et[:, e0:e0 + 640], "ea eb", "eq")
-        for b in (2, 0, 3, 1):
+        for b in ((2, 0, 3, 1) if t else range(4)):
             mm(b, K, T.wq[:, 128 * b:128 * b + 128], T.wp[:, 128 * b:128 * b + 128], eq, es, "wq eq")
         ts(T.t4[:, 40 * t:40 * t + 40], T.tm[:], 4.0, tcol, A.mult, A.add, "tm col", "t4%d" % t)
         send(T.lt4[:, 40 * t:40 * t + 40], T.t4[:, 40 * t:40 * t + 40], "at%d" % t, "t4%d" % t)
         if t > 0:
-            entries(t)
+            scan(T.w2[:], T.dk[:], T.nr[:, 0:C], 0.0, A.add, A.subtract, "dk nr nr0", "w2")
         else:
             ts(T.na[:], T.nr[:, 1:C + 1], 512.0, None, A.mult, None, "nr", "na")
+            ts(T.nb[:], T.nr[:, 0:C], 513.0, -1.0, A.mult, A.add, "nr nr0", "nb")
         for b in range(4):
             h = T.ht[:, e0 + b:e0 + 640:4]
-            if b < 2:
+            if b < 2 or t == 0:
                 ts(h, bank(b, K), 0.0, 0.03125, A.max, A.mult, "", "ps%d h%d" % (b, b))
             else:
                 act(h, bank(b, K), F.Relu, "", "ps%d h%d" % (b, b), scale=0.03125)
         hq, hs = T.hq[:, K * t:K * t + K], T.hs[:, K * t:K * t + K]
+        if t == 0:
+            unfired(t)
         quant(hq, hs, T.ht[:, e0:e0 + 640], "h0 h1 h2 h3", "hq%d" % t)
         send(T.lq[:, K * t:K * t + K].bitcast(dt.uint8), hq.bitcast(dt.uint8), "ah%d" % t, "hq%d" % t)
         send(T.ls[:, K * t:K * t + K], hs, "ah%d" % t, "hq%d" % t)
         if t == 0:
-            ts(T.nb[:], T.nr[:, 0:C], 513.0, -1.0, A.mult, A.add, "nr nr0", "nb")
             const(T.tbc[:, 0:1], 1, 0, "tbc0")
             const(T.so[:, 0:1], 1, 0, "so0")
             for k in (1, 2):
                 const(st[:, X(k) + 1280:X(k) + 1296], 16, 0, "z%d" % k)
                 const(T.sc[:, 496 * k:496 * k + K], K, 4096 * C, "sc%d" % k)
-            tt(T.tbc[:, 1:C + 1], T.km[:].indirect(T.tgu[:]), T.kx[:], A.add, "km tgu kx", "tbc")
-            ranks(11, 14)
-            unfired(t)
-            ranks(14, 22)
+            ranks(19, 22)
             ts(T.r1[:], T.cw[:, 0:6], 0.05, -0.475, A.mult, A.add, "cw", "r1")
-            tt(T.dk[:], T.tbc[:, 0:C], T.tbc[:, 1:C + 1], A.subtract, "tbc tbc0", "dk")
+            tt(T.w2[:], T.ns[:], T.tb0[:], A.add, "ns tb0", "w2")
             ts(T.r2[:], T.r1[:], -20.0, None, A.mult, None, "r1", "r2")
-            entries(t)
-            tt(T.r3[:], T.r2[:], T.cw[:, 0:6], A.add, "r2 cw", "r3")
             counting(t)
-            cp(T.rep[:], T.r3[:], "r3", "rep")
-            tt(T.vn[:], y2(t), T.lbn[:], A.add, "y20 lbn", "vn")
-            fired(t)
-            quant(T.iq[:], T.ip[:], T.eye[:], "eye0 eye1 eye2 eye3", "iq")
             accs = " ".join("acc%d" % m for m in range(22))
             ts(T.spu[:], T.acc[:, 0:20], 0.5, 159.5, A.mult, A.add, accs, "spu")
             ts(T.endu[:], T.acc[:, 20:22], 0.5, 160.0, A.mult, A.add, accs, "endu")
-            cp(T.va[:].indirect(T.spu[:]), T.vn[:], "vn spu", "va")
+            cp(T.va[:].indirect(T.spu[:]), y2(t), "y20 spu", "va")
             second, sk = T.va[:], "va"
         else:
             counting(t)
-            fired(t)
             tt(T.va[:], y2(t).indirect(T.sig[:]), T.lb1[:], A.add, "y2%d sig lb1" % t, "va")
             second, sk = T.vl[:, C * (t - 1):C * t], "va vl%d" % (t - 1)
         if t == 1:
             act(T.lb2[:], T.lb1[:], F.Identity, "lb1", "lb2", bias=NO - P / 4, scale=-1.0)
+        if t > 0:
+            d = P * (t - 1)
+            act(st[:, d + 640:d + 1280], T.m2[:], F.Copy, "m2", "m%d" % (t - 1), scale=0.5)
         act(T.a1[:], st[:, x:x + 1280].indirect(T.lt4[:, 40 * t:40 * t + 40]), F.Copy, "%s lt4%d" % (xk, t), "a1", scale=0.5)
         if t == 0:
             act(T.prev[:], bank(4, C), F.Copy, "", "ps4 prev")
-        tt(T.c1[:], T.f1[:], T.bq[:], A.add, "f1 bq0 bq1 bq2 bq3", "c1")
+            for b in range(4):
+                act(T.bq[:, 20 * b:20 * b + 20], T.cw[:], F.Identity, "cw", "bq%d" % b, bias=0.25 * b, scale=0.0)
+                act(T.xo[:, 20 * b:20 * b + 20], T.cw[:], F.Identity, "cw", "xo%d" % b, bias=C + 0.25 * b)
+            act(T.tbc[:, 1:C + 1], T.kmx[:].indirect(T.tgu[:]), F.Copy, "kmx tgu", "tbc")
+            act(T.dk[:], T.tbc[:, 1:C + 1], F.Identity, "tbc", "dk", bias=1.0, scale=-1.0)
+            tt(T.r3[:], T.r2[:], T.cw[:, 0:6], A.add, "r2 cw", "r3")
+        else:
+            fired(t)
         scan(T.so[:, 1:C + 1], T.va[:], second, 0.0, A.min, A.min, sk, "so")
         tt(T.win[:, 32 * t:32 * t + 32], T.so[:, 0:C + 1].indirect(T.endu[:]), T.mb[:], A.add, "so so0 endu mb", "win%d" % t)
         send(T.lwin[:, 24 * t:24 * t + 20], T.win[:, 32 * t:32 * t + 20], "aw%d" % t, "win%d" % t)
         if t == 0:
+            cp(T.rep[:], T.r3[:], "r3", "rep")
+            quant(T.iq[:], T.ip[:], T.eye[:], "eye0 eye1 eye2 eye3", "iq")
+            fired(t)
+            add(T.dk[:], T.tbc[:, 0:C], "gb", "tbc tbc0", "dk")
             cp(T.keys[:].indirect(T.spu[:]), T.key[:], "key spu", "keys")
-        else:
-            d = P * (t - 1)
-            tt(T.m2[:], st[:, x:x + 1280].indirect(T.lt4[:, 40 * (t - 1):40 * t]), st[:, d:d + 640], A.add,
-               "%s lt4%d" % (xk, t - 1), "m2")
-            act(st[:, d + 640:d + 1280], T.m2[:], F.Copy, "m2", "m%d" % (t - 1), scale=0.5)
+        choice()
         if t == 1:
             late(1)
         if t == R - 1:
@@ -355,9 +366,9 @@ def rank_program(g, core, T, topo):
     def merge(t):
         d, lo = P * (t - 1), P * max(t - 2, 0)
         lq, ls = T.lq[:, K * (t - 1):K * t], T.ls[:, K * (t - 1):K * t]
-        for b in range(4):
-            for k in (b, 4 + b):
-                mm(k, K, T.iq[:, 128 * b:128 * b + 128], T.ip[:, 128 * b:128 * b + 128], lq, ls, "iq lq%d" % (t - 1))
+        for k in (0, 1, 4, 2, 3, 5, 6, 7):
+            b = k % 4
+            mm(k, K, T.iq[:, 128 * b:128 * b + 128], T.ip[:, 128 * b:128 * b + 128], lq, ls, "iq lq%d" % (t - 1))
         if t == 1:
             scan(T.keyh[:], T.km[:], T.keys[:], 0.0, A.add, A.min, "km keys", "keyh")
         for b in range(4):
@@ -370,7 +381,7 @@ def rank_program(g, core, T, topo):
             if t == 1 and b == 2:
                 ts(T.sig[:], T.kf[:], 512.0, None, A.mult, None, "kf", "sig")
         if t == 1:
-            act(T.lb2[:], T.lbn[:].indirect(T.sig[:]), F.Identity, "lbn sig", "lb2", bias=NO - P / 4, scale=-1.0)
+            act(T.lb2[:], T.lbn[:].indirect(T.sig[:]), F.Identity, "lbn sig", "lb2", bias=NO - P / 4, scale=-2.0)
         tt(T.i1[:], T.lwin[:, 24 * (t - 1):24 * (t - 1) + 20].indirect(T.rep[:, 0:5]), T.c1[:], A.add,
            "lwin%d rep c1" % (t - 1), "i1")
         tt(T.i2[:], T.i1[:], T.xo[:], A.min, "i1 xo0 xo1 xo2 xo3", "i2")

@@ -1,10 +1,13 @@
 from concourse.mybir import dt, AluOpType, ActivationFunctionType
 
 C, K, R = 320, 160, 3
-P = 2576
-TOP = 480
-BIG = 16384.0
-NO = 2048.0
+CV = C + 16
+P = 2624
+LIFT = 16384.0
+DOWN = 3.0 / 512
+LATE = 496
+TOP = 1110.0
+SO2 = 328
 F32, BF, F16, I32, U16, Q4, U8 = "float32", "bfloat16", "float16", "int32", "uint16", "float8_e4m3fn_x4", "uint8"
 
 
@@ -16,32 +19,28 @@ SCRATCH = {
     "st": sb(3 * P + 1280 + 1280, BF),
     "ub": sb(512, BF), "vb": sb(512, BF), "tgi": sb(20, I32), "tgu": sb(20, U16),
     "uq": sb(128, Q4), "us": sb(128, U8), "upq": sb(256, Q4), "ups": sb(256, U8), "vq": sb(128, Q4), "vs": sb(128, U8),
-    "wq": sb(512, Q4), "wp": sb(512, U8), "half": sb(512, BF), "eye": sb(2048, BF), "iq": sb(512, Q4), "ip": sb(512, U8),
+    "wq": sb(512, Q4), "wp": sb(512, U8), "half": sb(516, BF), "eye": sb(516, BF), "iq": sb(512, Q4), "ip": sb(512, U8),
     "xq": sb(4 * C, Q4), "xs": sb(4 * C, U8), "et": sb(3 * 640, BF), "eq": sb(3 * K, Q4), "es": sb(3 * K, U8),
     "ht": sb(3 * 640, BF), "hq": sb(3 * K, Q4), "hs": sb(3 * K, U8), "lq": sb(3 * K, Q4), "ls": sb(3 * K, U8),
-    "pi": sb(2, I32), "pj": sb(8, I32), "col": sb(8, F32), "uoi": sb(16, I32), "uo": sb(16, U16),
-    "jm": sb(C, BF), "cj": sb(C, F32), "km4": sb(K, BF),
-    "km": sb(C, BF), "ka": sb(C + 2, BF), "kr": sb(C, BF), "k1": sb(C, BF), "kb": sb(K, F32),
-    "cjf": sb(C, F32), "cjk": sb(C, F32), "mb": sb(32, F32), "cw": sb(20, F32), "cwf": sb(20, F32), "tj": sb(20, F32),
-    "bias": sb(22, F32), "acc": sb(22, F32), "junk": sb(22 * C, BF), "key": sb(C, F32), "k2": sb(C, F32),
-    "kx": sb(C, F32), "kmx": sb(C, F32), "tb0": sb(C, F32),
-    "spu": sb(20, U16), "endu": sb(2, U16), "keys": sb(C, F32), "keyh": sb(C, F32), "ki": sb(20, I32), "kf": sb(20, F32),
-    "sig": sb(20, U16), "tbc": sb(C + 8, F32), "dk": sb(C, F32),
-    "r1": sb(6, I32), "r2": sb(6, F32), "r3": sb(6, F32), "rep": sb(6, U16), "bq": sb(80, F32), "xo": sb(80, F32),
-    "nr": sb(C + 2, BF), "prev": sb(C, F32), "hh": sb(C, BF), "ww": sb(C, F16), "wh": sb(C, F16),
-    "ta": sb(20, F32), "pos": sb(3 * 24, F32), "posu": sb(20, U16), "sc": sb(3 * 496, F32), "sh": sb(K, F32), "eo": sb(40, U16),
-    "ti": sb(40, I32), "tm": sb(40, I32), "t4": sb(120, U16), "lt4": sb(120, U16),
-    "sg": sb(C, F32), "na": sb(C, BF), "nb": sb(C, BF), "ns": sb(C, F16), "pen": sb(C, F32),
-    "lbn": sb(C, F32), "lb1": sb(C, F32), "lb2": sb(C, F32), "w2": sb(C, F32), "y2": sb(3 * C, F32),
-    "va": sb(C, F32), "vl": sb(2 * C, F32), "so": sb(C + 8, F32),
-    "win": sb(3 * 32, F32), "lwin": sb(3 * 24, F32),
-    "f1": sb(80, F32), "c1": sb(80, F32), "i1": sb(80, F32), "i2": sb(80, F32), "fo": sb(80, U16),
-    "a1": sb(640, BF), "m2": sb(640, BF),
-    "oi": sb(K, I32), "oe": sb(K, F32), "oo": sb(K, F32), "yo": sb(C, F32),
+    "pi": sb(2, I32), "pj": sb(4, I32), "col": sb(16, F32), "uoi": sb(16, I32), "uo": sb(16, U16),
+    "one": sb(CV + 2, BF), "jm": sb(32, F32), "cj": sb(CV + 8, F32), "cjf": sb(C, F32), "r32": sb(CV + 2, BF),
+    "da": sb(64, F32), "d4": sb(K, BF), "dc": sb(C, BF), "og": sb(C, F32), "own": sb(C, F32), "ig": sb(128, F32),
+    "cw": sb(20, F32), "cwf": sb(20, F32), "xo": sb(20, F32), "tab": sb(2 * LATE, F32),
+    "bias": sb(22, F32), "acc": sb(24, F32), "junk": sb(24 * K, BF), "key": sb(CV + 8, F32),
+    "spu": sb(20, U16), "keys": sb(C, F32), "keyh": sb(C, F32), "ki": sb(20, I32), "kj": sb(20, I32),
+    "sort": sb(48, U16), "lsort": sb(48, U16),
+    "nr": sb(C + 32, BF), "prev": sb(C, F32), "rr": sb(CV + 2, F16), "zz": sb(CV + 2, BF), "dz": sb(CV + 2, BF),
+    "hold": sb(CV + 2, BF), "jj": sb(CV, BF), "ja": sb(2, F32), "ju": sb(2, U16), "eo": sb(80, U16),
+    "tr": sb(K, F32), "th": sb(K, F32), "sg": sb(C, BF), "cd": sb(C, F16), "hd": sb(C, F16),
+    "v1": sb(20, F32), "o1": sb(20, F32), "o2": sb(20, F32), "dl": sb(20, F32), "cf": sb(20, F32),
+    "lst": sb(3 * 64, U16), "llst": sb(3 * 64, U16),
+    "uu": sb(C, F32), "ww": sb(C, F32), "so": sb(2 * SO2, F32), "ga": sb(128, F32), "gm": sb(64, F32),
+    "j1": sb(20, F32), "j2": sb(20, F32), "j3": sb(20, F32), "pre": sb(20, F32), "fo": sb(80, U16),
+    "a1": sb(640, BF), "m2": sb(640, BF), "oo": sb(K, F32), "yo": sb(C, F32),
     "ps": ("psum", [128, 4096], F32),
 }
-SEMAPHORES = (["cv", "cs", "ct", "cg", "sent", "lx", "ltg", "lu", "lv", "lw", "out", "ga", "gb", "gm1", "gm2"]
-              + ["at%d" % t for t in range(R)] + ["ah%d" % t for t in range(R)] + ["aw%d" % t for t in range(R)])
+SEMAPHORES = (["cv", "cs", "ct", "cg", "sent", "lx", "ltg", "lu", "lv", "lw", "out", "gm1", "gm2", "as"]
+              + [k + str(t) for k in ("at", "ah", "ao") for t in range(R)])
 
 
 def rank_program(g, core, T, topo):
@@ -67,7 +66,7 @@ def rank_program(g, core, T, topo):
 
     def order(q, r, w):
         need = {}
-        toks = [wrote[k] for k in list(r) + list(w) if k in wrote]
+        toks = [wrote[k] for k in r] + [wrote[k] for k in w if k in wrote]
         for k in w:
             toks += readers.get(k, [])
         for s, c in toks:
@@ -120,6 +119,9 @@ def rank_program(g, core, T, topo):
     def cp(o, i, r, w):
         op("v", lambda: V.tensor_copy(o, i), r, w)
 
+    def fill(o, c, w):
+        op("v", lambda: V.memset(o, c), "", w)
+
     def scan(o, d0, d1, init, o0, o1, r, w):
         op("v", lambda: V.tensor_tensor_scan(o, d0, d1, init, o0, o1), r, w)
 
@@ -130,6 +132,15 @@ def rank_program(g, core, T, topo):
             op("s", lambda: S.activation(o, i, f, scale=scale), r, w)
         else:
             op("s", lambda: S.activation(o, i, f, bias=bias, scale=scale, accum_out=acc), r, w)
+
+    def move(q, o, i, r, w):
+        if q == "v":
+            cp(o, i, r, w)
+        else:
+            act(o, i, F.Copy, r, w)
+
+    def column(o, i, r, w, sc, bi):
+        act(o, i, F.Identity, r, w, bias=bi, scale=sc)
 
     def quant(q, s, i, r, w):
         op("v", lambda: V.quantize_mx(q, s, i), r, w)
@@ -153,251 +164,333 @@ def rank_program(g, core, T, topo):
         return P * t + 1280
 
     st = T.st
-    icol, tcol, qcol, k1col, w0col, mbcol = [T.col[:, i:i + 1] for i in range(6)]
+    icol, tcol, qcol, thr, zini, inext, drop, dropa, dropd, dropk, qnext, drop4, tadd, drop1 = [T.col[:, i:i + 1] for i in range(14)]
+    W = CV + 1
 
     load("y", "ltg", [(T.tgi[:], T.tg[:])], "tgi")
     load("s", "lu", [(T.ub[:], T.u[:])], "ub")
     load("y", "lx", [(st[:, X(0):X(0) + 1280], T.x[:])], "x0")
     load("y", "lw", [(T.wq[:].bitcast(dt.uint8), T.wc[:]), (T.wp[:], T.ws[:])], "wq")
     load("y", "lv", [(T.vb[:], T.v[:])], "vb")
+    wrote["lsort"] = ("as", in_n)
     for t in range(R):
-        wrote["lt4%d" % t] = ("at%d" % t, in_n)
+        wrote["t4in%d" % t] = ("at%d" % t, in_n)
+        wrote["offin%d" % t] = ("ao%d" % t, in_n)
         wrote["lq%d" % t] = ("ah%d" % t, 2 * in_n)
-        wrote["lwin%d" % t] = ("aw%d" % t, in_n)
 
     iota(T.pi[:, 0:1], [[0, 1]], 1, "pi", True)
-    iota(T.jm[:], [[0, 20], [1, 16]], 0, "jm")
     iota(T.uoi[:], [[1, 2], [16, 8]], 0, "uoi", True)
-    const(T.ka[:, 0:1], 1, 0, "ka0")
-    const(T.nr[:, 0:1], 1, 1, "nr0")
-    iota(T.cjk[:], [[4096, C]], 0, "cjk")
-    iota(T.km4[:], [[0, 40], [1, 4]], 0, "km4")
-    const(T.sc[:, 0:K], K, 4096 * C, "sc0")
-    const(st[:, X(0) + 1280:X(0) + 1296], 16, 0, "z0")
-    op("v", lambda: V.memset(T.half[:], 0.5), "", "half")
-    scan(T.cj[:], T.half[:, 0:C], T.half[:, 0:C], -1.0, A.add, A.add, "half", "cj")
+    iota(T.jm[:, 16:32], [[0, 4], [1, 4]], 0, "jm4")
+    fill(T.half[:], 0.5, "half")
+    op("g", lambda: g.affine_select(T.eye[:], T.half[:], [[1, 516]], A.is_equal, 0.0, -3, -4), "half", "eye")
+    iota(T.nr[:, C:C + 32], [[1, 2], [0, 16]], 0, "nrv")
+    const(T.zz[:, 0:1], 1, 2080, "zz0")
+    const(T.rr[:, 0:1], 1, 0, "rr0")
+    const(st[:, X(0) + 1280:X(0) + 1344], 64, 0, "z0")
+    const(T.key[:, C:W], 17, 1, "keyv")
+    scan(T.cj[:, 0:W], T.half[:, 0:W], T.half[:, 0:W], -1.0, A.add, A.add, "half", "cj")
     ts(T.pj[:, 0:1], T.pi[:, 0:1], 15, None, A.bitwise_and, None, "pi", "pj0")
     ts(T.pj[:, 1:2], T.pi[:, 0:1], 3, None, A.bitwise_and, None, "pi", "pj1")
     ts(T.pj[:, 2:3], T.pi[:, 0:1], 2, 3, A.logical_shift_right, A.bitwise_and, "pi", "pj2")
-    act(T.cjf[:], T.cj[:], F.Copy, "cj", "cjf", scale=-1.0 / 512)
-    act(T.kx[:], T.cj[:], F.Copy, "cj", "kx", scale=512.0)
-    cp(T.col[:, 0:3], T.pj[:, 0:3], "pj0 pj1 pj2", "col")
-    ts(T.cw[:], T.cj[:, 0:C:16], icol, None, A.add, None, "cj col", "cw")
-    ts(mbcol, icol, 512.0, BIG, A.mult, A.add, "col", "mbcol")
-    ts(T.cwf[:], T.cw[:], -1.0 / 512, None, A.mult, None, "cw", "cwf")
-    ts(T.km[:], T.jm[:], icol, BIG, A.is_equal, A.mult, "jm col", "km")
+    act(T.one[:], T.half[:, 0:CV + 2], F.Copy, "half", "one", scale=2.0)
+    act(T.cjf[:], T.cj[:, 0:C], F.Identity, "cj", "cjf", bias=1.0, scale=1.0 / 4096)
     cp(T.uo[:], T.uoi[:], "uoi", "uo")
-    act(T.bias[:, 20:22], T.cw[:, 0:2], F.Identity, "cw", "biasb", bias=15.25, scale=16.0)
-    act(T.mb[:], T.cj[:, 0:32], F.Identity, "cj mbcol", "mb", bias=mbcol, scale=8192.0)
-    act(T.tj[:], T.cw[:], F.Identity, "cw", "tj", bias=float(TOP), scale=-1.0)
+    cp(T.col[:, 0:3], T.pj[:, 0:3], "pj0 pj1 pj2", "col")
+    j16 = T.cj[:, 0:16]
+    ts(T.cw[:], T.cj[:, 0:C:16], icol, None, A.add, None, "cj col", "cw")
+    ts(inext, icol, 1.0, None, A.add, None, "col", "inext")
+    ts(T.da[:, 0:16], j16, icol, -(1 + DOWN), A.is_equal, A.mult, "cj col", "da0")
+    ts(T.cwf[:], T.cw[:], 1.0 / 4096, 1.0, A.mult, A.add, "cw", "cwf")
+    ts(T.da[:, 16:32], j16, inext, LIFT - 1, A.is_equal, A.mult, "cj inext", "da1")
+    ts(drop, icol, 15.0, 1.0 / LIFT, A.is_equal, A.max, "col", "drop")
+    tt(T.da[:, 32:48], T.da[:, 0:16], T.da[:, 16:32], A.add, "da0 da1", "da2")
+    quant(T.uq[:], T.us[:], T.ub[:], "ub", "uq")
+    act(T.r32[:, 0:W], T.cj[:, 0:W], F.Identity, "cj", "r32", bias=-CV / 64, scale=1.0 / 32)
+    column(T.dc[:, 1:16], T.da[:, 33:48], "da2", "dc", 1.0, 1.0)
+    column(T.dc[:, 0:1], icol, "col", "dc0", 0.0, 0.0)
+    a = 16
+    while a < C:
+        b = min(a, C - a)
+        op("g", lambda: g.affine_select(T.dc[:, a:a + b], T.dc[:, 0:b], [[0, b]], A.is_ge, 0.0, 0, 0), "dc dc0", "dc")
+        a += b
+    iota(T.tab[:, 0:K], [[-1, K]], 0, "tab0", base=int(TOP))
+    iota(T.tab[:, LATE:LATE + K], [[1, K]], 0, "tab1", base=-int(TOP + P / 4))
+    for k in range(2):
+        const(T.tab[:, LATE * k + K:LATE * k + LATE], LATE - K, 0, "tab%d" % (2 + k))
+    const(T.so[:, 0:SO2 + 1:SO2], 2, 0, "so0")
+    for k in (1, 2):
+        const(st[:, X(k) + 1280:X(k) + 1344], 64, 0, "z%d" % k)
 
-    def ranks(a, b):
+    def repeat(buf, m, r, growth=1.0):
+        calls, a = [], 16
+        while a < m:
+            b = min(a, m - a)
+            calls.append(lambda a=a, b=b: act(buf[:, a:a + b], buf[:, 0:b], F.Copy, r, r.split()[0], scale=growth ** (a // 16)))
+            a += b
+        return calls
+
+    def ranks(a, b, between=()):
+        between = list(between)
         for m in range(a, b):
-            act(T.junk[:, C * m:C * m + C], T.key[:], F.Sign, "key biasa biasb", "acc%d" % m,
-                bias=T.bias[:, m:m + 1], scale=-1.0, acc=T.acc[:, m:m + 1])
+            h, c, k = (m // 10, m, "biasa") if m < 20 else ((m - 20) // 2, 20 + m % 2, "biasb")
+            act(T.junk[:, K * m:K * m + K], T.key[:, K * h:K * h + K], F.Sign, "key%d %s" % (h, k), "acc%d" % m,
+                bias=T.bias[:, c:c + 1], scale=-1.0, acc=T.acc[:, m:m + 1])
+            if between:
+                between.pop(0)()
 
     cp(T.tgu[:], T.tgi[:], "tgi", "tgu")
     tt(T.bias[:, 0:20], T.tgi[:], T.cwf[:], A.add, "tgi cwf", "biasa")
-    tt(T.key[:], T.cj[:].indirect(T.tgu[:]), T.cjf[:], A.add, "cj tgu cjf", "key")
-    quant(T.uq[:], T.us[:], T.ub[:], "ub", "uq")
-    ranks(0, 1)
-    cp(T.upq[:].bitcast(dt.uint32), T.uq[:].bitcast(dt.uint32).indirect(T.uo[:]), "uq uo", "upq")
-    ts(k1col, icol, 15.0, 1.0, A.is_lt, A.add, "col", "k1col")
-    ts(w0col, icol, 15.0, -(TOP + 1.0), A.is_lt, A.mult, "col", "w0col")
-    ts(T.ka[:, 1:C + 1], T.jm[:], icol, -1.0 / BIG, A.is_equal, A.mult, "jm col", "ka")
+    for h in range(2):
+        tt(T.key[:, K * h:K * h + K], T.cj[:, 0:C].indirect(T.tgu[:, 10 * h:10 * h + 10]), T.cjf[:, K * h:K * h + K], A.add,
+           "cj tgu cjf", "key%d" % h)
+        if h == 0:
+            cp(T.upq[:].bitcast(dt.uint32), T.uq[:].bitcast(dt.uint32).indirect(T.uo[:]), "uq uo", "upq")
     act(T.ups[:], T.us[:].indirect(T.uo[:]), F.Copy, "uq uo", "ups")
-    for b in range(4):
-        op("g", lambda: g.affine_select(T.eye[:, 512 * b:512 * b + 512], T.half[:], [[1, 512]], A.is_equal, 0.0, -b, -4),
-           "half", "eye%d" % b)
+    column(thr, icol, "col", "thr", 16.0, 15.5)
+    column(zini, icol, "col", "zini", -1.0, 2087.5)
 
-    def y2(t):
-        return T.y2[:, C * t:C * t + C]
+    def masks4():
+        ts(qnext, qcol, 1.0, None, A.add, None, "col", "qnext")
+        ts(T.da[:, 48:64], T.jm[:, 16:32], qcol, None, A.not_equal, None, "jm4 col", "da3")
+        ts(T.jm[:, 0:16], T.jm[:, 16:32], qnext, LIFT, A.is_equal, A.mult, "jm4 qnext", "jm0")
+        ts(drop1, qcol, 3.0, 1.0 / LIFT, A.is_equal, A.max, "col", "drop1")
+        tt(T.d4[:, 0:16], T.da[:, 48:64], T.jm[:, 0:16], A.add, "da3 jm0", "d4")
 
-    def unfired(t):
-        scan(T.ns[:], T.na[:], T.nb[:], 512.0, A.add, A.subtract, "na nb", "ns")
-        act(T.pen[:], T.ns[:], F.Relu, "ns", "pen", bias=-2 * NO * (K - 0.5), scale=2 * NO)
+    def sort_half(h):
+        accs = " ".join("acc%d" % m for m in range(10 * h, 10 * h + 10))
+        ts(T.spu[:, 10 * h:10 * h + 10], T.acc[:, 10 * h:10 * h + 10], 0.5, 79.5, A.mult, A.add, accs, "spu%d" % h)
+        return lambda: cp(T.keys[:, K * h:K * h + K].indirect(T.spu[:, 10 * h:10 * h + 10]), T.key[:, K * h:K * h + K],
+                          "key%d spu%d" % (h, h), "keys%d" % h)
 
-    def counting(t):
-        tt(y2(t), T.w2[:], T.pen[:], A.add, "w2 pen", "y2%d" % t)
+    def sort_lists(between):
+        scan(T.keyh[:], T.dc[:], T.keys[:], 0.0, A.mult, A.max, "dc dc0 keys0 keys1", "keyh")
+        between()
+        for h in range(2):
+            ts(T.sort[:, 40 + 2 * h:42 + 2 * h], T.acc[:, 20 + 2 * h:22 + 2 * h], 0.5, K * h + 80.0, A.mult, A.add,
+               "acc%d acc%d" % (20 + 2 * h, 21 + 2 * h), "sort4%d" % h)
+        ts(T.ki[:], T.keyh[:, 15:C:16], dropk, None, A.mult, None, "keyh dropk", "ki")
+        ts(T.sort[:, 20:40], T.keyh[:, 15:C:16], drop, -1.0, A.mult, A.add, "keyh drop", "sort20")
+        ts(T.kj[:], T.ki[:], 4095, None, A.bitwise_and, None, "ki", "kj")
+        cp(T.sort[:, 0:20], T.kj[:], "kj", "sort0")
+        send(T.lsort[:, 0:44], T.sort[:, 0:44], "as", "sort0 sort20 sort40 sort41")
 
-    def late(t):
-        tt(T.vl[:, C * t:C * t + C], y2(t).indirect(T.sig[:]), T.lb2[:], A.add, "y2%d sig lb2" % t, "vl%d" % t)
+    def owners():
+        for h in range(2):
+            act(T.own[:, K * h:K * h + K], T.og[:].indirect(T.lsort[:, 20 + 10 * h:30 + 10 * h]), F.Copy, "og lsort", "own%d" % h,
+                scale=4.0 ** (20 * h))
 
-    def fired(t):
-        ts(T.f1[:], T.pos[:, 24 * t:24 * t + 20].indirect(T.rep[:, 0:5]), float(K), float(K), A.is_lt, A.mult,
-           "pos%d rep" % t, "f1")
+    def extreme(k):
+        a, alu = SO2 * k, (A.max, A.min)[k]
+        scan(T.so[:, a + 1:a + C + 1], T.ww[:], T.ww[:], 0.0, alu, alu, "ww", "so%d" % (k + 1))
 
-    def choice():
-        tt(T.c1[:], T.f1[:], T.bq[:], A.add, "f1 bq0 bq1 bq2 bq3", "c1")
+    def at_ends(k):
+        a = SO2 * k
+        tt(T.ga[:, 64 * k:64 * k + 64], T.so[:, a:a + C + 1].indirect(T.lsort[:, 40:44]), T.ig[:, 64 * k:64 * k + 64], A.mult,
+           "so0 so%d lsort ig0 ig1 ig2 ig3" % (k + 1), "ga%d" % k)
+
+    def of_halves(k):
+        tt(T.gm[:, 32 * k:32 * k + 20], T.ga[:, 64 * k:64 * k + 20], T.ga[:, 64 * k + 32:64 * k + 52], A.max, "ga%d" % k, "gm%d" % k)
 
     def fire(t):
-        x, xk = X(t), "x%d" % t
-        xq, xs = T.xq[:, C * t:C * t + C], T.xs[:, C * t:C * t + C]
-        quant(xq, xs, st[:, x:x + 1280], xk, "xq%d" % t)
-        mm(4, C, T.upq[:, 0:128], T.ups[:, 0:128], xq, xs, "upq ups xq%d" % t)
-        mm(5, C, T.upq[:, 128:256], T.ups[:, 128:256], xq, xs, "upq ups xq%d" % t)
+        x, xk, L = X(t), "x%d" % t, 64 * t
+        for h in range(2):
+            a = C * t + K * h
+            quant(T.xq[:, a:a + K], T.xs[:, a:a + K], st[:, x + 640 * h:x + 640 * h + 640], xk, "xq%d%d" % (t, h))
+            mm(4 + h, K, T.upq[:, 0:128], T.ups[:, 0:128], T.xq[:, a:a + K], T.xs[:, a:a + K], "upq ups xq%d%d" % (t, h))
+        mm(6, C, T.upq[:, 128:256], T.ups[:, 128:256], T.xq[:, C * t:C * t + C], T.xs[:, C * t:C * t + C], "upq ups xq%d0 xq%d1" % (t, t))
+        nr = T.nr[:, 0:W]
         if t == 0:
-            ranks(1, 6)
-            tt(T.kmx[:], T.kx[:], T.km[:], A.add, "kx km", "kmx")
-            ts(T.k1[:], T.jm[:], 0.0, k1col, A.mult, A.add, "jm k1col", "k1")
-            scan(T.kr[:], T.ka[:, 0:C], T.km[:], 0.0, A.mult, A.subtract, "ka ka0 km", "kr")
-            ts(T.nr[:, 1:C + 1], bank(4, C), 0.0, None, A.is_le, None, "", "ps4 nr")
-            tt(T.k2[:], T.cj[:].indirect(T.tgu[:]), T.cjk[:], A.add, "cj tgu cjk", "k2")
-            act(T.sg[:], bank(5, C), F.Sign, "", "ps5 sg")
-            act(T.tb0[:], T.kmx[:].indirect(T.tgu[:]), F.Copy, "kmx tgu", "tb0", scale=-1.0)
-            act(T.lbn[:], T.sg[:], F.Relu, "sg", "lbn", scale=NO)
-            add(T.tb0[:], T.lbn[:], "ga", "lbn", "tb0")
-            ranks(6, 19)
+            ranks(0, 12)
+            masks4()
+            for h in range(2):
+                ts(T.nr[:, K * h:K * h + K], bank(4 + h, K), 0.0, None, A.is_le, None, "", "ps%d nr%d" % (4 + h, h))
         else:
-            if t == 1:
-                late(0)
-            act(T.m2[:], st[:, x:x + 1280].indirect(T.lt4[:, 40 * (t - 1):40 * t]), F.Copy, "lt4%d" % (t - 1), "m2")
-            wait("g", wrote["d%d3" % t])
-            add(T.m2[:], st[:, P * (t - 1):P * (t - 1) + 640], "gm%d" % t, "", "m2")
-            act(T.sg[:], bank(5, C), F.Sign, "", "ps5 sg")
-            tt(T.nr[:, 1:C + 1], bank(4, C), T.prev[:], A.is_le, "prev", "ps4 nr")
-            act(T.na[:], T.nr[:, 1:C + 1], F.Copy, "nr", "na", scale=512.0)
-            act(T.nb[:], T.nr[:, 0:C], F.Identity, "nr nr0", "nb", bias=-1.0, scale=513.0)
-            act(T.lb1[:], T.sg[:].indirect(T.sig[:]), F.Relu, "sg sig", "lb1", scale=NO)
+            act(T.m2[:], st[:, x:x + 1280].indirect(T.llst[:, L - 64:L - 24]), F.Copy, "%s t4in%d" % (xk, t - 1), "m2")
+            add(T.m2[:], st[:, P * (t - 1):P * (t - 1) + 640], "gm%d" % t, " ".join("d%d%d" % (t, b) for b in range(4)), "m2")
+            for h in range(2):
+                tt(T.nr[:, K * h:K * h + K], bank(4 + h, K), T.prev[:, K * h:K * h + K], A.is_le, "prev%d" % h, "ps%d nr%d" % (4 + h, h))
+            act(T.sg[:], bank(6, C), F.Sign, "", "ps6 sg")
+
+        def scores_kept():
+            for h in range(2):
+                act(T.prev[:, K * h:K * h + K], bank(4 + h, K), F.Copy, "", "ps%d prev%d" % (4 + h, h))
+
+        def places():
+            scan(T.cd[:], T.dc[:], T.nr[:, 0:C], 0.0, A.mult, A.add, "dc dc0 nr0 nr1", "cd")
+
+        def places2():
+            ts(T.v1[:], T.cd[:, 15:C:16], dropa, icol, A.mult, A.add, "cd dropa col", "v1")
+
+        def places3():
+            tt(T.o1[:], T.v1[:], T.rr[:, 0:C:16], A.add, "v1 rr rr0", "o1")
+
+        def delays():
+            scan(T.hd[:], T.dc[:], T.sg[:], 0.0, A.mult, A.max, "dc dc0 sg", "hd")
+
+        def offer(between):
+            ts(T.dl[:], T.hd[:, 15:C:16], dropd, 0.0, A.mult, A.max, "hd dropd", "dl")
+            ts(T.cf[:], T.o1[:], K - 0.5, float(K), A.is_lt, A.mult, "o1", "cf")
+            tt(T.o2[:], T.o1[:], T.dl[:], A.add, "o1 dl", "o2")
+            between()
+            cp(T.lst[:, L + 40:L + 60], T.o2[:], "o2", "off%d" % t)
+            send(T.llst[:, L + 40:L + 60], T.lst[:, L + 40:L + 60], "ao%d" % t, "off%d" % t)
+
+        def targets():
+            act(T.tr[:], T.key[:, 0:W].indirect(T.eo[:, 64:74]), F.Copy, "key0 key1 keyv eo4", "tr")
+
+        def targets2():
+            scan(T.th[:], T.d4[:], T.tr[:], 0.0, A.mult, A.max, "d4 tr", "th")
+
+        def targets3():
+            ts(T.lst[:, L:L + 40], T.th[:, 3:K:4], drop4, tadd, A.mult, A.add, "th drop4 tadd", "t4%d" % t)
+            send(T.llst[:, L:L + 40], T.lst[:, L:L + 40], "at%d" % t, "t4%d" % t)
+
+        scan(T.rr[:, 1:W + 1], T.one[:, 0:W], nr, 0.0, A.add, A.subtract, "one nr0 nr1 nrv", "rr")
+        scan(T.zz[:, 1:W + 1], T.one[:, 0:W], nr, zini, A.add, A.subtract, "one nr0 nr1 nrv zini", "zz")
+        act(T.jj[:], T.rr[:, 1:CV + 1], F.Sign, "rr thr", "ja", bias=thr, scale=-1.0, acc=T.ja[:, 0:1])
+        if t == 0:
+            scatter = sort_half(0)
+        else:
+            places()
+        scan(T.dz[:, 0:W], T.zz[:, 1:W + 1], T.zz[:, 0:W], 0.0, A.max, A.subtract, "zz zz0", "dz")
+        if t > 0:
+            places2()
+        scan(T.hold[:, 0:W], T.dz[:, 0:W], T.r32[:, 0:W], -8.0, A.add, A.min, "dz r32", "hold")
+        if t == 0:
+            scatter()
+        ts(T.ju[:, 0:1], T.ja[:, 0:1], 0.5, CV / 2, A.mult, A.add, "ja", "ju")
+        if t == 0:
+            ranks(12, 20)
+        else:
+            places3()
             if t < R - 1:
-                act(T.prev[:], bank(4, C), F.Copy, "", "ps4 prev")
-        scan(T.ww[:], T.k1[:], T.nr[:, 0:C], w0col, A.add, A.subtract, "k1 nr nr0 w0col", "ww")
-        scan(T.hh[:], T.kr[:], T.nr[:, 1:C + 1], 0.0, A.add, A.max, "kr nr", "hh")
-        scan(T.wh[:], T.km[:], T.ww[:], 0.0, A.add, A.min, "km ww", "wh")
-        tt(T.ta[:], T.hh[:, 15:C:16], T.tj[:], A.mult, "hh tj", "ta")
-        pos = T.pos[:, 24 * t:24 * t + 20]
-        tt(pos, T.wh[:, 15:C:16], T.ta[:], A.add, "wh ta", "pos%d" % t)
-        if t == 0:
-            ts(T.kb[:], T.km4[:], qcol, 2.0 ** 22, A.is_equal, A.mult, "km4 col", "kb")
-        cp(T.posu[:], pos, "pos%d" % t, "posu")
-        sc = T.sc[:, 496 * t:496 * t + 496]
-        cp(sc.indirect(T.posu[:]), T.k2[:], "k2 posu", "sc%d" % t)
-        if t > 0:
-            unfired(t)
-        scan(T.sh[:], T.kb[:], T.sc[:, 496 * t:496 * t + K], 0.0, A.add, A.min, "kb sc%d" % t, "sh")
-        ts(T.eo[:], T.sh[:, 3:K:4], 1.0 / 1024, tcol, A.mult, A.add, "sh col", "eo")
-        cp(T.ti[:], T.sh[:, 3:K:4], "sh", "ti")
-        e0, xw = 640 * t, st[:, x:x + 1296]
-        src = "%s z%d eo" % (xk, t)
-        if t == 0:
-            cp(T.et[:, e0:e0 + 640], xw.indirect(T.eo[:]), src, "ea eb")
-        else:
-            cp(T.et[:, e0:e0 + 320], xw.indirect(T.eo[:, 0:20]), src, "ea")
-            act(T.et[:, e0 + 320:e0 + 640], xw.indirect(T.eo[:, 20:40]), F.Copy, src, "eb")
-        ts(T.tm[:], T.ti[:], 4095, None, A.bitwise_and, None, "ti", "tm")
-        eq, es = T.eq[:, K * t:K * t + K], T.es[:, K * t:K * t + K]
-        quant(eq, es, T.et[:, e0:e0 + 640], "ea eb", "eq")
-        for b in ((2, 0, 3, 1) if t else range(4)):
-            mm(b, K, T.wq[:, 128 * b:128 * b + 128], T.wp[:, 128 * b:128 * b + 128], eq, es, "wq eq")
-        ts(T.t4[:, 40 * t:40 * t + 40], T.tm[:], 4.0, tcol, A.mult, A.add, "tm col", "t4%d" % t)
-        send(T.lt4[:, 40 * t:40 * t + 40], T.t4[:, 40 * t:40 * t + 40], "at%d" % t, "t4%d" % t)
-        if t > 0:
-            scan(T.w2[:], T.dk[:], T.nr[:, 0:C], 0.0, A.add, A.subtract, "dk nr nr0", "w2")
-        else:
-            ts(T.na[:], T.nr[:, 1:C + 1], 512.0, None, A.mult, None, "nr", "na")
-            ts(T.nb[:], T.nr[:, 0:C], 513.0, -1.0, A.mult, A.add, "nr nr0", "nb")
-        for b in range(4):
+                scores_kept()
+        held = T.hold[:, 0:W].indirect(T.ju[:, 0:1])
+        e0, xw = 640 * t, st[:, x:x + 1344]
+        who = "vsss" if t else "vvss"
+
+        def entries(b):
+            move(who[b], T.et[:, e0 + b:e0 + 640:4], xw.indirect(T.eo[:, 16 * b:16 * b + 10]), "%s z%d eo%d" % (xk, t, b), "e%d" % b)
+
+        def relu(b, q):
             h = T.ht[:, e0 + b:e0 + 640:4]
-            if b < 2 or t == 0:
+            if q == "v":
                 ts(h, bank(b, K), 0.0, 0.03125, A.max, A.mult, "", "ps%d h%d" % (b, b))
             else:
                 act(h, bank(b, K), F.Relu, "", "ps%d h%d" % (b, b), scale=0.03125)
+
+        for b in (1, 0, 2, 3):
+            ts(T.eo[:, 16 * b:16 * b + 16], held, 128.0, 2.0 * CV + b, A.mult, A.add, "hold ju", "eo%d" % b)
+        if t > 0:
+            delays()
+        ts(T.eo[:, 64:80], held, 32.0, CV / 2, A.mult, A.add, "hold ju", "eo4")
+        eq, es = T.eq[:, K * t:K * t + K], T.es[:, K * t:K * t + K]
         hq, hs = T.hq[:, K * t:K * t + K], T.hs[:, K * t:K * t + K]
         if t == 0:
-            unfired(t)
+            act(T.sg[:], bank(6, C), F.Sign, "", "ps6 sg")
+            column(T.bias[:, 20:22], T.cw[:, 0:2], "cw", "biasb", 16.0, 16.5)
+            column(dropa, drop, "drop", "dropa", 1 / DOWN, 0.0)
+            column(dropd, drop, "drop", "dropd", float(LATE), 0.0)
+            column(dropk, drop, "drop", "dropk", 4096.0, 0.0)
+            ranks(20, 24)
+            entries(0)
+            scatter = sort_half(1)
+            entries(1)
+            scatter()
+            calls = repeat(T.d4, K, "d4")
+            for call in (lambda: entries(2), lambda: entries(3), targets):
+                calls.pop(0)()
+                call()
+            calls.pop(0)()
+            places()
+            delays()
+            places2()
+            sort_lists(places3)
+            offer(lambda: None)
+            column(drop4, drop1, "drop1", "drop4", 4.0, 0.0)
+            column(tadd, tcol, "col", "tadd", 1.0, -4.0)
+            column(T.og[:, 0:16], T.da[:, 0:16], "da0", "og", -4.0 ** -20 / (1 + DOWN), 0.0)
+            column(T.xo[:], T.cw[:], "cw", "xo", -1.0, TOP - C)
+            calls = repeat(T.og, C, "og", 4.0)
+            calls.pop(0)()
+        else:
+            entries(1)
+            entries(2)
+            entries(3)
+            offer(lambda: entries(0))
+            targets()
+        quant(eq, es, T.et[:, e0:e0 + 640], "e0 e1 e2 e3", "eq")
+        for b in (2, 0, 3, 1):
+            mm(b, K, T.wq[:, 128 * b:128 * b + 128], T.wp[:, 128 * b:128 * b + 128], eq, es, "wq eq")
+        if t == 0:
+            targets2()
+            fill(T.ga[:, 0:32], 0.25, "ga0")
+            targets3()
+            scan(T.ig[:, 0:32], T.ga[:, 0:32], T.one[:, 0:32], 4.0 ** 21, A.mult, A.mult, "ga0 one", "ig0")
+            for b in (2, 0, 3, 1):
+                relu(b, "vvss"[b])
+                calls.pop(0)()
+        else:
+            extreme(1)
+            targets2()
+            relu(2, "s")
+            relu(0, "v")
+            relu(3, "s")
+            targets3()
+            relu(1, "v")
         quant(hq, hs, T.ht[:, e0:e0 + 640], "h0 h1 h2 h3", "hq%d" % t)
         send(T.lq[:, K * t:K * t + K].bitcast(dt.uint8), hq.bitcast(dt.uint8), "ah%d" % t, "hq%d" % t)
         send(T.ls[:, K * t:K * t + K], hs, "ah%d" % t, "hq%d" % t)
-        if t == 0:
-            const(T.tbc[:, 0:1], 1, 0, "tbc0")
-            const(T.so[:, 0:1], 1, 0, "so0")
-            for k in (1, 2):
-                const(st[:, X(k) + 1280:X(k) + 1296], 16, 0, "z%d" % k)
-                const(T.sc[:, 496 * k:496 * k + K], K, 4096 * C, "sc%d" % k)
-            ranks(19, 22)
-            ts(T.r1[:], T.cw[:, 0:6], 0.05, -0.475, A.mult, A.add, "cw", "r1")
-            tt(T.w2[:], T.ns[:], T.tb0[:], A.add, "ns tb0", "w2")
-            ts(T.r2[:], T.r1[:], -20.0, None, A.mult, None, "r1", "r2")
-            counting(t)
-            accs = " ".join("acc%d" % m for m in range(22))
-            ts(T.spu[:], T.acc[:, 0:20], 0.5, 159.5, A.mult, A.add, accs, "spu")
-            ts(T.endu[:], T.acc[:, 20:22], 0.5, 160.0, A.mult, A.add, accs, "endu")
-            cp(T.va[:].indirect(T.spu[:]), y2(t), "y20 spu", "va")
-            second, sk = T.va[:], "va"
-        else:
-            counting(t)
-            tt(T.va[:], y2(t).indirect(T.sig[:]), T.lb1[:], A.add, "y2%d sig lb1" % t, "va")
-            second, sk = T.vl[:, C * (t - 1):C * t], "va vl%d" % (t - 1)
         if t == 1:
-            act(T.lb2[:], T.lb1[:], F.Identity, "lb1", "lb2", bias=NO - P / 4, scale=-1.0)
+            const(T.cj[:, C:W], 17, -1, "cj")
+        if t == 0:
+            for k, sc in ((1, 4.0 ** -20), (2, -1.0), (3, -4.0 ** -20)):
+                ts(T.ig[:, 32 * k:32 * k + 32], T.ig[:, 0:32], sc, None, A.mult, None, "ig0", "ig%d" % k)
+            for b in range(4):
+                quant(T.iq[:, 128 * b:128 * b + 128], T.ip[:, 128 * b:128 * b + 128], T.eye[:, 3 - b:515 - b], "eye", "iq%d" % b)
+            scores_kept()
+            owners()
+        act(T.uu[:], T.tab[:].indirect(T.llst[:, L + 40:L + 60]), F.Copy, "tab0 tab1 tab2 tab3 offin%d" % t, "uu")
+        act(T.a1[:], st[:, x:x + 1280].indirect(T.llst[:, L:L + 40]), F.Copy, "%s t4in%d" % (xk, t), "a1", scale=0.5)
         if t > 0:
             d = P * (t - 1)
             act(st[:, d + 640:d + 1280], T.m2[:], F.Copy, "m2", "m%d" % (t - 1), scale=0.5)
-        act(T.a1[:], st[:, x:x + 1280].indirect(T.lt4[:, 40 * t:40 * t + 40]), F.Copy, "%s lt4%d" % (xk, t), "a1", scale=0.5)
-        if t == 0:
-            act(T.prev[:], bank(4, C), F.Copy, "", "ps4 prev")
-            for b in range(4):
-                act(T.bq[:, 20 * b:20 * b + 20], T.cw[:], F.Identity, "cw", "bq%d" % b, bias=0.25 * b, scale=0.0)
-                act(T.xo[:, 20 * b:20 * b + 20], T.cw[:], F.Identity, "cw", "xo%d" % b, bias=C + 0.25 * b)
-            act(T.tbc[:, 1:C + 1], T.kmx[:].indirect(T.tgu[:]), F.Copy, "kmx tgu", "tbc")
-            act(T.dk[:], T.tbc[:, 1:C + 1], F.Identity, "tbc", "dk", bias=1.0, scale=-1.0)
-            tt(T.r3[:], T.r2[:], T.cw[:, 0:6], A.add, "r2 cw", "r3")
-        else:
-            fired(t)
-        scan(T.so[:, 1:C + 1], T.va[:], second, 0.0, A.min, A.min, sk, "so")
-        tt(T.win[:, 32 * t:32 * t + 32], T.so[:, 0:C + 1].indirect(T.endu[:]), T.mb[:], A.add, "so so0 endu mb", "win%d" % t)
-        send(T.lwin[:, 24 * t:24 * t + 20], T.win[:, 32 * t:32 * t + 20], "aw%d" % t, "win%d" % t)
-        if t == 0:
-            cp(T.rep[:], T.r3[:], "r3", "rep")
-            quant(T.iq[:], T.ip[:], T.eye[:], "eye0 eye1 eye2 eye3", "iq")
-            fired(t)
-            add(T.dk[:], T.tbc[:, 0:C], "gb", "tbc tbc0", "dk")
-            cp(T.keys[:].indirect(T.spu[:]), T.key[:], "key spu", "keys")
-        choice()
-        if t == 1:
-            late(1)
+            at_ends(1)
+        tt(T.ww[:], T.uu[:].indirect(T.lsort[:, 0:20]), T.own[:], A.mult, "uu lsort own0 own1", "ww")
+        if t > 0:
+            of_halves(1)
+        extreme(0)
+        if t > 0:
+            tt(T.j1[:], T.gm[:, 32:52], T.cf[:], A.subtract, "gm1 cf", "j1")
+        at_ends(0)
+        if t > 0:
+            tt(T.pre[:], T.j1[:], T.xo[:], A.max, "j1 xo", "pre")
+        of_halves(0)
         if t == R - 1:
             quant(T.vq[:], T.vs[:], T.vb[:], "vb", "vq")
-            ts(T.oi[:], T.sc[:, 496 * t:496 * t + K], 1.0 / 4096, None, A.mult, None, "sc%d" % t, "oi")
-            ts(T.oe[:], T.oi[:], float(C), -(C + 1.0), A.is_ge, A.mult, "oi", "oe")
-            tt(T.oo[:], T.oi[:], T.oe[:], A.add, "oi oe", "oo")
-            store("y", T.ol[:], T.oo[0:128:16, :], "oo")
+        tt(T.j2[:], T.gm[:, 0:20], T.cf[:], A.subtract, "gm0 cf", "j2")
+        tt(T.j3[:], T.j2[:], T.pre[:] if t else T.xo[:], A.max, "j2 pre" if t else "j2 xo", "j3")
+        for b in (0, 2, 1, 3):
+            ts(T.fo[:, 20 * b:20 * b + 20], T.j3[:], -4.0, 4 * TOP + b + (P if t else 0), A.mult, A.add, "j3", "fo%d" % b)
 
     def merge(t):
         d, lo = P * (t - 1), P * max(t - 2, 0)
         lq, ls = T.lq[:, K * (t - 1):K * t], T.ls[:, K * (t - 1):K * t]
-        for k in (0, 1, 4, 2, 3, 5, 6, 7):
-            b = k % 4
-            mm(k, K, T.iq[:, 128 * b:128 * b + 128], T.ip[:, 128 * b:128 * b + 128], lq, ls, "iq lq%d" % (t - 1))
-        if t == 1:
-            scan(T.keyh[:], T.km[:], T.keys[:], 0.0, A.add, A.min, "km keys", "keyh")
+        for b in (0, 2, 1, 3):
+            mm(b, K, T.iq[:, 128 * b:128 * b + 128], T.ip[:, 128 * b:128 * b + 128], lq, ls, "iq%d lq%d" % (b, t - 1))
         for b in range(4):
+            c = (b + 2) % 4
             tt(st[:, d + 640 + b:d + 1280:4], bank(b, K), T.a1[:, b:640:4], A.add, "a1", "ps%d n%d%d" % (b, t, b))
-            act(st[:, d + b:d + 640:4], bank(4 + b, K), F.Copy, "", "ps%d d%d%d" % (4 + b, t, b), scale=2.0)
-            if t == 1 and b == 0:
-                ts(T.ki[:], T.keyh[:, 15:C:16], 0.3125, None, A.add, None, "keyh", "ki")
-            if t == 1 and b == 1:
-                tt(T.kf[:], T.ki[:], T.keyh[:, 15:C:16], A.subtract, "keyh ki", "kf")
-            if t == 1 and b == 2:
-                ts(T.sig[:], T.kf[:], 512.0, None, A.mult, None, "kf", "sig")
-        if t == 1:
-            act(T.lb2[:], T.lbn[:].indirect(T.sig[:]), F.Identity, "lbn sig", "lb2", bias=NO - P / 4, scale=-2.0)
-        tt(T.i1[:], T.lwin[:, 24 * (t - 1):24 * (t - 1) + 20].indirect(T.rep[:, 0:5]), T.c1[:], A.add,
-           "lwin%d rep c1" % (t - 1), "i1")
-        tt(T.i2[:], T.i1[:], T.xo[:], A.min, "i1 xo0 xo1 xo2 xo3", "i2")
-        ts(T.fo[:], T.i2[:], (d - lo) / 4, 4.0, A.add, A.mult, "i2", "fo")
+            act(st[:, d + c:d + 640:4], bank(c, K), F.Copy, "", "ps%d d%d%d" % (c, t, c), scale=2.0)
         w = st[:, lo:d + 2560]
-        src = "fo x%d m%d m%d " % (t - 1, t - 1, t - 2) + " ".join("n%d%d d%d%d" % (t, b, t, b) for b in range(4))
+        src = "x%d " % (t - 1) + ("m%d z%d " % (t - 2, t - 2) if t > 1 else "") + " ".join("n%d%d d%d%d" % (t, b, t, b) for b in range(4))
         x = X(t)
         for b in (0, 2, 1, 3):
-            o, i = st[:, x + b:x + 1280:4], w.indirect(T.fo[:, 20 * b:20 * b + 20])
-            if b < 2:
-                cp(o, i, src, "x%d%d" % (t, b))
-            else:
-                act(o, i, F.Copy, src, "x%d%d" % (t, b))
+            move("vvss"[b], st[:, x + b:x + 1280:4], w.indirect(T.fo[:, 20 * b:20 * b + 20]), src + " fo%d" % b, "x%d%d" % (t, b))
         for q in ("v", "s"):
             wait(q, wrote["x%d1" % t])
             wait(q, wrote["x%d3" % t])
+        wrote["x%d" % t] = wrote["x%d1" % t]
 
     for t in range(R):
         if t > 0:
@@ -405,13 +498,15 @@ def rank_program(g, core, T, topo):
         fire(t)
     merge(R)
     x, c0 = X(R), C * R
-    quant(T.xq[:, c0:c0 + C], T.xs[:, c0:c0 + C], st[:, x:x + 1280], "", "xq3")
+    act(T.oo[:], T.cj[:, 0:W].indirect(T.eo[:, 64:74]), F.Copy, "cj eo4", "oo")
+    store("y", T.ol[:], T.oo[0:128:16, :], "oo")
     for h in range(2):
         a = c0 + K * h
-        mm(h, K, T.vq[:], T.vs[:], T.xq[:, a:a + K], T.xs[:, a:a + K], "vq xq3")
-    store("y", T.oc[:], T.xq[:, c0:c0 + C].bitcast(dt.uint8), "xq3")
+        quant(T.xq[:, a:a + K], T.xs[:, a:a + K], st[:, x + 640 * h:x + 640 * h + 640], "", "xq3%d" % h)
+        mm(h, K, T.vq[:], T.vs[:], T.xq[:, a:a + K], T.xs[:, a:a + K], "vq xq3%d" % h)
+    store("y", T.oc[:], T.xq[:, c0:c0 + C].bitcast(dt.uint8), "xq30 xq31")
     for k in range(4):
-        store("y", T.osc[4 * k:4 * k + 4, :], T.xs[32 * k:32 * k + 4, c0:c0 + C], "xq3")
+        store("y", T.osc[4 * k:4 * k + 4, :], T.xs[32 * k:32 * k + 4, c0:c0 + C], "xq30 xq31")
     cp(T.yo[:, 0:K], bank(0, K), "", "ps0 ya")
     act(T.yo[:, K:C], bank(1, K), F.Copy, "", "ps1 yb")
     store("s", T.y[:], T.yo[:], "ya yb")

@@ -2,6 +2,7 @@ from concourse.mybir import dt, AluOpType, ActivationFunctionType
 
 C, K, R = 320, 160, 3
 CV = C + 16
+W = CV + 1
 P = 2624
 LIFT = 16384.0
 DOWN = 3.0 / 512
@@ -17,7 +18,7 @@ def sb(n, t):
 
 SCRATCH = {
     "st": sb(3 * P + 1280 + 1280, BF),
-    "ub": sb(512, BF), "vb": sb(512, BF), "tgi": sb(20, I32), "tgu": sb(20, U16),
+    "ub": sb(512, BF), "vb": sb(512, BF), "tgi": sb(20, I32), "tgu": sb(20, U16), "ltg": sb(20, U16),
     "uq": sb(128, Q4), "us": sb(128, U8), "upq": sb(256, Q4), "ups": sb(256, U8), "vq": sb(128, Q4), "vs": sb(128, U8),
     "wq": sb(512, Q4), "wp": sb(512, U8), "half": sb(516, BF), "eye": sb(516, BF), "iq": sb(512, Q4), "ip": sb(512, U8),
     "xq": sb(4 * C, Q4), "xs": sb(4 * C, U8), "et": sb(3 * 640, BF), "eq": sb(3 * K, Q4), "es": sb(3 * K, U8),
@@ -25,22 +26,50 @@ SCRATCH = {
     "pi": sb(2, I32), "pj": sb(4, I32), "col": sb(16, F32), "uoi": sb(16, I32), "uo": sb(16, U16),
     "one": sb(CV + 2, BF), "jm": sb(32, F32), "cj": sb(CV + 8, F32), "cjf": sb(C, F32), "r32": sb(CV + 2, BF),
     "da": sb(64, F32), "d4": sb(K, BF), "dc": sb(C, BF), "og": sb(C, F32), "own": sb(C, F32), "ig": sb(128, F32),
-    "cw": sb(20, F32), "cwf": sb(20, F32), "xo": sb(20, F32), "tab": sb(2 * LATE, F32),
-    "bias": sb(22, F32), "acc": sb(24, F32), "junk": sb(24 * K, BF), "key": sb(CV + 8, F32),
-    "spu": sb(20, U16), "keys": sb(C, F32), "keyh": sb(C, F32), "ki": sb(20, I32), "kj": sb(20, I32),
-    "sort": sb(48, U16), "lsort": sb(48, U16),
+    "cw": sb(20, F32), "cwf": sb(20, F32), "xo": sb(20, F32), "tab": sb(2 * LATE, F32), "fourth": sb(32, BF),
+    "bias": sb(22, F32), "acc": sb(24, F32), "junk": sb(24 * K, BF), "key": sb(C, F32), "keyr": sb(CV + 8, F32),
+    "spu": sb(32, U16), "lspu": sb(32, U16), "keys": sb(C, F32), "keyh": sb(C, F32), "ki": sb(20, I32), "kj": sb(20, I32),
+    "sort": sb(40, U16), "ends": sb(4, U16),
     "nr": sb(C + 32, BF), "prev": sb(C, F32), "rr": sb(CV + 2, F16), "zz": sb(CV + 2, BF), "dz": sb(CV + 2, BF),
-    "hold": sb(CV + 2, BF), "jj": sb(CV, BF), "ja": sb(2, F32), "ju": sb(2, U16), "eo": sb(80, U16),
-    "tr": sb(K, F32), "th": sb(K, F32), "sg": sb(C, BF), "cd": sb(C, F16), "hd": sb(C, F16),
+    "hold": sb(CV + 2, BF), "jj": sb(CV, BF), "ja": sb(2, F32), "ju": sb(2, U16), "eo": sb(64, U16),
+    "tr": sb(K, F32), "th": sb(K, F32), "t4": sb(120, U16), "sg": sb(C, BF), "cd": sb(C, F16), "hd": sb(C, F16),
     "v1": sb(20, F32), "o1": sb(20, F32), "o2": sb(20, F32), "dl": sb(20, F32), "cf": sb(20, F32),
     "lst": sb(3 * 64, U16), "llst": sb(3 * 64, U16),
-    "uu": sb(C, F32), "ww": sb(C, F32), "so": sb(2 * SO2, F32), "ga": sb(128, F32), "gm": sb(64, F32),
+    "uu": sb(C, F32), "ww": sb(2 * C, F32), "so": sb(2 * SO2, F32), "ga": sb(128, F32), "gm": sb(64, F32),
     "j1": sb(20, F32), "j2": sb(20, F32), "j3": sb(20, F32), "pre": sb(20, F32), "fo": sb(80, U16),
     "a1": sb(640, BF), "m2": sb(640, BF), "oo": sb(K, F32), "yo": sb(C, F32),
     "ps": ("psum", [128, 4096], F32),
 }
-SEMAPHORES = (["cv", "cs", "ct", "cg", "sent", "lx", "ltg", "lu", "lv", "lw", "out", "gm1", "gm2", "as"]
-              + [k + str(t) for k in ("at", "ah", "ao") for t in range(R)])
+SEMAPHORES = (["cv", "cs", "ct", "cg", "sent", "lx", "ltg", "lu", "lv", "lw", "out", "gm1", "gm2", "as0", "as1", "ag"]
+              + [k + str(t) for k in ("ah", "ao") for t in range(R)])
+
+FIRST = {
+    "v": "half pj0 pj1 pj2 cj col uo cw da0 cwf tgu drop1 drop da1 key0 da2 biasa uq key1 upq0 ups0 upq1 jm0 xq1 og16 xq0 da3 dropk "
+         "nr1 dropa nr0 d4 thr fourth ups1 rr zz ig0 og32 dz spu0 dropd hold ju cd eo2 eo1 xo d416 hd v1 eo3 dl og64 o1 spu1 eo0 o2 "
+         "ent e3 off keyr1 eq keyr0 iq3 keys0 hq keyh0 keys1 ends0 prev1 keyh1 tau0 iq1 ki tau1 th kj ends1 t4 sort0 iq2 ww iq0 so1 "
+         "cf ga0 n1 gm0 n0 j2 n2 j3 n3 fo3 fo0 fo2 fo1 xb0 xb2",
+    "s": "one cjf inext zini dc r32 og qnext dc1 acc0 acc1 acc2 acc10 acc3 acc4 acc11 biasb acc12 acc5 acc6 acc13 acc14 acc7 acc8 "
+         "acc15 drop4 acc9 ja sg acc16 acc17 acc18 acc19 e2 e1 e0 ig3 d432 og128 acc23 tadd ig1 h0 h2 h3 h1 og256 acc20 acc22 d464 "
+         "acc21 ig2 d4128 tr uu own0 own1 a10 a11 d2 d3 d0 d1 xb3 xb1 prev0",
+    "g": "pi uoi z2 z0 so0 nrv tab3 jm4 dc16 ltg dc32 z1 dc64 rr0 dc128 zz0 dc256 tab0 lspu0 eye lspu1 llst keyv tab2 tab1 lq cjv",
+    "t": "ps5 ps4 ps6 ps0 ps2 ps3 ps1 pd1 pd2 pd0 pd3",
+    "y": "tgi ub x0 wq",
+}
+LATER = {
+    "v": "xq0 xq1 nr0 nr1 rr zz cd dz v1 ju hold o1 eo3 hd eo0 dl eo1 eo2 o2 ent off e1 eq so2 h2 cf vq hq tr ga1 th gm1 t4 ww j1 "
+         "so1 ga0 gm0 pre j2 n0 j3 n1 fo1 fo0 n2 n3 fo2 fo3 xb0 xb2",
+    "s": "m2 ja sg e3 e0 e2 h1 h3 h0 uu m a10 a11 prev1 oo d2 d3 d1 d0 xb1 xb3 prev0",
+    "g": "add llst lq",
+    "t": "ps4 ps5 ps6 ps1 ps3 ps2 ps0 pd0 pd2 pd1 pd3",
+    "y": "vb sol",
+}
+LAST = {
+    "v": "xa0 xa1 xq0 xb2 xb3 xq1",
+    "s": "xa2 xa3 xb0 xb1 y0 y1",
+    "g": "",
+    "t": "ps0 ps1",
+    "y": "soc0 sy0 soc1 sos0 sos1 sos2 sy1 sos3",
+}
 
 
 def rank_program(g, core, T, topo):
@@ -54,463 +83,353 @@ def rank_program(g, core, T, topo):
     out_mask, out_n, in_n = topo.mask(core, nxt), len(topo.engines(core, nxt)), len(topo.engines(prv, core))
     V, S, PE = g.vector, g.scalar, g.tensor
     queue = {"v": V, "s": S, "t": PE, "g": g, "y": g.sync}
-    count = {"v": 0, "s": 0, "t": 0, "g": 0}
-    seen = {q: {} for q in queue}
-    wrote, readers = {}, {}
-    sent = [0]
+    calls, wrote, readers, phase, sent = [], {}, {}, [0], [0]
 
-    def wait(q, tok):
-        if seen[q].get(tok[0], 0) < tok[1]:
-            queue[q].wait_ge(T.sem[tok[0]], tok[1])
-            seen[q][tok[0]] = tok[1]
-
-    def order(q, r, w):
-        need = {}
-        toks = [wrote[k] for k in r] + [wrote[k] for k in w if k in wrote]
-        for k in w:
-            toks += readers.get(k, [])
-        for s, c in toks:
-            need[s] = max(need.get(s, 0), c)
-        for s in need:
-            wait(q, (s, need[s]))
-
-    def done(tok, r, w):
-        for k in r:
-            readers.setdefault(k, []).append(tok)
-        for k in w:
-            wrote[k] = tok
-            readers[k] = []
-
-    def op(q, call, r, w):
+    def note(ways, r, w, token=None, name=None):
         r, w = r.split(), w.split()
-        order(q, r, w)
-        count[q] += 1
-        call().then_inc(T.sem["c" + q], 1)
-        done(("c" + q, count[q]), r, w)
+        before = set(wrote[k] for k in r) | set(wrote[k] for k in w if k in wrote)
+        for k in w:
+            before |= set(readers.get(k, []))
+        for k in r:
+            readers.setdefault(k, []).append(len(calls))
+        for k in w:
+            wrote[k], readers[k] = len(calls), []
+        calls.append({"ways": ways, "before": before, "token": token, "phase": phase[0], "name": name or w[-1].split("@")[0]})
 
-    def load(q, sem, pairs, w):
-        for o, i in pairs:
-            queue[q].dma_start(o, i).then_inc(T.sem[sem], 16)
-        done((sem, 16 * len(pairs)), [], w.split())
+    def compute(q, call):
+        return lambda: call().then_inc(T.sem["c" + q], 1)
 
-    def store(q, o, i, r):
-        order(q, r.split(), [])
-        queue[q].dma_start(o, i).then_inc(T.sem.out, 16)
+    def pick(i, idx):
+        return i if idx is None else i.indirect(idx)
+
+    def load(sem, pairs, r, w):
+        def call():
+            for o, i in pairs:
+                g.sync.dma_start(o, i).then_inc(T.sem[sem], 16)
+        note({"y": call}, r, w, (sem, 16 * len(pairs)))
+
+    def store(o, i, r, name):
+        note({k: lambda k=k: queue[k].dma_start(o, i).then_inc(T.sem.out, 16) for k in "ys"}, r, "", ("out", 0), name)
 
     def add(o, i, sem, r, w):
-        order("g", r.split(), [w])
-        g.dma_start(o, i, accum_op=A.add).then_inc(T.sem[sem], 16)
-        done((sem, 16), r.split(), [w])
+        note({"g": lambda: g.dma_start(o, i, accum_op=A.add).then_inc(T.sem[sem], 16)}, r, w, (sem, 16), "add")
 
-    def send(o, i, sem, r):
-        order("g", r.split(), [])
-        g.remote_dma(o, i, T.sem[sem], T.sem.sent, pid, rid, out_mask)
-        sent[0] += out_n
+    def send(pairs, sem, r, w):
+        def call():
+            for o, i in pairs:
+                g.remote_dma(o, i, T.sem[sem], T.sem.sent, pid, rid, out_mask)
+        sent[0] += out_n * len(pairs)
+        note({"g": call}, r, w, (sem, in_n * len(pairs)))
 
-    def ts(o, i, s1, s2, o0, o1, r, w):
-        if o1 is None:
-            op("v", lambda: V.tensor_scalar(o, i, s1, None, o0), r, w)
-        else:
-            op("v", lambda: V.tensor_scalar(o, i, s1, s2, o0, o1), r, w)
+    def vec(call, r, w):
+        note({"v": compute("v", call)}, r, w)
 
-    def tt(o, a, b, alu, r, w):
-        op("v", lambda: V.tensor_tensor(o, a, b, alu), r, w)
+    def ts(o, i, s1, s2, o0, o1, r, w, idx=None):
+        more = () if o1 is None else (o1,)
+        vec(lambda: V.tensor_scalar(o, pick(i, idx), s1, s2, o0, *more), r, w)
+
+    def tt(o, a, b, alu, r, w, idx=None):
+        vec(lambda: V.tensor_tensor(o, pick(a, idx), b, alu), r, w)
 
     def cp(o, i, r, w):
-        op("v", lambda: V.tensor_copy(o, i), r, w)
+        vec(lambda: V.tensor_copy(o, i), r, w)
 
     def fill(o, c, w):
-        op("v", lambda: V.memset(o, c), "", w)
+        vec(lambda: V.memset(o, c), "", w)
 
     def scan(o, d0, d1, init, o0, o1, r, w):
-        op("v", lambda: V.tensor_tensor_scan(o, d0, d1, init, o0, o1), r, w)
-
-    def act(o, i, f, r, w, bias=0.0, scale=1.0, acc=None):
-        if f == F.Copy and scale == 1.0:
-            op("s", lambda: S.activation(o, i, f), r, w)
-        elif f == F.Copy:
-            op("s", lambda: S.activation(o, i, f, scale=scale), r, w)
-        else:
-            op("s", lambda: S.activation(o, i, f, bias=bias, scale=scale, accum_out=acc), r, w)
-
-    def move(q, o, i, r, w):
-        if q == "v":
-            cp(o, i, r, w)
-        else:
-            act(o, i, F.Copy, r, w)
-
-    def column(o, i, r, w, sc, bi):
-        act(o, i, F.Identity, r, w, bias=bi, scale=sc)
+        vec(lambda: V.tensor_tensor_scan(o, d0, d1, init, o0, o1), r, w)
 
     def quant(q, s, i, r, w):
-        op("v", lambda: V.quantize_mx(q, s, i), r, w)
+        vec(lambda: V.quantize_mx(q, s, i), r, w)
+
+    def sign(o, i, r, w, bias=0.0, scale=1.0, acc=None):
+        note({"s": compute("s", lambda: S.activation(o, i, F.Sign, bias=bias, scale=scale, accum_out=acc))}, r, w)
+
+    def line(o, i, r, w, scale=1.0, bias=0.0, idx=None, relu=False):
+        def on_v():
+            if scale == 1.0 and bias == 0.0:
+                return V.tensor_copy(o, pick(i, idx))
+            if relu:
+                return V.tensor_scalar(o, pick(i, idx), 0.0, scale, A.max, A.mult)
+            return V.tensor_scalar(o, pick(i, idx), scale, bias, A.mult, A.add)
+
+        def on_s():
+            if scale == 1.0 and bias == 0.0:
+                return S.activation(o, pick(i, idx), F.Copy)
+            return S.activation(o, pick(i, idx), F.Relu if relu else F.Identity, bias=bias, scale=scale)
+        note({"v": compute("v", on_v), "s": compute("s", on_s)}, r, w)
 
     def bank(b, m):
         return T.ps[:, 512 * b:512 * b + m]
 
-    def mm(b, m, lq, ls, rq, rs, r):
-        op("t", lambda: PE.matmul_mx(bank(b, m), lq, ls, rq, rs, True, True), r, "ps%d" % b)
+    def mm(b, m, lq, ls, rq, rs, r, name=None):
+        note({"t": compute("t", lambda: PE.matmul_mx(bank(b, m), lq, ls, rq, rs, True, True))}, r, "ps%d" % b, name=name)
 
     def iota(o, pat, ch, w, whole=False, base=0):
-        if whole:
-            op("g", lambda: g.iota(o, pat, base, ch), "", w)
-        else:
-            op("g", lambda: g.iota(o, pat, base, ch, allow_small_or_imprecise_dtypes=True), "", w)
+        more = {} if whole else {"allow_small_or_imprecise_dtypes": True}
+        note({"g": compute("g", lambda: g.iota(o, pat, base, ch, **more))}, "", w)
 
-    def const(o, m, c, w):
-        iota(o, [[0, m]], 0, w, base=c)
+    def const(o, c, w):
+        iota(o, [[0, o.shape[1]]], 0, w, base=c)
+
+    def select(o, i, pat, alu, base, ch, r, w):
+        note({"g": compute("g", lambda: g.affine_select(o, i, pat, alu, 0.0, base, ch))}, r, w)
+
+    def repeat(buf, m, key, growth=1.0, on_g=False):
+        a = 16
+        while a < m:
+            b, w = min(a, m - a), "%s %s%d" % (key, key, a)
+            if on_g:
+                select(buf[:, a:a + b], buf[:, 0:b], [[0, b]], A.is_ge, 0, 0, key, w)
+            else:
+                line(buf[:, a:a + b], buf[:, 0:b], key, w, scale=growth ** (a // 16))
+            a += b
 
     def X(t):
         return P * t + 1280
 
+    def xk(t, h="ab"):
+        return "x0" if t == 0 else " ".join("x%s%d@%d" % (k, b, t) for b in range(4) for k in h)
+
     st = T.st
     icol, tcol, qcol, thr, zini, inext, drop, dropa, dropd, dropk, qnext, drop4, tadd, drop1 = [T.col[:, i:i + 1] for i in range(14)]
-    W = CV + 1
 
-    load("y", "ltg", [(T.tgi[:], T.tg[:])], "tgi")
-    load("s", "lu", [(T.ub[:], T.u[:])], "ub")
-    load("y", "lx", [(st[:, X(0):X(0) + 1280], T.x[:])], "x0")
-    load("y", "lw", [(T.wq[:].bitcast(dt.uint8), T.wc[:]), (T.wp[:], T.ws[:])], "wq")
-    load("y", "lv", [(T.vb[:], T.v[:])], "vb")
-    wrote["lsort"] = ("as", in_n)
-    for t in range(R):
-        wrote["t4in%d" % t] = ("at%d" % t, in_n)
-        wrote["offin%d" % t] = ("ao%d" % t, in_n)
-        wrote["lq%d" % t] = ("ah%d" % t, 2 * in_n)
+    load("ltg", [(T.tgi[:], T.tg[:])], "", "tgi")
+    load("lu", [(T.ub[:], T.u[:])], "", "ub")
+    load("lx", [(st[:, X(0):X(0) + 1280], T.x[:])], "", "x0")
+    load("lw", [(T.wq[:].bitcast(dt.uint8), T.wc[:]), (T.wp[:], T.ws[:])], "x0", "wq")
+    phase[0] = 1
+    load("lv", [(T.vb[:], T.v[:])], "wq", "vb")
+    quant(T.vq[:], T.vs[:], T.vb[:], "vb", "vq")
+    phase[0] = 0
 
     iota(T.pi[:, 0:1], [[0, 1]], 1, "pi", True)
     iota(T.uoi[:], [[1, 2], [16, 8]], 0, "uoi", True)
     iota(T.jm[:, 16:32], [[0, 4], [1, 4]], 0, "jm4")
     fill(T.half[:], 0.5, "half")
-    op("g", lambda: g.affine_select(T.eye[:], T.half[:], [[1, 516]], A.is_equal, 0.0, -3, -4), "half", "eye")
+    select(T.eye[:], T.half[:], [[1, 516]], A.is_equal, -3, -4, "half", "eye")
     iota(T.nr[:, C:C + 32], [[1, 2], [0, 16]], 0, "nrv")
-    const(T.zz[:, 0:1], 1, 2080, "zz0")
-    const(T.rr[:, 0:1], 1, 0, "rr0")
-    const(st[:, X(0) + 1280:X(0) + 1344], 64, 0, "z0")
-    const(T.key[:, C:W], 17, 1, "keyv")
-    scan(T.cj[:, 0:W], T.half[:, 0:W], T.half[:, 0:W], -1.0, A.add, A.add, "half", "cj")
-    ts(T.pj[:, 0:1], T.pi[:, 0:1], 15, None, A.bitwise_and, None, "pi", "pj0")
-    ts(T.pj[:, 1:2], T.pi[:, 0:1], 3, None, A.bitwise_and, None, "pi", "pj1")
-    ts(T.pj[:, 2:3], T.pi[:, 0:1], 2, 3, A.logical_shift_right, A.bitwise_and, "pi", "pj2")
-    act(T.one[:], T.half[:, 0:CV + 2], F.Copy, "half", "one", scale=2.0)
-    act(T.cjf[:], T.cj[:, 0:C], F.Identity, "cj", "cjf", bias=1.0, scale=1.0 / 4096)
-    cp(T.uo[:], T.uoi[:], "uoi", "uo")
-    cp(T.col[:, 0:3], T.pj[:, 0:3], "pj0 pj1 pj2", "col")
-    j16 = T.cj[:, 0:16]
-    ts(T.cw[:], T.cj[:, 0:C:16], icol, None, A.add, None, "cj col", "cw")
-    ts(inext, icol, 1.0, None, A.add, None, "col", "inext")
-    ts(T.da[:, 0:16], j16, icol, -(1 + DOWN), A.is_equal, A.mult, "cj col", "da0")
-    ts(T.cwf[:], T.cw[:], 1.0 / 4096, 1.0, A.mult, A.add, "cw", "cwf")
-    ts(T.da[:, 16:32], j16, inext, LIFT - 1, A.is_equal, A.mult, "cj inext", "da1")
-    ts(drop, icol, 15.0, 1.0 / LIFT, A.is_equal, A.max, "col", "drop")
-    tt(T.da[:, 32:48], T.da[:, 0:16], T.da[:, 16:32], A.add, "da0 da1", "da2")
-    quant(T.uq[:], T.us[:], T.ub[:], "ub", "uq")
-    act(T.r32[:, 0:W], T.cj[:, 0:W], F.Identity, "cj", "r32", bias=-CV / 64, scale=1.0 / 32)
-    column(T.dc[:, 1:16], T.da[:, 33:48], "da2", "dc", 1.0, 1.0)
-    column(T.dc[:, 0:1], icol, "col", "dc0", 0.0, 0.0)
-    a = 16
-    while a < C:
-        b = min(a, C - a)
-        op("g", lambda: g.affine_select(T.dc[:, a:a + b], T.dc[:, 0:b], [[0, b]], A.is_ge, 0.0, 0, 0), "dc dc0", "dc")
-        a += b
+    const(T.zz[:, 0:1], 2080, "zz0")
+    const(T.rr[:, 0:1], 0, "rr0")
+    const(T.keyr[:, C:W], 1, "keyv")
+    const(T.so[:, 0:SO2 + 1:SO2], 0, "so0")
+    for t in range(R):
+        const(st[:, X(t) + 1280:X(t) + 1344], 0, "z%d" % t)
     iota(T.tab[:, 0:K], [[-1, K]], 0, "tab0", base=int(TOP))
     iota(T.tab[:, LATE:LATE + K], [[1, K]], 0, "tab1", base=-int(TOP + P / 4))
     for k in range(2):
-        const(T.tab[:, LATE * k + K:LATE * k + LATE], LATE - K, 0, "tab%d" % (2 + k))
-    const(T.so[:, 0:SO2 + 1:SO2], 2, 0, "so0")
-    for k in (1, 2):
-        const(st[:, X(k) + 1280:X(k) + 1344], 64, 0, "z%d" % k)
+        const(T.tab[:, LATE * k + K:LATE * k + LATE], 0, "tab%d" % (2 + k))
+    scan(T.cj[:, 0:W], T.half[:, 0:W], T.half[:, 0:W], -1.0, A.add, A.add, "half", "cjv cj")
+    ts(T.pj[:, 0:1], T.pi[:, 0:1], 15, None, A.bitwise_and, None, "pi", "pj0")
+    ts(T.pj[:, 1:2], T.pi[:, 0:1], 3, None, A.bitwise_and, None, "pi", "pj1")
+    ts(T.pj[:, 2:3], T.pi[:, 0:1], 2, 3, A.logical_shift_right, A.bitwise_and, "pi", "pj2")
+    cp(T.col[:, 0:3], T.pj[:, 0:3], "pj0 pj1 pj2", "col")
+    cp(T.uo[:], T.uoi[:], "uoi", "uo")
+    line(T.one[:], T.half[:, 0:CV + 2], "half", "one", 2.0)
+    line(T.cjf[:], T.cj[:, 0:C], "cj", "cjf", 1.0 / 4096, 1.0)
+    line(T.r32[:, 0:W], T.cj[:, 0:W], "cj cjv", "r32", 1.0 / 32, -CV / 64)
+    const(T.cj[:, C:W], -1, "cjv")
+    ts(T.cw[:], T.cj[:, 0:C:16], icol, None, A.add, None, "cj col", "cw")
+    ts(drop, icol, 15.0, 1.0 / LIFT, A.is_equal, A.max, "col", "drop")
+    ts(drop1, qcol, 3.0, 1.0 / LIFT, A.is_equal, A.max, "col", "drop1")
+    for o, i, r, w, sc, bi in ((T.cwf[:], T.cw[:], "cw", "cwf", 1.0 / 4096, 1.0), (T.xo[:], T.cw[:], "cw", "xo", -1.0, TOP - C),
+                               (T.bias[:, 20:22], T.cw[:, 0:2], "cw", "biasb", 16.0, 16.5),
+                               (thr, icol, "col", "thr", 16.0, 15.5), (zini, icol, "col", "zini", -1.0, 2087.5),
+                               (inext, icol, "col", "inext", 1.0, 1.0), (qnext, qcol, "col", "qnext", 1.0, 1.0),
+                               (tadd, tcol, "col", "tadd", 1.0, -4.0), (dropa, drop, "drop", "dropa", 1 / DOWN, 0.0),
+                               (dropd, drop, "drop", "dropd", float(LATE), 0.0), (dropk, drop, "drop", "dropk", 4096.0, 0.0),
+                               (drop4, drop1, "drop1", "drop4", 4.0, 0.0)):
+        line(o, i, r, w, sc, bi)
+    ts(T.da[:, 0:16], T.cj[:, 0:16], icol, -(1 + DOWN), A.is_equal, A.mult, "cj col", "da0")
+    ts(T.da[:, 16:32], T.cj[:, 0:16], inext, LIFT - 1, A.is_equal, A.mult, "cj inext", "da1")
+    tt(T.da[:, 32:48], T.da[:, 0:16], T.da[:, 16:32], A.add, "da0 da1", "da2")
+    line(T.dc[:, 0:1], icol, "col", "dc", 0.0)
+    line(T.dc[:, 1:16], T.da[:, 33:48], "da2 dc", "dc dc1", 1.0, 1.0)
+    repeat(T.dc, C, "dc", on_g=True)
+    ts(T.da[:, 48:64], T.jm[:, 16:32], qcol, None, A.not_equal, None, "jm4 col", "da3")
+    ts(T.jm[:, 0:16], T.jm[:, 16:32], qnext, LIFT, A.is_equal, A.mult, "jm4 qnext", "jm0")
+    tt(T.d4[:, 0:16], T.da[:, 48:64], T.jm[:, 0:16], A.add, "da3 jm0", "d4")
+    repeat(T.d4, K, "d4")
+    line(T.og[:, 0:16], T.da[:, 0:16], "da0", "og", -4.0 ** -20 / (1 + DOWN))
+    repeat(T.og, C, "og", 4.0)
+    fill(T.fourth[:], 0.25, "fourth")
+    scan(T.ig[:, 0:32], T.fourth[:], T.one[:, 0:32], 4.0 ** 21, A.mult, A.mult, "fourth one", "ig0")
+    for k, sc in ((1, 4.0 ** -20), (2, -1.0), (3, -4.0 ** -20)):
+        line(T.ig[:, 32 * k:32 * k + 32], T.ig[:, 0:32], "ig0", "ig%d" % k, sc)
+    for b in range(4):
+        quant(T.iq[:, 128 * b:128 * b + 128], T.ip[:, 128 * b:128 * b + 128], T.eye[:, 3 - b:515 - b], "eye", "iq%d" % b)
+    quant(T.uq[:], T.us[:], T.ub[:], "ub", "uq")
+    for h in range(2):
+        a, idx = 128 * h, T.uo[:, 8 * h:8 * h + 8]
+        cp(T.upq[:, a:a + 128].bitcast(dt.uint32), T.uq[:].bitcast(dt.uint32).indirect(idx), "uq uo", "upq%d" % h)
+        line(T.ups[:, a:a + 128], T.us[:], "uq uo", "ups%d" % h, idx=idx)
 
-    def repeat(buf, m, r, growth=1.0):
-        calls, a = [], 16
-        while a < m:
-            b = min(a, m - a)
-            calls.append(lambda a=a, b=b: act(buf[:, a:a + b], buf[:, 0:b], F.Copy, r, r.split()[0], scale=growth ** (a // 16)))
-            a += b
-        return calls
-
-    def ranks(a, b, between=()):
-        between = list(between)
-        for m in range(a, b):
-            h, c, k = (m // 10, m, "biasa") if m < 20 else ((m - 20) // 2, 20 + m % 2, "biasb")
-            act(T.junk[:, K * m:K * m + K], T.key[:, K * h:K * h + K], F.Sign, "key%d %s" % (h, k), "acc%d" % m,
-                bias=T.bias[:, c:c + 1], scale=-1.0, acc=T.acc[:, m:m + 1])
-            if between:
-                between.pop(0)()
+    def signs(m, src, h, c, r):
+        sign(T.junk[:, K * m:K * m + K], src[:, K * h:K * h + K], r, "acc%d" % m, T.bias[:, c:c + 1], -1.0, T.acc[:, m:m + 1])
 
     cp(T.tgu[:], T.tgi[:], "tgi", "tgu")
+    send([(T.ltg[:], T.tgu[:])], "ag", "tgu", "ltg")
     tt(T.bias[:, 0:20], T.tgi[:], T.cwf[:], A.add, "tgi cwf", "biasa")
     for h in range(2):
-        tt(T.key[:, K * h:K * h + K], T.cj[:, 0:C].indirect(T.tgu[:, 10 * h:10 * h + 10]), T.cjf[:, K * h:K * h + K], A.add,
-           "cj tgu cjf", "key%d" % h)
-        if h == 0:
-            cp(T.upq[:].bitcast(dt.uint32), T.uq[:].bitcast(dt.uint32).indirect(T.uo[:]), "uq uo", "upq")
-    act(T.ups[:], T.us[:].indirect(T.uo[:]), F.Copy, "uq uo", "ups")
-    column(thr, icol, "col", "thr", 16.0, 15.5)
-    column(zini, icol, "col", "zini", -1.0, 2087.5)
+        a, b, c = K * h, 10 * h, 16 * h
+        tt(T.key[:, a:a + K], T.cj[:, 0:C], T.cjf[:, a:a + K], A.add, "cj tgu cjf", "key%d" % h, T.tgu[:, b:b + 10])
+        tt(T.keyr[:, a:a + K], T.cj[:, 0:C], T.cjf[:, a:a + K], A.add, "cj ltg cjf", "keyr%d" % h, T.ltg[:, b:b + 10])
+        for m in range(b, b + 10):
+            signs(m, T.key, h, m, "biasa key%d" % h)
+        ts(T.spu[:, c:c + 10], T.acc[:, b:b + 10], 0.5, 79.5, A.mult, A.add, " ".join("acc%d" % m for m in range(b, b + 10)), "spu%d" % h)
+        send([(T.lspu[:, c:c + 10], T.spu[:, c:c + 10])], "as%d" % h, "spu%d" % h, "lspu%d" % h)
+        cp(T.keys[:, a:a + K].indirect(T.lspu[:, c:c + 10]), T.keyr[:, a:a + K], "keyr%d lspu%d" % (h, h), "keys%d" % h)
+        scan(T.keyh[:, a:a + K], T.dc[:, 0:K], T.keys[:, a:a + K], 0.0, A.mult, A.max, "dc keys%d" % h, "keyh%d" % h)
+        ts(T.sort[:, 20 + b:30 + b], T.keyh[:, a + 15:a + K:16], drop, -1.0, A.mult, A.add, "keyh%d drop" % h, "tau%d" % h)
+        for k in range(2):
+            signs(20 + 2 * h + k, T.keyr, h, 20 + k, "biasb keyr%d" % h)
+        ts(T.ends[:, 2 * h:2 + 2 * h], T.acc[:, 20 + 2 * h:22 + 2 * h], 0.5, a + 80.0, A.mult, A.add,
+           "acc%d acc%d" % (20 + 2 * h, 21 + 2 * h), "ends%d" % h)
+        line(T.own[:, a:a + K], T.og[:], "og tau%d" % h, "own%d" % h, 4.0 ** (20 * h), idx=T.sort[:, 20 + b:30 + b])
+    ts(T.ki[:], T.keyh[:, 15:C:16], dropk, None, A.mult, None, "keyh0 keyh1 dropk", "ki")
+    ts(T.kj[:], T.ki[:], 4095, None, A.bitwise_and, None, "ki", "kj")
+    cp(T.sort[:, 0:20], T.kj[:], "kj", "sort0")
 
-    def masks4():
-        ts(qnext, qcol, 1.0, None, A.add, None, "col", "qnext")
-        ts(T.da[:, 48:64], T.jm[:, 16:32], qcol, None, A.not_equal, None, "jm4 col", "da3")
-        ts(T.jm[:, 0:16], T.jm[:, 16:32], qnext, LIFT, A.is_equal, A.mult, "jm4 qnext", "jm0")
-        ts(drop1, qcol, 3.0, 1.0 / LIFT, A.is_equal, A.max, "col", "drop1")
-        tt(T.d4[:, 0:16], T.da[:, 48:64], T.jm[:, 0:16], A.add, "da3 jm0", "d4")
-
-    def sort_half(h):
-        accs = " ".join("acc%d" % m for m in range(10 * h, 10 * h + 10))
-        ts(T.spu[:, 10 * h:10 * h + 10], T.acc[:, 10 * h:10 * h + 10], 0.5, 79.5, A.mult, A.add, accs, "spu%d" % h)
-        return lambda: cp(T.keys[:, K * h:K * h + K].indirect(T.spu[:, 10 * h:10 * h + 10]), T.key[:, K * h:K * h + K],
-                          "key%d spu%d" % (h, h), "keys%d" % h)
-
-    def sort_lists(between):
-        scan(T.keyh[:], T.dc[:], T.keys[:], 0.0, A.mult, A.max, "dc dc0 keys0 keys1", "keyh")
-        between()
-        for h in range(2):
-            ts(T.sort[:, 40 + 2 * h:42 + 2 * h], T.acc[:, 20 + 2 * h:22 + 2 * h], 0.5, K * h + 80.0, A.mult, A.add,
-               "acc%d acc%d" % (20 + 2 * h, 21 + 2 * h), "sort4%d" % h)
-        ts(T.ki[:], T.keyh[:, 15:C:16], dropk, None, A.mult, None, "keyh dropk", "ki")
-        ts(T.sort[:, 20:40], T.keyh[:, 15:C:16], drop, -1.0, A.mult, A.add, "keyh drop", "sort20")
-        ts(T.kj[:], T.ki[:], 4095, None, A.bitwise_and, None, "ki", "kj")
-        cp(T.sort[:, 0:20], T.kj[:], "kj", "sort0")
-        send(T.lsort[:, 0:44], T.sort[:, 0:44], "as", "sort0 sort20 sort40 sort41")
-
-    def owners():
-        for h in range(2):
-            act(T.own[:, K * h:K * h + K], T.og[:].indirect(T.lsort[:, 20 + 10 * h:30 + 10 * h]), F.Copy, "og lsort", "own%d" % h,
-                scale=4.0 ** (20 * h))
-
-    def extreme(k):
-        a, alu = SO2 * k, (A.max, A.min)[k]
-        scan(T.so[:, a + 1:a + C + 1], T.ww[:], T.ww[:], 0.0, alu, alu, "ww", "so%d" % (k + 1))
-
-    def at_ends(k):
-        a = SO2 * k
-        tt(T.ga[:, 64 * k:64 * k + 64], T.so[:, a:a + C + 1].indirect(T.lsort[:, 40:44]), T.ig[:, 64 * k:64 * k + 64], A.mult,
-           "so0 so%d lsort ig0 ig1 ig2 ig3" % (k + 1), "ga%d" % k)
-
-    def of_halves(k):
+    def best(k, t):
+        a, alu, ww = SO2 * k, (A.max, A.min)[k], T.ww[:, C * (t % 2):C * (t % 2) + C]
+        scan(T.so[:, a + 1:a + C + 1], ww, ww, 0.0, alu, alu, "ww@%d" % (t % 2), "so%d" % (k + 1))
+        tt(T.ga[:, 64 * k:64 * k + 64], T.so[:, a:a + C + 1], T.ig[:, 64 * k:64 * k + 64], A.mult,
+           "so0 so%d ends0 ends1 ig0 ig1 ig2 ig3" % (k + 1), "ga%d" % k, T.ends[:])
         tt(T.gm[:, 32 * k:32 * k + 20], T.ga[:, 64 * k:64 * k + 20], T.ga[:, 64 * k + 32:64 * k + 52], A.max, "ga%d" % k, "gm%d" % k)
 
     def fire(t):
-        x, xk, L = X(t), "x%d" % t, 64 * t
+        x, L, e0 = X(t), 64 * t, 640 * t
         for h in range(2):
             a = C * t + K * h
-            quant(T.xq[:, a:a + K], T.xs[:, a:a + K], st[:, x + 640 * h:x + 640 * h + 640], xk, "xq%d%d" % (t, h))
-            mm(4 + h, K, T.upq[:, 0:128], T.ups[:, 0:128], T.xq[:, a:a + K], T.xs[:, a:a + K], "upq ups xq%d%d" % (t, h))
-        mm(6, C, T.upq[:, 128:256], T.ups[:, 128:256], T.xq[:, C * t:C * t + C], T.xs[:, C * t:C * t + C], "upq ups xq%d0 xq%d1" % (t, t))
-        nr = T.nr[:, 0:W]
-        if t == 0:
-            ranks(0, 12)
-            masks4()
-            for h in range(2):
+            quant(T.xq[:, a:a + K], T.xs[:, a:a + K], st[:, x + 640 * h:x + 640 * h + 640], xk(t), "xq%d@%d" % (h, t))
+            mm(4 + h, K, T.upq[:, 0:128], T.ups[:, 0:128], T.xq[:, a:a + K], T.xs[:, a:a + K], "upq0 ups0 xq%d@%d" % (h, t))
+        mm(6, C, T.upq[:, 128:256], T.ups[:, 128:256], T.xq[:, C * t:C * t + C], T.xs[:, C * t:C * t + C],
+           "upq1 ups1 xq0@%d xq1@%d" % (t, t))
+        for h in range(2):
+            if t == 0:
                 ts(T.nr[:, K * h:K * h + K], bank(4 + h, K), 0.0, None, A.is_le, None, "", "ps%d nr%d" % (4 + h, h))
-        else:
-            act(T.m2[:], st[:, x:x + 1280].indirect(T.llst[:, L - 64:L - 24]), F.Copy, "%s t4in%d" % (xk, t - 1), "m2")
-            add(T.m2[:], st[:, P * (t - 1):P * (t - 1) + 640], "gm%d" % t, " ".join("d%d%d" % (t, b) for b in range(4)), "m2")
-            for h in range(2):
+            else:
                 tt(T.nr[:, K * h:K * h + K], bank(4 + h, K), T.prev[:, K * h:K * h + K], A.is_le, "prev%d" % h, "ps%d nr%d" % (4 + h, h))
-            act(T.sg[:], bank(6, C), F.Sign, "", "ps6 sg")
-
-        def scores_kept():
-            for h in range(2):
-                act(T.prev[:, K * h:K * h + K], bank(4 + h, K), F.Copy, "", "ps%d prev%d" % (4 + h, h))
-
-        def places():
-            scan(T.cd[:], T.dc[:], T.nr[:, 0:C], 0.0, A.mult, A.add, "dc dc0 nr0 nr1", "cd")
-
-        def places2():
-            ts(T.v1[:], T.cd[:, 15:C:16], dropa, icol, A.mult, A.add, "cd dropa col", "v1")
-
-        def places3():
-            tt(T.o1[:], T.v1[:], T.rr[:, 0:C:16], A.add, "v1 rr rr0", "o1")
-
-        def delays():
-            scan(T.hd[:], T.dc[:], T.sg[:], 0.0, A.mult, A.max, "dc dc0 sg", "hd")
-
-        def offer(between):
-            ts(T.dl[:], T.hd[:, 15:C:16], dropd, 0.0, A.mult, A.max, "hd dropd", "dl")
-            ts(T.cf[:], T.o1[:], K - 0.5, float(K), A.is_lt, A.mult, "o1", "cf")
-            tt(T.o2[:], T.o1[:], T.dl[:], A.add, "o1 dl", "o2")
-            between()
-            cp(T.lst[:, L + 40:L + 60], T.o2[:], "o2", "off%d" % t)
-            send(T.llst[:, L + 40:L + 60], T.lst[:, L + 40:L + 60], "ao%d" % t, "off%d" % t)
-
-        def targets():
-            act(T.tr[:], T.key[:, 0:W].indirect(T.eo[:, 64:74]), F.Copy, "key0 key1 keyv eo4", "tr")
-
-        def targets2():
-            scan(T.th[:], T.d4[:], T.tr[:], 0.0, A.mult, A.max, "d4 tr", "th")
-
-        def targets3():
-            ts(T.lst[:, L:L + 40], T.th[:, 3:K:4], drop4, tadd, A.mult, A.add, "th drop4 tadd", "t4%d" % t)
-            send(T.llst[:, L:L + 40], T.lst[:, L:L + 40], "at%d" % t, "t4%d" % t)
-
+            if t < R - 1:
+                line(T.prev[:, K * h:K * h + K], bank(4 + h, K), "", "ps%d prev%d" % (4 + h, h))
+        sign(T.sg[:], bank(6, C), "", "ps6 sg")
+        nr = T.nr[:, 0:W]
         scan(T.rr[:, 1:W + 1], T.one[:, 0:W], nr, 0.0, A.add, A.subtract, "one nr0 nr1 nrv", "rr")
         scan(T.zz[:, 1:W + 1], T.one[:, 0:W], nr, zini, A.add, A.subtract, "one nr0 nr1 nrv zini", "zz")
-        act(T.jj[:], T.rr[:, 1:CV + 1], F.Sign, "rr thr", "ja", bias=thr, scale=-1.0, acc=T.ja[:, 0:1])
-        if t == 0:
-            scatter = sort_half(0)
-        else:
-            places()
+        sign(T.jj[:], T.rr[:, 1:CV + 1], "rr thr", "ja", thr, -1.0, T.ja[:, 0:1])
         scan(T.dz[:, 0:W], T.zz[:, 1:W + 1], T.zz[:, 0:W], 0.0, A.max, A.subtract, "zz zz0", "dz")
-        if t > 0:
-            places2()
         scan(T.hold[:, 0:W], T.dz[:, 0:W], T.r32[:, 0:W], -8.0, A.add, A.min, "dz r32", "hold")
-        if t == 0:
-            scatter()
         ts(T.ju[:, 0:1], T.ja[:, 0:1], 0.5, CV / 2, A.mult, A.add, "ja", "ju")
-        if t == 0:
-            ranks(12, 20)
-        else:
-            places3()
-            if t < R - 1:
-                scores_kept()
-        held = T.hold[:, 0:W].indirect(T.ju[:, 0:1])
-        e0, xw = 640 * t, st[:, x:x + 1344]
-        who = "vsss" if t else "vvss"
-
-        def entries(b):
-            move(who[b], T.et[:, e0 + b:e0 + 640:4], xw.indirect(T.eo[:, 16 * b:16 * b + 10]), "%s z%d eo%d" % (xk, t, b), "e%d" % b)
-
-        def relu(b, q):
-            h = T.ht[:, e0 + b:e0 + 640:4]
-            if q == "v":
-                ts(h, bank(b, K), 0.0, 0.03125, A.max, A.mult, "", "ps%d h%d" % (b, b))
-            else:
-                act(h, bank(b, K), F.Relu, "", "ps%d h%d" % (b, b), scale=0.03125)
-
-        for b in (1, 0, 2, 3):
-            ts(T.eo[:, 16 * b:16 * b + 16], held, 128.0, 2.0 * CV + b, A.mult, A.add, "hold ju", "eo%d" % b)
-        if t > 0:
-            delays()
-        ts(T.eo[:, 64:80], held, 32.0, CV / 2, A.mult, A.add, "hold ju", "eo4")
+        for b in range(4):
+            ts(T.eo[:, 16 * b:16 * b + 16], T.hold[:, 0:W], 128.0, 2.0 * CV + b, A.mult, A.add, "hold ju", "eo%d" % b, T.ju[:, 0:1])
+            line(T.et[:, e0 + b:e0 + 640:4], st[:, x:x + 1344], "%s z%d eo%d" % (xk(t), t, b), "e%d" % b, idx=T.eo[:, 16 * b:16 * b + 10])
         eq, es = T.eq[:, K * t:K * t + K], T.es[:, K * t:K * t + K]
         hq, hs = T.hq[:, K * t:K * t + K], T.hs[:, K * t:K * t + K]
-        if t == 0:
-            act(T.sg[:], bank(6, C), F.Sign, "", "ps6 sg")
-            column(T.bias[:, 20:22], T.cw[:, 0:2], "cw", "biasb", 16.0, 16.5)
-            column(dropa, drop, "drop", "dropa", 1 / DOWN, 0.0)
-            column(dropd, drop, "drop", "dropd", float(LATE), 0.0)
-            column(dropk, drop, "drop", "dropk", 4096.0, 0.0)
-            ranks(20, 24)
-            entries(0)
-            scatter = sort_half(1)
-            entries(1)
-            scatter()
-            calls = repeat(T.d4, K, "d4")
-            for call in (lambda: entries(2), lambda: entries(3), targets):
-                calls.pop(0)()
-                call()
-            calls.pop(0)()
-            places()
-            delays()
-            places2()
-            sort_lists(places3)
-            offer(lambda: None)
-            column(drop4, drop1, "drop1", "drop4", 4.0, 0.0)
-            column(tadd, tcol, "col", "tadd", 1.0, -4.0)
-            column(T.og[:, 0:16], T.da[:, 0:16], "da0", "og", -4.0 ** -20 / (1 + DOWN), 0.0)
-            column(T.xo[:], T.cw[:], "cw", "xo", -1.0, TOP - C)
-            calls = repeat(T.og, C, "og", 4.0)
-            calls.pop(0)()
-        else:
-            entries(1)
-            entries(2)
-            entries(3)
-            offer(lambda: entries(0))
-            targets()
         quant(eq, es, T.et[:, e0:e0 + 640], "e0 e1 e2 e3", "eq")
-        for b in (2, 0, 3, 1):
+        for b in range(4):
             mm(b, K, T.wq[:, 128 * b:128 * b + 128], T.wp[:, 128 * b:128 * b + 128], eq, es, "wq eq")
-        if t == 0:
-            targets2()
-            fill(T.ga[:, 0:32], 0.25, "ga0")
-            targets3()
-            scan(T.ig[:, 0:32], T.ga[:, 0:32], T.one[:, 0:32], 4.0 ** 21, A.mult, A.mult, "ga0 one", "ig0")
-            for b in (2, 0, 3, 1):
-                relu(b, "vvss"[b])
-                calls.pop(0)()
-        else:
-            extreme(1)
-            targets2()
-            relu(2, "s")
-            relu(0, "v")
-            relu(3, "s")
-            targets3()
-            relu(1, "v")
-        quant(hq, hs, T.ht[:, e0:e0 + 640], "h0 h1 h2 h3", "hq%d" % t)
-        send(T.lq[:, K * t:K * t + K].bitcast(dt.uint8), hq.bitcast(dt.uint8), "ah%d" % t, "hq%d" % t)
-        send(T.ls[:, K * t:K * t + K], hs, "ah%d" % t, "hq%d" % t)
-        if t == 1:
-            const(T.cj[:, C:W], 17, -1, "cj")
-        if t == 0:
-            for k, sc in ((1, 4.0 ** -20), (2, -1.0), (3, -4.0 ** -20)):
-                ts(T.ig[:, 32 * k:32 * k + 32], T.ig[:, 0:32], sc, None, A.mult, None, "ig0", "ig%d" % k)
-            for b in range(4):
-                quant(T.iq[:, 128 * b:128 * b + 128], T.ip[:, 128 * b:128 * b + 128], T.eye[:, 3 - b:515 - b], "eye", "iq%d" % b)
-            scores_kept()
-            owners()
-        act(T.uu[:], T.tab[:].indirect(T.llst[:, L + 40:L + 60]), F.Copy, "tab0 tab1 tab2 tab3 offin%d" % t, "uu")
-        act(T.a1[:], st[:, x:x + 1280].indirect(T.llst[:, L:L + 40]), F.Copy, "%s t4in%d" % (xk, t), "a1", scale=0.5)
+            line(T.ht[:, e0 + b:e0 + 640:4], bank(b, K), "", "ps%d h%d" % (b, b), 0.03125, relu=True)
+        quant(hq, hs, T.ht[:, e0:e0 + 640], "h0 h1 h2 h3", "hq@%d" % t)
+        send([(T.lq[:, K * t:K * t + K].bitcast(dt.uint8), hq.bitcast(dt.uint8)), (T.ls[:, K * t:K * t + K], hs)],
+             "ah%d" % t, "hq@%d" % t, "lq@%d" % t)
+        scan(T.cd[:], T.dc[:], T.nr[:, 0:C], 0.0, A.mult, A.add, "dc nr0 nr1", "cd")
+        scan(T.hd[:], T.dc[:], T.sg[:], 0.0, A.mult, A.max, "dc sg", "hd")
+        ts(T.v1[:], T.cd[:, 15:C:16], dropa, icol, A.mult, A.add, "cd dropa col", "v1")
+        tt(T.o1[:], T.v1[:], T.rr[:, 0:C:16], A.add, "v1 rr rr0", "o1")
+        ts(T.dl[:], T.hd[:, 15:C:16], dropd, 0.0, A.mult, A.max, "hd dropd", "dl")
+        tt(T.o2[:], T.o1[:], T.dl[:], A.add, "o1 dl", "o2")
+        cp(T.lst[:, L + 16:L + 36], T.o2[:], "o2", "off@%d" % t)
+        ts(T.lst[:, L:L + 16], T.hold[:, 0:W], 32.0, CV / 2, A.mult, A.add, "hold ju", "ent@%d" % t, T.ju[:, 0:1])
+        send([(T.llst[:, L:L + 36], T.lst[:, L:L + 36])], "ao%d" % t, "off@%d ent@%d" % (t, t), "llst@%d" % t)
+        ts(T.cf[:], T.o1[:], K - 0.5, float(K), A.is_lt, A.mult, "o1", "cf")
         if t > 0:
             d = P * (t - 1)
-            act(st[:, d + 640:d + 1280], T.m2[:], F.Copy, "m2", "m%d" % (t - 1), scale=0.5)
-            at_ends(1)
-        tt(T.ww[:], T.uu[:].indirect(T.lsort[:, 0:20]), T.own[:], A.mult, "uu lsort own0 own1", "ww")
-        if t > 0:
-            of_halves(1)
-        extreme(0)
-        if t > 0:
+            line(T.m2[:], st[:, x:x + 1280], "%s t4@%d" % (xk(t), t - 1), "m2", idx=T.t4[:, 40 * t - 40:40 * t])
+            add(T.m2[:], st[:, d:d + 640], "gm%d" % t, " ".join("d%d@%d" % (b, t) for b in range(4)), "m2")
+            line(st[:, d + 640:d + 1280], T.m2[:], "m2", " ".join("n%d@%d" % (b, t) for b in range(4)) + " m", 0.5)
+            best(1, t - 1)
             tt(T.j1[:], T.gm[:, 32:52], T.cf[:], A.subtract, "gm1 cf", "j1")
-        at_ends(0)
-        if t > 0:
             tt(T.pre[:], T.j1[:], T.xo[:], A.max, "j1 xo", "pre")
-        of_halves(0)
-        if t == R - 1:
-            quant(T.vq[:], T.vs[:], T.vb[:], "vb", "vq")
+        line(T.tr[:], T.keyr[:, 0:W], "keyr0 keyr1 keyv llst@%d" % t, "tr", idx=T.llst[:, L:L + 10])
+        scan(T.th[:], T.d4[:], T.tr[:], 0.0, A.mult, A.max, "d4 tr", "th")
+        ts(T.t4[:, 40 * t:40 * t + 40], T.th[:, 3:K:4], drop4, tadd, A.mult, A.add, "th drop4 tadd", "t4@%d" % t)
+        for h in range(2):
+            a = 40 * t + 20 * h
+            line(T.a1[:, 320 * h:320 * h + 320], st[:, x:x + 1280], "%s t4@%d" % (xk(t), t), "a1%d" % h, 0.5, idx=T.t4[:, a:a + 20])
+        line(T.uu[:], T.tab[:], "tab0 tab1 tab2 tab3 llst@%d" % t, "uu", idx=T.llst[:, L + 16:L + 36])
+        tt(T.ww[:, C * (t % 2):C * (t % 2) + C], T.uu[:], T.own[:], A.mult, "uu sort0 own0 own1", "ww@%d" % (t % 2), T.sort[:, 0:20])
+        best(0, t)
         tt(T.j2[:], T.gm[:, 0:20], T.cf[:], A.subtract, "gm0 cf", "j2")
         tt(T.j3[:], T.j2[:], T.pre[:] if t else T.xo[:], A.max, "j2 pre" if t else "j2 xo", "j3")
-        for b in (0, 2, 1, 3):
+        for b in range(4):
             ts(T.fo[:, 20 * b:20 * b + 20], T.j3[:], -4.0, 4 * TOP + b + (P if t else 0), A.mult, A.add, "j3", "fo%d" % b)
 
     def merge(t):
-        d, lo = P * (t - 1), P * max(t - 2, 0)
+        d, lo, x = P * (t - 1), P * max(t - 2, 0), X(t)
         lq, ls = T.lq[:, K * (t - 1):K * t], T.ls[:, K * (t - 1):K * t]
-        for b in (0, 2, 1, 3):
-            mm(b, K, T.iq[:, 128 * b:128 * b + 128], T.ip[:, 128 * b:128 * b + 128], lq, ls, "iq%d lq%d" % (b, t - 1))
+        for b in range(4):
+            mm(b, K, T.iq[:, 128 * b:128 * b + 128], T.ip[:, 128 * b:128 * b + 128], lq, ls, "iq%d lq@%d" % (b, t - 1), "pd%d" % b)
         for b in range(4):
             c = (b + 2) % 4
-            tt(st[:, d + 640 + b:d + 1280:4], bank(b, K), T.a1[:, b:640:4], A.add, "a1", "ps%d n%d%d" % (b, t, b))
-            act(st[:, d + c:d + 640:4], bank(c, K), F.Copy, "", "ps%d d%d%d" % (c, t, c), scale=2.0)
-        w = st[:, lo:d + 2560]
-        src = "x%d " % (t - 1) + ("m%d z%d " % (t - 2, t - 2) if t > 1 else "") + " ".join("n%d%d d%d%d" % (t, b, t, b) for b in range(4))
-        x = X(t)
-        for b in (0, 2, 1, 3):
-            move("vvss"[b], st[:, x + b:x + 1280:4], w.indirect(T.fo[:, 20 * b:20 * b + 20]), src + " fo%d" % b, "x%d%d" % (t, b))
-        for q in ("v", "s"):
-            wait(q, wrote["x%d1" % t])
-            wait(q, wrote["x%d3" % t])
-        wrote["x%d" % t] = wrote["x%d1" % t]
+            tt(st[:, d + 640 + b:d + 1280:4], bank(b, K), T.a1[:, b:640:4], A.add, "a10 a11", "ps%d n%d@%d" % (b, b, t))
+            line(st[:, d + c:d + 640:4], bank(c, K), "", "ps%d d%d@%d" % (c, c, t), 2.0)
+        src = xk(t - 1) + "".join(" n%d@%d d%d@%d" % (b, k, b, k) for b in range(4) for k in range(max(t - 1, 1), t + 1))
+        if t > 1:
+            src += " z%d" % (t - 2)
+        for b in range(4):
+            r = src + " fo%d" % b
+            if t < R:
+                line(st[:, x + b:x + 1280:4], st[:, lo:d + 2560], r, "xa%d@%d xb%d@%d" % (b, t, b, t), idx=T.fo[:, 20 * b:20 * b + 20])
+            else:
+                phase[0] = R
+                for h in range(2):
+                    a, c = x + 640 * h, 20 * b + 10 * h
+                    line(st[:, a + b:a + 640:4], st[:, lo:d + 2560], r, "x%s%d@%d" % ("ab"[h], b, t), idx=T.fo[:, c:c + 10])
 
     for t in range(R):
-        if t > 0:
-            merge(t)
+        phase[0] = t
         fire(t)
-    merge(R)
+        if t == R - 1:
+            line(T.oo[:], T.cj[:, 0:W], "cj cjv ent@%d" % t, "oo", idx=T.lst[:, 64 * t:64 * t + 10])
+            store(T.ol[:], T.oo[0:128:16, :], "oo", "sol")
+        merge(t + 1)
     x, c0 = X(R), C * R
-    act(T.oo[:], T.cj[:, 0:W].indirect(T.eo[:, 64:74]), F.Copy, "cj eo4", "oo")
-    store("y", T.ol[:], T.oo[0:128:16, :], "oo")
     for h in range(2):
         a = c0 + K * h
-        quant(T.xq[:, a:a + K], T.xs[:, a:a + K], st[:, x + 640 * h:x + 640 * h + 640], "", "xq3%d" % h)
-        mm(h, K, T.vq[:], T.vs[:], T.xq[:, a:a + K], T.xs[:, a:a + K], "vq xq3%d" % h)
-    store("y", T.oc[:], T.xq[:, c0:c0 + C].bitcast(dt.uint8), "xq30 xq31")
+        quant(T.xq[:, a:a + K], T.xs[:, a:a + K], st[:, x + 640 * h:x + 640 * h + 640], xk(R, "ab"[h]), "xq%d@3" % h)
+        mm(h, K, T.vq[:], T.vs[:], T.xq[:, a:a + K], T.xs[:, a:a + K], "vq xq%d@3" % h)
+        line(T.yo[:, K * h:K * h + K], bank(h, K), "", "ps%d y%d" % (h, h))
+        store(T.oc[:, 640 * h:640 * h + 640], T.xq[:, a:a + K].bitcast(dt.uint8), "xq%d@3" % h, "soc%d" % h)
+        store(T.y[:, K * h:K * h + K], T.yo[:, K * h:K * h + K], "y%d" % h, "sy%d" % h)
     for k in range(4):
-        store("y", T.osc[4 * k:4 * k + 4, :], T.xs[32 * k:32 * k + 4, c0:c0 + C], "xq30 xq31")
-    cp(T.yo[:, 0:K], bank(0, K), "", "ps0 ya")
-    act(T.yo[:, K:C], bank(1, K), F.Copy, "", "ps1 yb")
-    store("s", T.y[:], T.yo[:], "ya yb")
-    g.wait_ge(T.sem.out, 16 * 7)
-    g.wait_ge(T.sem.sent, sent[0])
-    for q in ("v", "s", "t", "g"):
-        wait("g", ("c" + q, count[q]))
+        store(T.osc[4 * k:4 * k + 4, :], T.xs[32 * k:32 * k + 4, c0:c0 + C], "xq0@3 xq1@3", "sos%d" % k)
+
+    named = {(c["phase"], c["name"]): i for i, c in enumerate(calls)}
+    todo = {q: [named[p, k] for p, lists in enumerate((FIRST, LATER, LATER, LAST)) for k in lists[q].split() if (p, k) in named]
+            for q in queue}
+    issued = set()
+    count, seen = {q: 0 for q in queue}, {q: {} for q in queue}
+
+    def wait(q, sem, c):
+        if seen[q].get(sem, 0) < c:
+            queue[q].wait_ge(T.sem[sem], c)
+            seen[q][sem] = c
+
+    while len(issued) < len(calls):
+        q = [k for k in queue if todo[k] and calls[todo[k][0]]["before"] <= issued][0]
+        i, need = todo[q].pop(0), {}
+        for j in calls[i]["before"]:
+            sem, c = calls[j]["token"]
+            need[sem] = max(need.get(sem, 0), c)
+        for sem in need:
+            wait(q, sem, need[sem])
+        calls[i]["ways"][q]()
+        if calls[i]["token"] is None:
+            count[q] += 1
+            calls[i]["token"] = ("c" + q, count[q])
+        issued.add(i)
+    wait("g", "out", 16 * 9)
+    wait("g", "sent", sent[0])
+    for q in "vstg":
+        wait("g", "c" + q, count[q])

from concourse.mybir import dt, AluOpType, ActivationFunctionType

C, K, R = 320, 160, 3
CV = C + 16
W = CV + 1
P = 2624
LIFT = 16384.0
DOWN = 3.0 / 512
LATE = 496
TOP = 1110.0
SO2 = 328
F32, BF, F16, I32, U16, Q4, U8 = "float32", "bfloat16", "float16", "int32", "uint16", "float8_e4m3fn_x4", "uint8"


def sb(n, t):
    return ("sbuf", [128, n], t)


SCRATCH = {
    "st": sb(3 * P + 1280 + 1280, BF),
    "ub": sb(512, BF), "vb": sb(512, BF), "tgi": sb(20, I32), "tgu": sb(20, U16), "ltg": sb(20, U16),
    "uq": sb(128, Q4), "us": sb(128, U8), "upq": sb(256, Q4), "ups": sb(256, U8), "vq": sb(128, Q4), "vs": sb(128, U8),
    "wq": sb(512, Q4), "wp": sb(512, U8), "half": sb(516, BF), "eye": sb(516, BF), "iq": sb(512, Q4), "ip": sb(512, U8),
    "xq": sb(4 * C, Q4), "xs": sb(4 * C, U8), "et": sb(3 * 640, BF), "eq": sb(3 * K, Q4), "es": sb(3 * K, U8),
    "ht": sb(3 * 640, BF), "hq": sb(3 * K, Q4), "hs": sb(3 * K, U8), "lq": sb(3 * K, Q4), "ls": sb(3 * K, U8),
    "pi": sb(2, I32), "pj": sb(4, I32), "col": sb(16, F32), "uoi": sb(16, I32), "uo": sb(16, U16),
    "one": sb(CV + 2, BF), "jm": sb(32, F32), "cj": sb(CV + 8, F32), "cjf": sb(C, F32), "r32": sb(CV + 2, BF),
    "da": sb(64, F32), "d4": sb(K, BF), "dc": sb(C, BF), "og": sb(C, F32), "own": sb(C, F32), "ig": sb(128, F32),
    "cw": sb(20, F32), "cwf": sb(20, F32), "xo": sb(20, F32), "tab": sb(2 * LATE, F32), "fourth": sb(32, BF),
    "bias": sb(22, F32), "acc": sb(24, F32), "junk": sb(24 * K, BF), "key": sb(C, F32), "keyr": sb(CV + 8, F32),
    "spu": sb(32, U16), "lspu": sb(32, U16), "keys": sb(C, F32), "keyh": sb(C, F32), "ki": sb(20, I32), "kj": sb(20, I32),
    "sort": sb(40, U16), "ends": sb(4, U16),
    "nr": sb(C + 32, BF), "prev": sb(C, F32), "rr": sb(CV + 2, F16), "zz": sb(CV + 2, BF), "dz": sb(CV + 2, BF),
    "hold": sb(CV + 2, BF), "jj": sb(CV, BF), "ja": sb(2, F32), "ju": sb(2, U16), "eo": sb(64, U16),
    "tr": sb(K, F32), "th": sb(K, F32), "t4": sb(120, U16), "sg": sb(C, BF), "cd": sb(C, F16), "hd": sb(C, F16),
    "v1": sb(20, F32), "o1": sb(20, F32), "o2": sb(20, F32), "dl": sb(20, F32), "cf": sb(20, F32),
    "lst": sb(3 * 64, U16), "llst": sb(3 * 64, U16),
    "uu": sb(C, F32), "ww": sb(2 * C, F32), "so": sb(2 * SO2, F32), "ga": sb(128, F32), "gm": sb(64, F32),
    "j1": sb(20, F32), "j2": sb(20, F32), "j3": sb(20, F32), "pre": sb(20, F32), "fo": sb(80, U16),
    "a1": sb(640, BF), "m2": sb(640, BF), "oo": sb(K, F32), "yo": sb(C, F32),
    "ps": ("psum", [128, 4096], F32),
}
SEMAPHORES = (["cv", "cs", "ct", "cg", "sent", "lx", "ltg", "lu", "lv", "lw", "out", "gm1", "gm2", "as0", "as1", "ag"]
              + [k + str(t) for k in ("ah", "ao") for t in range(R)])

FIRST = {
    "v": "half pj0 pj1 pj2 cj col uo cw da0 cwf tgu drop1 drop da1 key0 da2 biasa uq key1 upq0 ups0 upq1 jm0 xq1 og16 xq0 da3 dropk "
         "nr1 dropa nr0 d4 thr fourth ups1 rr zz ig0 og32 dz spu0 dropd hold ju cd eo2 eo1 xo d416 hd v1 eo3 dl og64 o1 spu1 eo0 o2 "
         "ent e3 off keyr1 eq keyr0 iq3 keys0 hq keyh0 keys1 ends0 prev1 keyh1 tau0 iq1 ki tau1 th kj ends1 t4 sort0 iq2 ww iq0 so1 "
         "cf ga0 n1 gm0 n0 j2 n2 j3 n3 fo3 fo0 fo2 fo1 xb0 xb2",
    "s": "one cjf inext zini dc r32 og qnext dc1 acc0 acc1 acc2 acc10 acc3 acc4 acc11 biasb acc12 acc5 acc6 acc13 acc14 acc7 acc8 "
         "acc15 drop4 acc9 ja sg acc16 acc17 acc18 acc19 e2 e1 e0 ig3 d432 og128 acc23 tadd ig1 h0 h2 h3 h1 og256 acc20 acc22 d464 "
         "acc21 ig2 d4128 tr uu own0 own1 a10 a11 d2 d3 d0 d1 xb3 xb1 prev0",
    "g": "pi uoi z2 z0 so0 nrv tab3 jm4 dc16 ltg dc32 z1 dc64 rr0 dc128 zz0 dc256 tab0 lspu0 eye lspu1 llst keyv tab2 tab1 lq cjv",
    "t": "ps5 ps4 ps6 ps0 ps2 ps3 ps1 pd1 pd2 pd0 pd3",
    "y": "tgi ub x0 wq",
}
LATER = {
    "v": "xq0 xq1 nr0 nr1 rr zz cd dz v1 ju hold o1 eo3 hd eo0 dl eo1 eo2 o2 ent off e1 eq so2 h2 cf vq hq tr ga1 th gm1 t4 ww j1 "
         "so1 ga0 gm0 pre j2 n0 j3 n1 fo1 fo0 n2 n3 fo2 fo3 xb0 xb2",
    "s": "m2 ja sg e3 e0 e2 h1 h3 h0 uu m a10 a11 prev1 oo d2 d3 d1 d0 xb1 xb3 prev0",
    "g": "add llst lq",
    "t": "ps4 ps5 ps6 ps1 ps3 ps2 ps0 pd0 pd2 pd1 pd3",
    "y": "vb sol",
}
LAST = {
    "v": "xa0 xa1 xq0 xb2 xb3 xq1",
    "s": "xa2 xa3 xb0 xb1 y0 y1",
    "g": "",
    "t": "ps0 ps1",
    "y": "soc0 sy0 soc1 sos0 sos1 sos2 sy1 sos3",
}


def rank_program(g, core, T, topo):
    rank = T.rank_of(core)
    if rank is None:
        return
    A, F = AluOpType, ActivationFunctionType
    n = len(T.cores)
    nxt, prv = T.cores[(rank + 1) % n], T.cores[(rank - 1) % n]
    rid, pid = topo.addr(nxt)[0], topo.addr(nxt)[1]
    out_mask, out_n, in_n = topo.mask(core, nxt), len(topo.engines(core, nxt)), len(topo.engines(prv, core))
    V, S, PE = g.vector, g.scalar, g.tensor
    queue = {"v": V, "s": S, "t": PE, "g": g, "y": g.sync}
    calls, wrote, readers, phase, sent = [], {}, {}, [0], [0]

    def note(ways, r, w, token=None, name=None):
        r, w = r.split(), w.split()
        before = set(wrote[k] for k in r) | set(wrote[k] for k in w if k in wrote)
        for k in w:
            before |= set(readers.get(k, []))
        for k in r:
            readers.setdefault(k, []).append(len(calls))
        for k in w:
            wrote[k], readers[k] = len(calls), []
        calls.append({"ways": ways, "before": before, "token": token, "phase": phase[0], "name": name or w[-1].split("@")[0]})

    def compute(q, call):
        return lambda: call().then_inc(T.sem["c" + q], 1)

    def pick(i, idx):
        return i if idx is None else i.indirect(idx)

    def load(sem, pairs, r, w):
        def call():
            for o, i in pairs:
                g.sync.dma_start(o, i).then_inc(T.sem[sem], 16)
        note({"y": call}, r, w, (sem, 16 * len(pairs)))

    def store(o, i, r, name):
        note({k: lambda k=k: queue[k].dma_start(o, i).then_inc(T.sem.out, 16) for k in "ys"}, r, "", ("out", 0), name)

    def add(o, i, sem, r, w):
        note({"g": lambda: g.dma_start(o, i, accum_op=A.add).then_inc(T.sem[sem], 16)}, r, w, (sem, 16), "add")

    def send(pairs, sem, r, w):
        def call():
            for o, i in pairs:
                g.remote_dma(o, i, T.sem[sem], T.sem.sent, pid, rid, out_mask)
        sent[0] += out_n * len(pairs)
        note({"g": call}, r, w, (sem, in_n * len(pairs)))

    def vec(call, r, w):
        note({"v": compute("v", call)}, r, w)

    def ts(o, i, s1, s2, o0, o1, r, w, idx=None):
        more = () if o1 is None else (o1,)
        vec(lambda: V.tensor_scalar(o, pick(i, idx), s1, s2, o0, *more), r, w)

    def tt(o, a, b, alu, r, w, idx=None):
        vec(lambda: V.tensor_tensor(o, pick(a, idx), b, alu), r, w)

    def cp(o, i, r, w):
        vec(lambda: V.tensor_copy(o, i), r, w)

    def fill(o, c, w):
        vec(lambda: V.memset(o, c), "", w)

    def scan(o, d0, d1, init, o0, o1, r, w):
        vec(lambda: V.tensor_tensor_scan(o, d0, d1, init, o0, o1), r, w)

    def quant(q, s, i, r, w):
        vec(lambda: V.quantize_mx(q, s, i), r, w)

    def sign(o, i, r, w, bias=0.0, scale=1.0, acc=None):
        note({"s": compute("s", lambda: S.activation(o, i, F.Sign, bias=bias, scale=scale, accum_out=acc))}, r, w)

    def line(o, i, r, w, scale=1.0, bias=0.0, idx=None, relu=False):
        def on_v():
            if scale == 1.0 and bias == 0.0:
                return V.tensor_copy(o, pick(i, idx))
            if relu:
                return V.tensor_scalar(o, pick(i, idx), 0.0, scale, A.max, A.mult)
            return V.tensor_scalar(o, pick(i, idx), scale, bias, A.mult, A.add)

        def on_s():
            if scale == 1.0 and bias == 0.0:
                return S.activation(o, pick(i, idx), F.Copy)
            return S.activation(o, pick(i, idx), F.Relu if relu else F.Identity, bias=bias, scale=scale)
        note({"v": compute("v", on_v), "s": compute("s", on_s)}, r, w)

    def bank(b, m):
        return T.ps[:, 512 * b:512 * b + m]

    def mm(b, m, lq, ls, rq, rs, r, name=None):
        note({"t": compute("t", lambda: PE.matmul_mx(bank(b, m), lq, ls, rq, rs, True, True))}, r, "ps%d" % b, name=name)

    def iota(o, pat, ch, w, whole=False, base=0):
        more = {} if whole else {"allow_small_or_imprecise_dtypes": True}
        note({"g": compute("g", lambda: g.iota(o, pat, base, ch, **more))}, "", w)

    def const(o, c, w):
        iota(o, [[0, o.shape[1]]], 0, w, base=c)

    def select(o, i, pat, alu, base, ch, r, w):
        note({"g": compute("g", lambda: g.affine_select(o, i, pat, alu, 0.0, base, ch))}, r, w)

    def repeat(buf, m, key, growth=1.0, on_g=False):
        a = 16
        while a < m:
            b, w = min(a, m - a), "%s %s%d" % (key, key, a)
            if on_g:
                select(buf[:, a:a + b], buf[:, 0:b], [[0, b]], A.is_ge, 0, 0, key, w)
            else:
                line(buf[:, a:a + b], buf[:, 0:b], key, w, scale=growth ** (a // 16))
            a += b

    def X(t):
        return P * t + 1280

    def xk(t, h="ab"):
        return "x0" if t == 0 else " ".join("x%s%d@%d" % (k, b, t) for b in range(4) for k in h)

    st = T.st
    icol, tcol, qcol, thr, zini, inext, drop, dropa, dropd, dropk, qnext, drop4, tadd, drop1 = [T.col[:, i:i + 1] for i in range(14)]

    load("ltg", [(T.tgi[:], T.tg[:])], "", "tgi")
    load("lu", [(T.ub[:], T.u[:])], "", "ub")
    load("lx", [(st[:, X(0):X(0) + 1280], T.x[:])], "", "x0")
    load("lw", [(T.wq[:].bitcast(dt.uint8), T.wc[:]), (T.wp[:], T.ws[:])], "x0", "wq")
    phase[0] = 1
    load("lv", [(T.vb[:], T.v[:])], "wq", "vb")
    quant(T.vq[:], T.vs[:], T.vb[:], "vb", "vq")
    phase[0] = 0

    iota(T.pi[:, 0:1], [[0, 1]], 1, "pi", True)
    iota(T.uoi[:], [[1, 2], [16, 8]], 0, "uoi", True)
    iota(T.jm[:, 16:32], [[0, 4], [1, 4]], 0, "jm4")
    fill(T.half[:], 0.5, "half")
    select(T.eye[:], T.half[:], [[1, 516]], A.is_equal, -3, -4, "half", "eye")
    iota(T.nr[:, C:C + 32], [[1, 2], [0, 16]], 0, "nrv")
    const(T.zz[:, 0:1], 2080, "zz0")
    const(T.rr[:, 0:1], 0, "rr0")
    const(T.keyr[:, C:W], 1, "keyv")
    const(T.so[:, 0:SO2 + 1:SO2], 0, "so0")
    for t in range(R):
        const(st[:, X(t) + 1280:X(t) + 1344], 0, "z%d" % t)
    iota(T.tab[:, 0:K], [[-1, K]], 0, "tab0", base=int(TOP))
    iota(T.tab[:, LATE:LATE + K], [[1, K]], 0, "tab1", base=-int(TOP + P / 4))
    for k in range(2):
        const(T.tab[:, LATE * k + K:LATE * k + LATE], 0, "tab%d" % (2 + k))
    scan(T.cj[:, 0:W], T.half[:, 0:W], T.half[:, 0:W], -1.0, A.add, A.add, "half", "cjv cj")
    ts(T.pj[:, 0:1], T.pi[:, 0:1], 15, None, A.bitwise_and, None, "pi", "pj0")
    ts(T.pj[:, 1:2], T.pi[:, 0:1], 3, None, A.bitwise_and, None, "pi", "pj1")
    ts(T.pj[:, 2:3], T.pi[:, 0:1], 2, 3, A.logical_shift_right, A.bitwise_and, "pi", "pj2")
    cp(T.col[:, 0:3], T.pj[:, 0:3], "pj0 pj1 pj2", "col")
    cp(T.uo[:], T.uoi[:], "uoi", "uo")
    line(T.one[:], T.half[:, 0:CV + 2], "half", "one", 2.0)
    line(T.cjf[:], T.cj[:, 0:C], "cj", "cjf", 1.0 / 4096, 1.0)
    line(T.r32[:, 0:W], T.cj[:, 0:W], "cj cjv", "r32", 1.0 / 32, -CV / 64)
    const(T.cj[:, C:W], -1, "cjv")
    ts(T.cw[:], T.cj[:, 0:C:16], icol, None, A.add, None, "cj col", "cw")
    ts(drop, icol, 15.0, 1.0 / LIFT, A.is_equal, A.max, "col", "drop")
    ts(drop1, qcol, 3.0, 1.0 / LIFT, A.is_equal, A.max, "col", "drop1")
    for o, i, r, w, sc, bi in ((T.cwf[:], T.cw[:], "cw", "cwf", 1.0 / 4096, 1.0), (T.xo[:], T.cw[:], "cw", "xo", -1.0, TOP - C),
                               (T.bias[:, 20:22], T.cw[:, 0:2], "cw", "biasb", 16.0, 16.5),
                               (thr, icol, "col", "thr", 16.0, 15.5), (zini, icol, "col", "zini", -1.0, 2087.5),
                               (inext, icol, "col", "inext", 1.0, 1.0), (qnext, qcol, "col", "qnext", 1.0, 1.0),
                               (tadd, tcol, "col", "tadd", 1.0, -4.0), (dropa, drop, "drop", "dropa", 1 / DOWN, 0.0),
                               (dropd, drop, "drop", "dropd", float(LATE), 0.0), (dropk, drop, "drop", "dropk", 4096.0, 0.0),
                               (drop4, drop1, "drop1", "drop4", 4.0, 0.0)):
        line(o, i, r, w, sc, bi)
    ts(T.da[:, 0:16], T.cj[:, 0:16], icol, -(1 + DOWN), A.is_equal, A.mult, "cj col", "da0")
    ts(T.da[:, 16:32], T.cj[:, 0:16], inext, LIFT - 1, A.is_equal, A.mult, "cj inext", "da1")
    tt(T.da[:, 32:48], T.da[:, 0:16], T.da[:, 16:32], A.add, "da0 da1", "da2")
    line(T.dc[:, 0:1], icol, "col", "dc", 0.0)
    line(T.dc[:, 1:16], T.da[:, 33:48], "da2 dc", "dc dc1", 1.0, 1.0)
    repeat(T.dc, C, "dc", on_g=True)
    ts(T.da[:, 48:64], T.jm[:, 16:32], qcol, None, A.not_equal, None, "jm4 col", "da3")
    ts(T.jm[:, 0:16], T.jm[:, 16:32], qnext, LIFT, A.is_equal, A.mult, "jm4 qnext", "jm0")
    tt(T.d4[:, 0:16], T.da[:, 48:64], T.jm[:, 0:16], A.add, "da3 jm0", "d4")
    repeat(T.d4, K, "d4")
    line(T.og[:, 0:16], T.da[:, 0:16], "da0", "og", -4.0 ** -20 / (1 + DOWN))
    repeat(T.og, C, "og", 4.0)
    fill(T.fourth[:], 0.25, "fourth")
    scan(T.ig[:, 0:32], T.fourth[:], T.one[:, 0:32], 4.0 ** 21, A.mult, A.mult, "fourth one", "ig0")
    for k, sc in ((1, 4.0 ** -20), (2, -1.0), (3, -4.0 ** -20)):
        line(T.ig[:, 32 * k:32 * k + 32], T.ig[:, 0:32], "ig0", "ig%d" % k, sc)
    for b in range(4):
        quant(T.iq[:, 128 * b:128 * b + 128], T.ip[:, 128 * b:128 * b + 128], T.eye[:, 3 - b:515 - b], "eye", "iq%d" % b)
    quant(T.uq[:], T.us[:], T.ub[:], "ub", "uq")
    for h in range(2):
        a, idx = 128 * h, T.uo[:, 8 * h:8 * h + 8]
        cp(T.upq[:, a:a + 128].bitcast(dt.uint32), T.uq[:].bitcast(dt.uint32).indirect(idx), "uq uo", "upq%d" % h)
        line(T.ups[:, a:a + 128], T.us[:], "uq uo", "ups%d" % h, idx=idx)

    def signs(m, src, h, c, r):
        sign(T.junk[:, K * m:K * m + K], src[:, K * h:K * h + K], r, "acc%d" % m, T.bias[:, c:c + 1], -1.0, T.acc[:, m:m + 1])

    cp(T.tgu[:], T.tgi[:], "tgi", "tgu")
    send([(T.ltg[:], T.tgu[:])], "ag", "tgu", "ltg")
    tt(T.bias[:, 0:20], T.tgi[:], T.cwf[:], A.add, "tgi cwf", "biasa")
    for h in range(2):
        a, b, c = K * h, 10 * h, 16 * h
        tt(T.key[:, a:a + K], T.cj[:, 0:C], T.cjf[:, a:a + K], A.add, "cj tgu cjf", "key%d" % h, T.tgu[:, b:b + 10])
        tt(T.keyr[:, a:a + K], T.cj[:, 0:C], T.cjf[:, a:a + K], A.add, "cj ltg cjf", "keyr%d" % h, T.ltg[:, b:b + 10])
        for m in range(b, b + 10):
            signs(m, T.key, h, m, "biasa key%d" % h)
        ts(T.spu[:, c:c + 10], T.acc[:, b:b + 10], 0.5, 79.5, A.mult, A.add, " ".join("acc%d" % m for m in range(b, b + 10)), "spu%d" % h)
        send([(T.lspu[:, c:c + 10], T.spu[:, c:c + 10])], "as%d" % h, "spu%d" % h, "lspu%d" % h)
        cp(T.keys[:, a:a + K].indirect(T.lspu[:, c:c + 10]), T.keyr[:, a:a + K], "keyr%d lspu%d" % (h, h), "keys%d" % h)
        scan(T.keyh[:, a:a + K], T.dc[:, 0:K], T.keys[:, a:a + K], 0.0, A.mult, A.max, "dc keys%d" % h, "keyh%d" % h)
        ts(T.sort[:, 20 + b:30 + b], T.keyh[:, a + 15:a + K:16], drop, -1.0, A.mult, A.add, "keyh%d drop" % h, "tau%d" % h)
        for k in range(2):
            signs(20 + 2 * h + k, T.keyr, h, 20 + k, "biasb keyr%d" % h)
        ts(T.ends[:, 2 * h:2 + 2 * h], T.acc[:, 20 + 2 * h:22 + 2 * h], 0.5, a + 80.0, A.mult, A.add,
           "acc%d acc%d" % (20 + 2 * h, 21 + 2 * h), "ends%d" % h)
        line(T.own[:, a:a + K], T.og[:], "og tau%d" % h, "own%d" % h, 4.0 ** (20 * h), idx=T.sort[:, 20 + b:30 + b])
    ts(T.ki[:], T.keyh[:, 15:C:16], dropk, None, A.mult, None, "keyh0 keyh1 dropk", "ki")
    ts(T.kj[:], T.ki[:], 4095, None, A.bitwise_and, None, "ki", "kj")
    cp(T.sort[:, 0:20], T.kj[:], "kj", "sort0")

    def best(k, t):
        a, alu, ww = SO2 * k, (A.max, A.min)[k], T.ww[:, C * (t % 2):C * (t % 2) + C]
        scan(T.so[:, a + 1:a + C + 1], ww, ww, 0.0, alu, alu, "ww@%d" % (t % 2), "so%d" % (k + 1))
        tt(T.ga[:, 64 * k:64 * k + 64], T.so[:, a:a + C + 1], T.ig[:, 64 * k:64 * k + 64], A.mult,
           "so0 so%d ends0 ends1 ig0 ig1 ig2 ig3" % (k + 1), "ga%d" % k, T.ends[:])
        tt(T.gm[:, 32 * k:32 * k + 20], T.ga[:, 64 * k:64 * k + 20], T.ga[:, 64 * k + 32:64 * k + 52], A.max, "ga%d" % k, "gm%d" % k)

    def fire(t):
        x, L, e0 = X(t), 64 * t, 640 * t
        for h in range(2):
            a = C * t + K * h
            quant(T.xq[:, a:a + K], T.xs[:, a:a + K], st[:, x + 640 * h:x + 640 * h + 640], xk(t), "xq%d@%d" % (h, t))
            mm(4 + h, K, T.upq[:, 0:128], T.ups[:, 0:128], T.xq[:, a:a + K], T.xs[:, a:a + K], "upq0 ups0 xq%d@%d" % (h, t))
        mm(6, C, T.upq[:, 128:256], T.ups[:, 128:256], T.xq[:, C * t:C * t + C], T.xs[:, C * t:C * t + C],
           "upq1 ups1 xq0@%d xq1@%d" % (t, t))
        for h in range(2):
            if t == 0:
                ts(T.nr[:, K * h:K * h + K], bank(4 + h, K), 0.0, None, A.is_le, None, "", "ps%d nr%d" % (4 + h, h))
            else:
                tt(T.nr[:, K * h:K * h + K], bank(4 + h, K), T.prev[:, K * h:K * h + K], A.is_le, "prev%d" % h, "ps%d nr%d" % (4 + h, h))
            if t < R - 1:
                line(T.prev[:, K * h:K * h + K], bank(4 + h, K), "", "ps%d prev%d" % (4 + h, h))
        sign(T.sg[:], bank(6, C), "", "ps6 sg")
        nr = T.nr[:, 0:W]
        scan(T.rr[:, 1:W + 1], T.one[:, 0:W], nr, 0.0, A.add, A.subtract, "one nr0 nr1 nrv", "rr")
        scan(T.zz[:, 1:W + 1], T.one[:, 0:W], nr, zini, A.add, A.subtract, "one nr0 nr1 nrv zini", "zz")
        sign(T.jj[:], T.rr[:, 1:CV + 1], "rr thr", "ja", thr, -1.0, T.ja[:, 0:1])
        scan(T.dz[:, 0:W], T.zz[:, 1:W + 1], T.zz[:, 0:W], 0.0, A.max, A.subtract, "zz zz0", "dz")
        scan(T.hold[:, 0:W], T.dz[:, 0:W], T.r32[:, 0:W], -8.0, A.add, A.min, "dz r32", "hold")
        ts(T.ju[:, 0:1], T.ja[:, 0:1], 0.5, CV / 2, A.mult, A.add, "ja", "ju")
        for b in range(4):
            ts(T.eo[:, 16 * b:16 * b + 16], T.hold[:, 0:W], 128.0, 2.0 * CV + b, A.mult, A.add, "hold ju", "eo%d" % b, T.ju[:, 0:1])
            line(T.et[:, e0 + b:e0 + 640:4], st[:, x:x + 1344], "%s z%d eo%d" % (xk(t), t, b), "e%d" % b, idx=T.eo[:, 16 * b:16 * b + 10])
        eq, es = T.eq[:, K * t:K * t + K], T.es[:, K * t:K * t + K]
        hq, hs = T.hq[:, K * t:K * t + K], T.hs[:, K * t:K * t + K]
        quant(eq, es, T.et[:, e0:e0 + 640], "e0 e1 e2 e3", "eq")
        for b in range(4):
            mm(b, K, T.wq[:, 128 * b:128 * b + 128], T.wp[:, 128 * b:128 * b + 128], eq, es, "wq eq")
            line(T.ht[:, e0 + b:e0 + 640:4], bank(b, K), "", "ps%d h%d" % (b, b), 0.03125, relu=True)
        quant(hq, hs, T.ht[:, e0:e0 + 640], "h0 h1 h2 h3", "hq@%d" % t)
        send([(T.lq[:, K * t:K * t + K].bitcast(dt.uint8), hq.bitcast(dt.uint8)), (T.ls[:, K * t:K * t + K], hs)],
             "ah%d" % t, "hq@%d" % t, "lq@%d" % t)
        scan(T.cd[:], T.dc[:], T.nr[:, 0:C], 0.0, A.mult, A.add, "dc nr0 nr1", "cd")
        scan(T.hd[:], T.dc[:], T.sg[:], 0.0, A.mult, A.max, "dc sg", "hd")
        ts(T.v1[:], T.cd[:, 15:C:16], dropa, icol, A.mult, A.add, "cd dropa col", "v1")
        tt(T.o1[:], T.v1[:], T.rr[:, 0:C:16], A.add, "v1 rr rr0", "o1")
        ts(T.dl[:], T.hd[:, 15:C:16], dropd, 0.0, A.mult, A.max, "hd dropd", "dl")
        tt(T.o2[:], T.o1[:], T.dl[:], A.add, "o1 dl", "o2")
        cp(T.lst[:, L + 16:L + 36], T.o2[:], "o2", "off@%d" % t)
        ts(T.lst[:, L:L + 16], T.hold[:, 0:W], 32.0, CV / 2, A.mult, A.add, "hold ju", "ent@%d" % t, T.ju[:, 0:1])
        send([(T.llst[:, L:L + 36], T.lst[:, L:L + 36])], "ao%d" % t, "off@%d ent@%d" % (t, t), "llst@%d" % t)
        ts(T.cf[:], T.o1[:], K - 0.5, float(K), A.is_lt, A.mult, "o1", "cf")
        if t > 0:
            d = P * (t - 1)
            line(T.m2[:], st[:, x:x + 1280], "%s t4@%d" % (xk(t), t - 1), "m2", idx=T.t4[:, 40 * t - 40:40 * t])
            add(T.m2[:], st[:, d:d + 640], "gm%d" % t, " ".join("d%d@%d" % (b, t) for b in range(4)), "m2")
            line(st[:, d + 640:d + 1280], T.m2[:], "m2", " ".join("n%d@%d" % (b, t) for b in range(4)) + " m", 0.5)
            best(1, t - 1)
            tt(T.j1[:], T.gm[:, 32:52], T.cf[:], A.subtract, "gm1 cf", "j1")
            tt(T.pre[:], T.j1[:], T.xo[:], A.max, "j1 xo", "pre")
        line(T.tr[:], T.keyr[:, 0:W], "keyr0 keyr1 keyv llst@%d" % t, "tr", idx=T.llst[:, L:L + 10])
        scan(T.th[:], T.d4[:], T.tr[:], 0.0, A.mult, A.max, "d4 tr", "th")
        ts(T.t4[:, 40 * t:40 * t + 40], T.th[:, 3:K:4], drop4, tadd, A.mult, A.add, "th drop4 tadd", "t4@%d" % t)
        for h in range(2):
            a = 40 * t + 20 * h
            line(T.a1[:, 320 * h:320 * h + 320], st[:, x:x + 1280], "%s t4@%d" % (xk(t), t), "a1%d" % h, 0.5, idx=T.t4[:, a:a + 20])
        line(T.uu[:], T.tab[:], "tab0 tab1 tab2 tab3 llst@%d" % t, "uu", idx=T.llst[:, L + 16:L + 36])
        tt(T.ww[:, C * (t % 2):C * (t % 2) + C], T.uu[:], T.own[:], A.mult, "uu sort0 own0 own1", "ww@%d" % (t % 2), T.sort[:, 0:20])
        best(0, t)
        tt(T.j2[:], T.gm[:, 0:20], T.cf[:], A.subtract, "gm0 cf", "j2")
        tt(T.j3[:], T.j2[:], T.pre[:] if t else T.xo[:], A.max, "j2 pre" if t else "j2 xo", "j3")
        for b in range(4):
            ts(T.fo[:, 20 * b:20 * b + 20], T.j3[:], -4.0, 4 * TOP + b + (P if t else 0), A.mult, A.add, "j3", "fo%d" % b)

    def merge(t):
        d, lo, x = P * (t - 1), P * max(t - 2, 0), X(t)
        lq, ls = T.lq[:, K * (t - 1):K * t], T.ls[:, K * (t - 1):K * t]
        for b in range(4):
            mm(b, K, T.iq[:, 128 * b:128 * b + 128], T.ip[:, 128 * b:128 * b + 128], lq, ls, "iq%d lq@%d" % (b, t - 1), "pd%d" % b)
        for b in range(4):
            c = (b + 2) % 4
            tt(st[:, d + 640 + b:d + 1280:4], bank(b, K), T.a1[:, b:640:4], A.add, "a10 a11", "ps%d n%d@%d" % (b, b, t))
            line(st[:, d + c:d + 640:4], bank(c, K), "", "ps%d d%d@%d" % (c, c, t), 2.0)
        src = xk(t - 1) + "".join(" n%d@%d d%d@%d" % (b, k, b, k) for b in range(4) for k in range(max(t - 1, 1), t + 1))
        if t > 1:
            src += " z%d" % (t - 2)
        for b in range(4):
            r = src + " fo%d" % b
            if t < R:
                line(st[:, x + b:x + 1280:4], st[:, lo:d + 2560], r, "xa%d@%d xb%d@%d" % (b, t, b, t), idx=T.fo[:, 20 * b:20 * b + 20])
            else:
                phase[0] = R
                for h in range(2):
                    a, c = x + 640 * h, 20 * b + 10 * h
                    line(st[:, a + b:a + 640:4], st[:, lo:d + 2560], r, "x%s%d@%d" % ("ab"[h], b, t), idx=T.fo[:, c:c + 10])

    for t in range(R):
        phase[0] = t
        fire(t)
        if t == R - 1:
            line(T.oo[:], T.cj[:, 0:W], "cj cjv ent@%d" % t, "oo", idx=T.lst[:, 64 * t:64 * t + 10])
            store(T.ol[:], T.oo[0:128:16, :], "oo", "sol")
        merge(t + 1)
    x, c0 = X(R), C * R
    for h in range(2):
        a = c0 + K * h
        quant(T.xq[:, a:a + K], T.xs[:, a:a + K], st[:, x + 640 * h:x + 640 * h + 640], xk(R, "ab"[h]), "xq%d@3" % h)
        mm(h, K, T.vq[:], T.vs[:], T.xq[:, a:a + K], T.xs[:, a:a + K], "vq xq%d@3" % h)
        line(T.yo[:, K * h:K * h + K], bank(h, K), "", "ps%d y%d" % (h, h))
        store(T.oc[:, 640 * h:640 * h + 640], T.xq[:, a:a + K].bitcast(dt.uint8), "xq%d@3" % h, "soc%d" % h)
        store(T.y[:, K * h:K * h + K], T.yo[:, K * h:K * h + K], "y%d" % h, "sy%d" % h)
    for k in range(4):
        store(T.osc[4 * k:4 * k + 4, :], T.xs[32 * k:32 * k + 4, c0:c0 + C], "xq0@3 xq1@3", "sos%d" % k)

    named = {(c["phase"], c["name"]): i for i, c in enumerate(calls)}
    todo = {q: [named[p, k] for p, lists in enumerate((FIRST, LATER, LATER, LAST)) for k in lists[q].split() if (p, k) in named]
            for q in queue}
    issued = set()
    count, seen = {q: 0 for q in queue}, {q: {} for q in queue}

    def wait(q, sem, c):
        if seen[q].get(sem, 0) < c:
            queue[q].wait_ge(T.sem[sem], c)
            seen[q][sem] = c

    while len(issued) < len(calls):
        q = [k for k in queue if todo[k] and calls[todo[k][0]]["before"] <= issued][0]
        i, need = todo[q].pop(0), {}
        for j in calls[i]["before"]:
            sem, c = calls[j]["token"]
            need[sem] = max(need.get(sem, 0), c)
        for sem in need:
            wait(q, sem, need[sem])
        calls[i]["ways"][q]()
        if calls[i]["token"] is None:
            count[q] += 1
            calls[i]["token"] = ("c" + q, count[q])
        issued.add(i)
    wait("g", "out", 16 * 9)
    wait("g", "sent", sent[0])
    for q in "vstg":
        wait("g", "c" + q, count[q])
